import numpy as np, ml_dtypes
CORES = [35,38,43,46]
N = 4
BF = ml_dtypes.bfloat16
def gentries(a):
    return np.ascontiguousarray(a.reshape(8, 16, -1).transpose(0, 2, 1)).reshape(8, -1)
def gtable(e):
    e = np.asarray(e); return np.ascontiguousarray(e.reshape(8, -1, 16).transpose(0, 2, 1)).reshape(128, -1).astype(np.int32)
W, K, R, B, S, HOP, T = 2048, 1024, 1024, 3, 2, 1, 6
LO = 0
def parts(rng):
    sh = (N, 8, 16, W)
    s = np.minimum(15, np.floor(16 * rng.random(sh) ** 2)); a = rng.integers(32, 257, sh) * 0.00390625
    m = np.exp2(-rng.choice(np.arange(5), sh, p=np.array([0.05, 0.1, 0.2, 0.3, 0.35])).astype(np.float64))
    x = rng.integers(-256, 256, sh); c = rng.integers(0, W, (N, 8, K))
    u = np.where(rng.random((N, 8, T, K)) < 0.5, np.floor(np.exp2(8 * rng.random((N, 8, T, K)))), rng.integers(0, 256, (N, 8, T, K)))
    z = rng.integers(0, 256, (N, 8, T, K))
    r = np.ascontiguousarray(np.argsort(rng.random((N, 8, T - 1, W // 2)), axis=-1)[..., :R])
    return s, a, m, x, c, np.clip(u, 0, 255), z, r
def pack(s, a, m, x, c, u, z, r):
    b = lambda v, p, n: np.ascontiguousarray(np.asarray(v, np.float32).reshape(N, p, n)).astype(BF)
    return {"sg": b(s, 128, W), "al": b(a, 128, W), "mj": b(m, 128, W), "nx": b(x, 128, W), "ce": np.stack([gtable(v) for v in c]),
            "uu": b(u, 8, T * K), "zz": b(z, 8, T * K), "rp": np.stack([gtable(v.reshape(8, -1)) for v in r])}
def two(rng, shape, lo, hi):
    return np.where(rng.random(shape) < 0.5, lo, hi)
def setup_inputs(rng):
    return pack(*parts(rng))
def setup_inputs_spread(rng):
    s, a, m, x, c, u, z, r = parts(rng); sh = (N, 8, 16, W); col = (N, 8, 1, W)
    s = np.minimum(15, np.floor(16 * rng.random(sh) * np.exp2(-3 * rng.random(col))))
    a = np.clip(np.exp2(-2 * rng.random(col)) * (0.5 + 0.5 * rng.random(sh)), 0.125, 1.0)
    m = np.exp2(-np.clip(rng.integers(0, 5, col) + rng.integers(-1, 2, sh), 0, 4).astype(np.float64))
    x = np.clip(np.floor((2 * rng.random(sh) - 1) * 256 * np.exp2(-6 * rng.random(col))), -256, 255)
    u = np.clip(np.floor(np.exp2(8 * rng.random((N, 8, 1, K))) * rng.random((N, 8, T, K))), 0, 255)
    z = np.clip(np.floor(256 * rng.random((N, 8, T, K)) ** 2), 0, 255)
    return pack(s, a, m, x, c, u, z, r)
def setup_inputs_ends(rng):
    s, a, m, x, c, u, z, r = parts(rng)
    s = two(rng, s.shape, 0, 15); a = two(rng, a.shape, 0.125, 1.0); m = two(rng, m.shape, 0.0625, 1.0); x = two(rng, x.shape, -256, 255)
    c = two(rng, c.shape, 0, W - 1); u = two(rng, u.shape, 0, 255); z = two(rng, z.shape, 0, 255)
    s[:, :, 0] = 0; s[:, :, 15] = 15; a[:, :, 15] = 1.0; m[:, :, 15] = 1.0
    c[..., K - 1] = W - 1; z[..., 15] = 0; z[..., K - 1] = 0
    places = np.concatenate([np.arange(R // 2), np.arange(W // 2 - R // 2, W // 2)])
    r = places[np.argsort(rng.random((N, 8, T - 1, R)), axis=-1)]
    return pack(s, a, m, x, c, u, z, r)
def setup_inputs_corners(rng):
    s, a, m, x, c, u, z, r = parts(rng); o = int(rng.integers(0, 4)); sh = (16, W)
    for q in range(N):
        for g in range(8):
            kind = (q + g + o) % 4
            if kind == 0:
                e = rng.integers(0, 4, sh); s[q, g] = 2 ** e; m[q, g] = np.exp2(-np.clip(e + rng.integers(-1, 2, sh), 0, 4).astype(np.float64))
            if kind == 1:
                s[q, g] = np.where(rng.random(sh) < 0.9, 15, s[q, g]); m[q, g] = np.where(rng.random(sh) < 0.9, 1.0, m[q, g])
            if kind == 2: m[q, g] = np.where(rng.random(sh) < 0.9, 0.0625, m[q, g])
            if kind == 3: x[q, g] = np.where(rng.random(sh) < 0.5, two(rng, sh, -256, 255), x[q, g])
    c = np.where(rng.random(c.shape) < 0.3, two(rng, c.shape, 0, W - 1), c)
    u = np.clip(rng.integers(0, 17, u.shape) * 2 ** rng.integers(0, 5, u.shape) + rng.integers(-1, 2, u.shape), 0, 255)
    z = np.clip(16 * rng.integers(0, 17, z.shape) + rng.integers(-1, 2, z.shape), 0, 255)
    return pack(s, a, m, x, c, u, z, r)
def setup_inputs_crowd(rng):
    s, a, m, x, c, u, z, r = parts(rng)
    c[:] = rng.integers(0, W, (N, 8, 1)); c[:, 1::4, K - 1] = (c[:, 1::4, K - 1] + rng.integers(1, W, (N, 2))) % W
    few = rng.integers(0, W, (N, 2, 4)); few[:, 0, 0] = W - 1; few[:, 0, 1] = 0
    c[:, 3::4] = np.take_along_axis(few, rng.integers(0, 4, (N, 2, K)), 2)
    u[:, :6] = u[:, :6, :, :1].copy(); z[:, :5] = z[:, :5, :, :1].copy()
    m[:, ::2] = m[:, ::2, :1].copy(); s[:, ::4] = s[:, ::4, :1].copy()
    h = W // 2; h0 = int(rng.integers(0, N)); st = int(rng.integers(1, 101)) * (2 * int(rng.integers(0, 2)) - 1)
    v = (int(rng.integers(0, h)) + st * np.arange(T + 1)) % h; odd = rng.integers(0, 2, T + 1)
    for t in range(T):
        for i in range(2): x[..., 2 * v[t] + i] = 2 * st + odd[t + 1] - i
    for i in range(2):
        e = 2 * v[1:] + i
        m[..., e] = 0.0625; s[..., e] = rng.integers(1, 16, (N, 8, 16, T)); s[:, :, 15, e] = 15
        a[..., e] = rng.integers(192, 257, (N, 8, 16, T)) * 0.00390625
    first = 255 * int(rng.integers(0, 2))
    for q in (h0, (h0 + HOP) % N):
        c[q] = 2 * v[0] + odd[0]
        z[q, :, 0] = first; z[q, :, 1] = 0; z[q, :, 2] = 255; z[q, :, 3:4] = 0
        z[q, 3::4, 1:4, K - 1] = 255 - z[q, 3::4, 1:4, K - 1]
    c[h0, 1::4, K - 1] = (c[h0, 1::4, K - 1] + rng.integers(1, W, 2)) % W
    return pack(s, a, m, x, c, u, z, r)
def setup_inputs_calm(rng):
    s, a, m, x, c, u, z, r = parts(rng)
    s = 8 + rng.integers(0, 2, s.shape); m = two(rng, m.shape, 0.0625, 0.125)
    for q in range(N): m[q, int(rng.integers(0, 8))] = 0.0625
    u = np.where(rng.random(u.shape) < 0.5, 8 * rng.integers(0, 32, u.shape), rng.integers(0, 256, u.shape))
    z = rng.choice(np.array([0, 127, 128, 143, 144, 255]), z.shape)
    h = W // 2; qa = int(rng.integers(0, N)); qb = (qa - HOP) % N; cell = np.arange(W); low = cell // h * h
    for q in (qa, qb): x[q] = np.clip(cell + x[q], low, low + h - 1) - cell
    s[qa, :, :, h:] = 8; c[qb] = rng.integers(h, W, (8, K))
    return pack(s, a, m, x, c, u, z, r)
def check_ranges(d):
    bad = []
    for k, lo, hi in (("sg", 0, 15), ("al", 0.125, 1), ("mj", 0.0625, 1), ("nx", -256, 255), ("ce", 0, W - 1), ("uu", 0, 255), ("zz", 0, 255), ("rp", 0, W // 2 - 1)):
        v = np.asarray(d[k]).astype(np.float64)
        if not (np.min(v) >= lo and np.max(v) <= hi): bad.append("range of " + k)
        elif k != "al" and k != "mj" and np.any(v != np.floor(v)): bad.append("whole numbers of " + k)
    if not np.all(np.isin(np.asarray(d["mj"]).astype(np.float64), np.array([0.0625, 0.125, 0.25, 0.5, 1.0]))): bad.append("powers of two of mj")
    e = np.sort(np.stack([gentries(np.asarray(v)) for v in d["rp"]]).reshape(N, 8, T - 1, R), axis=-1)
    if np.any(e[..., 1:] == e[..., :-1]): bad.append("distinct pairs of rp")
    return bad
def move(v, n):
    v = np.roll(v, n * HOP, axis=0); h = K // 2
    return np.concatenate([v[..., :h], np.roll(v[..., h:], n, axis=1)], axis=-1)
def reference(sg, al, mj, nx, ce, uu, zz, rp):
    s, a, m = [v.astype(np.float64).reshape(N, 8, 16, W) for v in (sg, al, mj)]; x = nx.astype(np.float32).astype(np.int64).reshape(N, 8, 16, W)
    u, z = [v.astype(np.float64).reshape(N, 8, T, K) for v in (uu, zz)]
    c = np.stack([gentries(v) for v in ce]).astype(np.int64); pairs = np.stack([gentries(v) for v in rp]).astype(np.int64).reshape(N, 8, T - 1, R)
    w = np.ones((N, 8, 16, K)); tally = np.zeros((N, 8, 16, K))
    qi = np.arange(N)[:, None, None]; gi = np.arange(8)[None, :, None]; slot = np.arange(K)[None, None, :]; hero = slot % 16
    for t in range(T):
        p = np.minimum(np.floor(u[:, :, t] * m[qi, gi, hero, c]), 15).astype(np.int64)
        d = (c + x[qi, gi, p, c]) & (W - 1); dd = d[:, :, None, :]
        rho = np.take_along_axis(s, dd, 3) * np.take_along_axis(m, dd, 3)
        real = 256 * rho[qi, gi, hero, slot] > z[:, :, t]
        w = np.clip(w * np.where(real[:, :, None, :], 2 * np.take_along_axis(a, dd, 3) * rho, 2 * np.maximum(1 - rho, 0)), 0.125, 4.0)
        tally = tally + w
        if t < T - 1:
            e = (2 * pairs[:, :, t] + (d[..., LO:LO + R] & 1))[:, :, None, :]; old = np.take_along_axis(m, e, 3)
            np.put_along_axis(m, e, np.where(rho[..., LO:LO + R] > 1, np.maximum(old * 0.5, 0.0625), old), 3)
        c = np.where(real, d ^ 1, d)
        if t < T - 1 and (t + 1) % S == 0: c, w, tally, u, z = [move(v, 1) for v in (c, w, tally, u, z)]
    return {"tl": move(tally, -(B - 1)).reshape(N, 128, K).astype(np.float32)}

def check_inputs(d):
    bad = list(check_ranges(d))
    if not bad:
        for name, y in reference(**d).items():
            for q in range(N):
                v = np.abs(np.asarray(y[q], np.float64)); s = np.sqrt(np.mean(v * v))
                if v.max() > 7 * s or s < 2.0 ** 0: bad.append('%s of rank %d is uneven or too small' % (name, q))
    return bad

@@ -1,0 +1,515 @@
+import math
+import numpy as np
+from concourse.bass import DstId, RemoteDMATransfer
+from concourse.mybir import AluOpType as A, ActivationFunctionType as F
+
+W, K, NT = 2048, 1024, 6
+H = K // 2
+NQ = 4
+Q = K // NQ
+P = 256
+WP = W + 2 * P
+CK = 32.0
+KM = 2.0 ** -48
+KI = 2.0 ** -52
+
+
+def _fit(e0, sign):
+    xs = []
+    for k in range(5):
+        t = (e0 + sign * k) * math.log(2.0)
+        x = -40.0
+        for _ in range(60):
+            x = t - math.log(-x)
+        xs.append(x)
+    s, b = np.polyfit(np.arange(5.0), np.array(xs), 1)
+    return float(s) / CK, float(b)
+
+
+SM, BM = _fit(-52, 1)
+SI, BI = _fit(-48, -1)
+
+SCRATCH = {
+    "sgs": ("sbuf", [128, WP], "bfloat16"), "als": ("sbuf", [128, WP + 16], "bfloat16"),
+    "mjs": ("sbuf", [128, W], "bfloat16"), "nxs": ("sbuf", [128, W], "bfloat16"),
+    "f1": ("sbuf", [128, W], "bfloat16"), "f2": ("sbuf", [128, W], "bfloat16"),
+    "tb0": ("sbuf", [128, WP], "float32"), "tb1": ("sbuf", [128, WP], "float32"),
+    "et": ("sbuf", [128, W], "float32"),
+    "ces": ("sbuf", [128, 64], "int32"), "rps": ("sbuf", [128, 320], "int32"), "v2": ("sbuf", [128, 320], "float32"),
+    "uz": ("sbuf", [8, 12, K], "bfloat16"), "raw": ("sbuf", [8, 8, K], "bfloat16"),
+    "stg": ("sbuf", [128, 512], "bfloat16"),
+    "l1": ("dram", [128, 256], "bfloat16"), "l2": ("dram", [128, 256], "bfloat16"),
+    "pb": ("sbuf", [128, 2], "bfloat16"), "pi": ("sbuf", [128, 4], "int32"), "pf": ("sbuf", [128, 12], "float32"),
+    "vw": ("sbuf", [128, 144], "int32"), "vt": ("sbuf", [128, 128], "int32"),
+    "vz": ("sbuf", [8, 144], "int32"), "vz2": ("sbuf", [8, 128], "int32"),
+    "bb": ("sbuf", [128, W], "bfloat16"), "dd": ("sbuf", [128, W], "bfloat16"),
+    "eq": ("sbuf", [128, 128], "bfloat16"), "i32": ("sbuf", [128, 128], "bfloat16"), "ir": ("sbuf", [128, 128], "bfloat16"),
+    "if32": ("sbuf", [128, 128], "float32"), "sh": ("sbuf", [128, 128], "float32"),
+    "ta": ("sbuf", [128, 128], "bfloat16"), "dm": ("sbuf", [128, 128], "bfloat16"),
+    "cw": ("sbuf", [128, 144], "float16"), "zw": ("sbuf", [8, 144], "bfloat16"),
+    "ua": ("sbuf", [8, 128], "float32"), "uc": ("sbuf", [8, 128], "float32"), "ub": ("sbuf", [8, 128], "bfloat16"),
+    "cst": ("sbuf", [128, 64], "bfloat16"),
+    "mi": ("sbuf", [128, K], "bfloat16"), "sn": ("sbuf", [128, K], "bfloat16"), "pr": ("sbuf", [128, K], "float16"),
+    "mg": ("sbuf", [128, K], "bfloat16"), "rho": ("sbuf", [128, K], "bfloat16"), "yv": ("sbuf", [128, K], "bfloat16"),
+    "nw": ("sbuf", [128, K], "float32"), "tt": ("sbuf", [128, K], "float32"), "yy": ("sbuf", [128, K], "float32"),
+    "oc": ("sbuf", [128, 128], "float32"), "oc16": ("sbuf", [128, 128], "uint16"),
+    "c0": ("sbuf", [128, 64], "int32"), "c16": ("sbuf", [128, 64], "uint16"),
+    "par": ("sbuf", [128, 64], "int32"), "ef": ("sbuf", [128, 64], "float32"), "e16": ("sbuf", [128, 64], "uint16"),
+    "ev": ("sbuf", [128, 64], "int32"), "nl": ("sbuf", [128, 64], "bfloat16"), "xf": ("sbuf", [128, 64], "float32"),
+    "fin": ("sbuf", [128, K], "float32"),
+}
+for _b in (1, 2):
+    SCRATCH["cs%d" % _b] = ("sbuf", [128, 64], "uint16")
+    SCRATCH["cr%d" % _b] = ("sbuf", [128, 64], "uint16")
+    SCRATCH["win%d" % _b] = ("sbuf", [128, K], "float32")
+    SCRATCH["tin%d" % _b] = ("sbuf", [128, K], "float32")
+    SCRATCH["lw%d" % _b] = ("dram", [128, H], "float32")
+    SCRATCH["lt%d" % _b] = ("dram", [128, H], "float32")
+for _t in range(NT):
+    SCRATCH["w%d" % _t] = ("sbuf", [128, K], "float32")
+for _b in range(8):
+    SCRATCH["ps%d" % _b] = ("psum", [128, 512], "float32")
+
+ARR = ["l1", "l2", "cr1", "cr2", "lw1", "lw2", "lt1", "lt2", "wl1", "wl2", "tl1", "tl2"] + ["fin%d" % i for i in range(NQ)]
+SEMAPHORES = ["qv", "qa", "qp", "qg", "ls"] + ["r_" + n for n in ARR] + ["d%d" % i for i in range(64)]
+
+
+def rank_program(g, core, T, topo):
+    rank = T.rank_of(core)
+    if rank is None:
+        return
+    n = len(T.cores)
+    eng = {"v": g.vector, "a": g.scalar, "p": g.tensor, "g": g, "s": g.sync}
+    cnt = {"v": 0, "a": 0, "p": 0, "g": 0, "d": 0, "ls": 0}
+    waited = {q: {} for q in eng}
+    total = {}
+    wr = {}
+    rd = {}
+
+    def need(q, ev, same):
+        if ev is None or (ev[2] == q and not same):
+            return
+        if waited[q].get(ev[0], 0) < ev[1]:
+            eng[q].wait_ge(T.sem[ev[0]], ev[1])
+            waited[q][ev[0]] = ev[1]
+
+    def order(q, reads, writes):
+        for k in reads:
+            need(q, wr.get(k), True)
+            if k.startswith("ps"):
+                for e in rd.get(k, []):
+                    need(q, e, False)
+        for k in writes:
+            need(q, wr.get(k), q != "p")
+            for e in rd.get(k, []):
+                need(q, e, q != "p")
+
+    def note(ev, reads, writes):
+        total[ev[0]] = ev[1]
+        for k in reads:
+            rd.setdefault(k, []).append(ev)
+        for k in writes:
+            wr[k] = ev
+            rd[k] = []
+
+    def op(q, fn, reads, writes):
+        order(q, reads, writes)
+        cnt[q] += 1
+        fn().then_inc(T.sem["q" + q], 1)
+        note(("q" + q, cnt[q], q), reads, writes)
+
+    def dma(q, out, in_, reads, writes):
+        order(q, reads, writes)
+        s = "d%d" % cnt["d"]
+        cnt["d"] += 1
+        eng[q].dma_start(out, in_).then_inc(T.sem[s], 16)
+        note((s, 16, None), reads, writes)
+
+    def mms(lst, reads, writes):
+        def fn():
+            ins = None
+            for m in lst:
+                ins = g.tensor.matmul(m[0], m[1], m[2], m[3], m[4])
+            return ins
+        op("p", fn, reads, writes)
+
+    def send(hop, name, out, srcs, reads):
+        dst = T.cores[(rank + hop) % n]
+        rid, pid, _ = topo.addr(dst)
+        m = topo.mask(core, dst)
+        order("g", reads, [])
+        if len(srcs) == 1:
+            g.remote_dma(out, srcs[0], T.sem["r_" + name], T.sem.ls, pid, rid, m)
+        else:
+            g.remote_dma_fused([RemoteDMATransfer(dst_ids=[DstId(rid=rid, pnc=pid)], dma_engine_mask=m,
+                                                  remote_sem=T.sem["r_" + name], srcs=srcs, dsts=[out], alu_op=1)],
+                               local_sem=T.sem.ls)
+        cnt["ls"] += len(topo.engines(core, dst))
+        total["ls"] = cnt["ls"]
+
+    def arrives(hop, name, key):
+        src = T.cores[(rank - hop) % n]
+        note(("r_" + name, len(topo.engines(src, core)), None), [], [key])
+
+    V, S = g.vector, g.scalar
+
+    def ts(out, in0, s1, s2, o0, o1, reads, writes):
+        if s2 is None:
+            op("v", lambda: V.tensor_scalar(out, in0, s1, None, o0), reads, writes)
+        else:
+            op("v", lambda: V.tensor_scalar(out, in0, s1, s2, o0, o1), reads, writes)
+
+    def tt(out, in0, in1, o, reads, writes):
+        op("v", lambda: V.tensor_tensor(out, in0, in1, o), reads, writes)
+
+    def cp(out, in_, reads, writes):
+        op("v", lambda: V.tensor_copy(out, in_), reads, writes)
+
+    def fill(out, x, writes):
+        op("v", lambda: V.memset(out, x), [], writes)
+
+    def act(out, in_, f, reads, writes, bias=None, scale=None):
+        if bias is None:
+            op("a", lambda: S.activation(out, in_, f), reads, writes)
+        else:
+            op("a", lambda: S.activation(out, in_, f, bias=bias, scale=scale), reads, writes)
+
+    ps = [T["ps%d" % b] for b in range(8)]
+    for nm, hop in (("l1", 1), ("l2", 2)):
+        arrives(hop, nm, nm)
+    for b in (1, 2):
+        arrives(1, "cr%d" % b, "cr%d" % b)
+        arrives(1, "lw%d" % b, "lw%d" % b)
+        arrives(1, "lt%d" % b, "lt%d" % b)
+        arrives(1, "wl%d" % b, "win%d_0" % b)
+        arrives(1, "tl%d" % b, "tin%d_0" % b)
+    for i in range(NQ):
+        arrives(2, "fin%d" % i, "fin%d" % i)
+
+    dma("s", T.mjs[:, 0:K], T.mj[:, 0:K], [], ["mjs0"])
+    dma("a", T.mjs[:, K:W], T.mj[:, K:W], [], ["mjs1"])
+    dma("s", T.nxs[:], T.nx[:], [], ["nxs"])
+    dma("a", T.ces[:], T.ce[:], [], ["ces"])
+    dma("a", T.uz[:, 0:2, :], T.uu[:, 0:2 * K], [], ["u0"])
+    dma("s", T.uz[:, 2:4, :], T.zz[:, 0:2 * K], [], ["z0"])
+    dma("s", T.rps[:], T.rp[:], [], ["rps"])
+    for nm, src in (("sg", T.sg), ("al", T.al)):
+        dma("s", T[nm + "s"][:, P:P + W], src[:], [], [nm + "s"])
+        dma("s", T[nm + "s"][:, 0:P], src[:, W - P:W], [], [nm + "l"])
+        dma("s", T[nm + "s"][:, P + W:WP], src[:, 0:P], [], [nm + "r"])
+    for b in (1, 2):
+        for x, src in enumerate((T.uu, T.zz)):
+            c = (b - 1) * 256 + x * 128
+            dma("s", T.stg[:, c:c + 128], src[:, 2 * b * K:2 * (b + 1) * K], [], ["stg%d%d" % (b, x)])
+
+    pf = [T.pf[:, i:i + 1] for i in range(12)]
+    vq = T.vw[:, 0:128]
+    op("g", lambda: g.iota(T.vw[:], [[1, 144]], 0, -1), [], ["vw"])
+    op("g", lambda: g.iota(T.pi[:, 0:1], [[0, 1]], 0, 1), [], ["pi0"])
+    op("g", lambda: g.iota(T.vz[:], [[1, 144]], 0, -16), [], ["vz"])
+    fill(T.bb[:], -2.0, ["bb"])
+    op("g", lambda: g.affine_select(T.bb[:], T.bb[:], [[-1, 16], [-16, 8], [0, 16]], A.is_equal, 0.0, 0, 1), ["bb"], ["bb"])
+    ts(T.eq[:], vq, 0.0, None, A.is_equal, None, ["vw"], ["eq"])
+    act(T.i32[:], T.eq[:], F.Silu, ["eq"], ["i32"], 0.0, CK)
+    ts(T.pi[:, 1:2], T.pi[:, 0:1], 15, None, A.bitwise_and, None, ["pi0"], ["pi1"])
+    ts(T.ua[:], T.vz[:, 0:128], 1.0, None, A.max, None, ["vz"], ["ua"])
+    cp(pf[0], T.pi[:, 1:2], ["pi1"], ["pf0"])
+    ts(T.vz2[:], T.vz[:, 0:128], 4, None, A.arith_shift_right, None, ["vz"], ["vz2"])
+    ts(pf[8], pf[0], 15.0, None, A.is_equal, None, ["pf0"], ["pf8"])
+    ts(pf[1], pf[0], 1.0, None, A.max, None, ["pf0"], ["pf1"])
+    ts(pf[9], pf[8], -16.0, 1.0, A.mult, A.add, ["pf8"], ["pf9"])
+    ts(pf[10], pf[8], 2.0, -1.0, A.mult, A.add, ["pf8"], ["pf10"])
+    op("v", lambda: V.reciprocal(pf[5], pf[1]), ["pf1"], ["pf5"])
+    ts(T.ta[:], vq, pf[9], pf[10], A.is_equal, A.mult, ["vw", "pf9", "pf10"], ["ta"])
+    ts(T.uc[:], T.vz2[:], 0.0, -2.0 * KI, A.is_equal, A.mult, ["vz2"], ["uc"])
+    tt(T.dm[:], T.ta[:], T.eq[:], A.add, ["ta", "eq"], ["dm"])
+
+    for b in range(4):
+        c = slice(b * 512, (b + 1) * 512)
+        mk = "mjs%d" % (b // 2)
+        ts(T.f1[:, c], T.mjs[:, c], 0.375, 2.0, A.min, A.mult, [mk], ["f1%d" % b])
+        ts(T.f2[:, c], T.mjs[:, c], 0.15, 5.0, A.min, A.mult, [mk], ["f2%d" % b])
+        mms([(ps[b][:], T.i32[:], T.mjs[:, c], True, False), (ps[b][:], T.i32[:], T.f1[:, c], False, False),
+             (ps[b][:], T.i32[:], T.f2[:, c], False, True)], ["i32", mk, "f1%d" % b, "f2%d" % b], ["ps%d" % b])
+        act(T.tb0[:, P + b * 512:P + (b + 1) * 512], ps[b][:], F.Silu, ["ps%d" % b], ["tb0" if b == 3 else "tb0p%d" % b], -CK, 2.0)
+    for b in range(4, 8):
+        mms([(ps[b][:], T.dm[:], T.nxs[:, (b - 4) * 512:(b - 3) * 512], True, True)], ["dm", "nxs"], ["ps%d" % b])
+    cp(T.oc16[:, 64:128], T.ces[:], ["ces"], ["cn16"])
+    op("v", lambda: V.reciprocal(T.ua[:], T.ua[:]), ["ua"], ["ua"])
+    fill(T.dd[:], (2.0 ** 20) / KM, ["dd"])
+    op("g", lambda: g.affine_select(T.dd[:], T.dd[:], [[-256, 16], [-16, 8], [255, 16]], A.is_equal, 0.0, 0, 1), ["dd"], ["dd"])
+    tt(T.ub[:], T.ua[:], T.uc[:], A.mult, ["ua", "uc"], ["ub"])
+    cp(T.pb[:, 0:1], pf[5], ["pf5"], ["pb"])
+    ts(pf[2], pf[0], 0.0, 17.0 * KI, A.is_equal, A.add, ["pf0"], ["pf2"])
+    ts(pf[7], T.pb[:, 0:1], pf[1], -17.0 * KI, A.mult, A.mult, ["pb", "pf1"], ["pf7"])
+    ts(pf[6], pf[5], KI, pf[2], A.mult, A.add, ["pf5", "pf2"], ["pf6"])
+    ts(pf[4], pf[0], -1.0, 15.0, A.mult, A.add, ["pf0"], ["pf4"])
+    tt(pf[3], pf[6], pf[7], A.add, ["pf6", "pf7"], ["pf3"])
+    for b in range(4, 8):
+        cp(T.et[:, (b - 4) * 512:(b - 3) * 512], ps[b][:], ["ps%d" % b], ["et" if b == 7 else "etp%d" % b])
+    ts(T.cw[:], T.vw[:], pf[4], 0.5, A.is_equal, A.mult, ["vw", "pf4"], ["cw"])
+    ts(T.if32[:], vq, 0.0, None, A.is_equal, None, ["vw"], ["if32"])
+    cp(T.oc[:, 64:128], T.ces[:], ["ces"], ["cf"])
+
+    def late_constants(x):
+        if x == 0:
+            ts(T.zw[:], T.vz[:], 15.0, 4096.0, A.is_equal, A.mult, ["vz"], ["zw"])
+            fill(T.cst[:], 3072.0 / CK, ["cst"])
+        if x == 1:
+            ts(T.v2[:], T.rps[:], 2.0, None, A.mult, None, ["rps"], ["v2"])
+            ts(T.ir[:], vq, 0.0, -2.0 / KM, A.is_equal, A.mult, ["vw"], ["ir"])
+            fill(T.als[:, WP:WP + 16], -1.0, ["als0"])
+        if x == 2:
+            ts(T.vt[:], vq, 127, None, A.bitwise_and, None, ["vw"], ["vt"])
+            ts(T.sh[:], T.vt[:], 16.0, None, A.is_equal, None, ["vt"], ["sh"])
+
+    send(1, "l1", T.l1[:], [T.stg[:, 0:256]], ["stg10", "stg11"])
+    send(2, "l2", T.l2[:], [T.stg[:, 256:512]], ["stg20", "stg21"])
+
+    def unpack_uz(b):
+        r0 = 4 * (b - 1)
+        for x in range(2):
+            dma("s", T.raw[:, r0 + 2 * x:r0 + 2 * x + 2, :], T["l%d" % b][:, 128 * x:128 * (x + 1)], ["l%d" % b], ["raw%d%d" % (b, x)])
+        rk = ["raw%d0" % b, "raw%d1" % b]
+        dma("s", T.uz[:, 4 * b:4 * b + 4, 0:H], T.raw[:, r0:r0 + 4, 0:H], rk, ["uzl%d" % b])
+        dma("s", T.uz[b:8, 4 * b:4 * b + 4, H:K], T.raw[0:8 - b, r0:r0 + 4, H:K], rk, ["uzm%d" % b])
+        dma("s", T.uz[0:b, 4 * b:4 * b + 4, H:K], T.raw[8 - b:8, r0:r0 + 4, H:K], rk, ["uzn%d" % b])
+
+    def weights(t):
+        b = t // 2
+        last = t == NT - 1
+        hop = t % 2 == 1 and not last
+        prev = "win%d" % b if t % 2 == 0 else "w%d" % (t - 1)
+        w = T["w%d" % t]
+        npc = NQ if last else 2
+        pc = K // npc
+        pcs = list(range(npc))[::-1] if hop else list(range(npc))
+
+        def qk(nm, i):
+            return ["%s%d" % (nm, x) for x in range(i * NQ // npc, (i + 1) * NQ // npc)]
+
+        def o_t(i):
+            c = slice(i * pc, (i + 1) * pc)
+            src = T.als[:].indirect(T.oc16[:, i * pc // 16:(i + 1) * pc // 16])
+            hf = i * pc // H
+            if t == 0:
+                cp(T.tt[:, c], src, ["als", "all", "alr", "als0", "oa16%d" % hf], qk("tt", i))
+            else:
+                pk = ["%s_%d" % (prev, hf)] + (["%s_2" % prev] if hf == 1 else [])
+                tt(T.tt[:, c], src, T[prev][:, c], A.mult, ["als", "all", "alr", "als0", "oa16%d" % hf] + pk, qk("tt", i))
+
+        def o_y(i):
+            c = slice(i * pc, (i + 1) * pc)
+            hf = i * pc // H
+            tt(T.yy[:, c], T.tt[:, c], ps[2 + hf][:, i * pc - hf * H:(i + 1) * pc - hf * H], A.mult,
+               qk("tt", i) + ["ps%d" % (2 + hf)], qk("yy", i))
+
+        def o_c(i):
+            c = slice(i * pc, (i + 1) * pc)
+            ts(w[:, c], T.yy[:, c], 0.125, 4.0, A.max, A.min, qk("yy", i), ["w%d_%d" % (t, i)])
+            if hop:
+                nb = b + 1
+                if i == 1:
+                    send(1, "lw%d" % nb, T["lw%d" % nb][:], [w[:, c]], ["w%d_1" % t])
+                else:
+                    send(1, "wl%d" % nb, T["win%d" % nb][:, c], [w[:, c]], ["w%d_0" % t])
+            if last:
+                hf = i * pc // H
+                send(2, "fin%d" % i, T.fin[:, c], [T.tin2[:, c], T.w4[:, c], w[:, c]],
+                     ["tin2_%d" % hf, "tin2_2", "w4_%d" % hf, "w5_%d" % i])
+
+        o_t(pcs[0])
+        if last:
+            yield
+        for j in range(npc):
+            if j + 1 < npc:
+                o_t(pcs[j + 1])
+            o_y(pcs[j])
+            if j > 0:
+                o_c(pcs[j - 1])
+        yield
+        o_c(pcs[-1])
+        if hop:
+            nb = b + 1
+            lw, win, lt, tin = T["lw%d" % nb], T["win%d" % nb], T["lt%d" % nb], T["tin%d" % nb]
+            dma("s", win[16:128, H:K], lw[0:112, :], ["lw%d" % nb], ["win%d_1" % nb])
+            dma("s", win[0:16, H:K], lw[112:128, :], ["lw%d" % nb], ["win%d_2" % nb])
+            for hf in (1, 0):
+                c = slice(hf * H, (hf + 1) * H)
+                srcs = [T["w%d" % (t - 1)][:, c], w[:, c]]
+                ks = ["w%d_%d" % (t - 1, hf), "w%d_%d" % (t, hf)]
+                if b > 0:
+                    srcs.append(T["tin%d" % b][:, c])
+                    ks += ["tin%d_%d" % (b, hf), "tin%d_2" % b]
+                if hf == 1:
+                    send(1, "lt%d" % nb, lt[:], srcs, ks)
+                else:
+                    send(1, "tl%d" % nb, tin[:, c], srcs, ks)
+            dma("g", tin[16:128, H:K], lt[0:112, :], ["lt%d" % nb], ["tin%d_1" % nb])
+            dma("g", tin[0:16, H:K], lt[112:128, :], ["lt%d" % nb], ["tin%d_2" % nb])
+
+    cf = T.oc[:, 64:128]
+    for t in range(NT):
+        b = t // 2
+        last = t == NT - 1
+        hop = t % 2 == 1 and not last
+        tr, tw = "tb%d" % (t % 2), "tb%d" % (1 - t % 2)
+        iu, iz = 4 * b + t % 2, 4 * b + 2 + t % 2
+        uk = ["u0"] if b == 0 else ["uzl%d" % b, "uzm%d" % b, "uzn%d" % b]
+        zk = ["z0"] if b == 0 else uk
+        came = b > 0 and t % 2 == 0
+        cn = "cr%d" % b if came else "cn16"
+
+        def cells(h):
+            return T[cn][:, 32 * h:32 * h + 32] if came else T.oc16[:, 64 + 32 * h:96 + 32 * h]
+
+        if not last:
+            dma("s", T[tw][:, P:P + W], T[tr][:, P:P + W], [tr], [tw])
+        if t in (1, 3):
+            unpack_uz((t + 1) // 2)
+        for h in range(2):
+            c = slice(h * H, (h + 1) * H)
+            act(T.mi[:, c], T[tr][:, P:P + W].indirect(cells(h)), F.Silu, [tr, cn], ["mi%d" % h], BI, SI)
+            mms([(ps[h][:], T.ub[:], T.uz[:, iu, c], True, False)], ["ub"] + uk, ["ps%d" % h])
+            mms([(ps[h][:, k:H:16], T.bb[:, 128 * k:128 * k + 128], T.mi[:, h * H + k:(h + 1) * H:16], False, k == 15) for k in range(16)],
+                ["bb", "mi%d" % h], ["ps%d" % h])
+        for h in range(2):
+            act(T.sn[:, h * H:(h + 1) * H], ps[h][:], F.Sign, ["ps%d" % h, "pf3"], ["sn%d" % h], pf[3], -1.0)
+        act(T[tr][:, 0:P], T[tr][:, W:W + P], F.Copy, [tr], [tr + "l"])
+        act(T[tr][:, P + W:WP], T[tr][:, P:2 * P], F.Copy, [tr], [tr + "r"])
+        rest = weights(t - 1) if t > 0 else iter(())
+        next(rest, None)
+        if t == 1:
+            late_constants(2)
+        if came:
+            cp(cf, T[cn][:], [cn], ["cf"])
+        for h in range(2):
+            c = slice(h * H, (h + 1) * H)
+            tt(T.pr[:, c], T.et[:].indirect(cells(h)), T.sn[:, c], A.mult, ["et", cn, "sn%d" % h], ["pr%d" % h])
+            o = ps[4 + h][:, 0:32]
+            mms([(o, T.if32[:], T.oc[:, 64 + 32 * h:96 + 32 * h], True, False)], ["if32", "cf"], ["ps%d" % (4 + h)])
+            mms([(o, T.cw[:, 15 - k:143 - k], T.pr[:, h * H + k:(h + 1) * H:16], False, k == 15) for k in range(16)],
+                ["cw", "pr%d" % h], ["ps%d" % (4 + h)])
+        lh = [slice(0, 32), slice(32, 64)]
+
+        def part(h):
+            if h is None:
+                return ps[6][:, 0:64], "ps6", 0, K, slice(0, 64)
+            return ps[6 + h][:, 0:32], "ps%d" % (6 + h), h * H, (h + 1) * H, lh[h]
+
+        if t == 0:
+            late_constants(0)
+        for h in ((0, 1) if last else (None,)):
+            o, ok, c0, c1, l = part(h)
+            mms([(o, T.i32[:], T.cst[:, l], True, False)] +
+                [(o, T.zw[:, 15 - k:143 - k], T.uz[:, iz, c0 + k:c1:16], False, False) for k in range(16)],
+                ["i32", "cst", "zw"] + zk, [ok])
+
+        def o_0(h):
+            cp(T.c0[:, lh[h]], ps[4 + h][:, 0:32], ["ps%d" % (4 + h)], ["c0%d" % h])
+
+        def o_p(h):
+            ts(T.par[:, lh[h]], T.c0[:, lh[h]], 1, None, A.bitwise_and, None, ["c0%d" % h], ["par%d" % h])
+
+        def o_e(h):
+            tt(T.ef[:, lh[h]], T.par[:, lh[h]], T.v2[:, 64 * t + 32 * h:64 * t + 32 * h + 32], A.add, ["par%d" % h, "v2"], ["ef%d" % h])
+
+        def o_f(h):
+            cp(T.e16[:, lh[h]], T.ef[:, lh[h]], ["ef%d" % h], ["e16%d" % h])
+
+        def o_v():
+            ts(T.ev[:], T.c0[:], W - 2, None, A.bitwise_and, None, ["c00", "c01"], ["ev"])
+
+        def o_2(h):
+            ts(T.c16[:, lh[h]], ps[4 + h][:, 0:32], float(P), None, A.add, None, ["ps%d" % (4 + h)], ["c16%d" % h])
+            for q in range(h * NQ // 2, (h + 1) * NQ // 2):
+                act(T.mg[:, q * Q:(q + 1) * Q], T[tr][:].indirect(T.c16[:, q * Q // 16:(q + 1) * Q // 16]), F.Silu,
+                    [tr, tr + "l", tr + "r", "c16%d" % h], ["mg%d" % q], BM, SM)
+
+        def o_r(q):
+            c = slice(q * Q, (q + 1) * Q)
+            tt(T.rho[:, c], T.sgs[:].indirect(T.c16[:, q * Q // 16:(q + 1) * Q // 16]), T.mg[:, c], A.mult,
+               ["sgs", "sgl", "sgr", "c16%d" % (q * Q // H), "mg%d" % q], ["rho%d" % q])
+
+        def o_i(q):
+            c = slice(q * Q, (q + 1) * Q)
+            ts(T.yv[:, c], T.rho[:, c], -KM, -CK, A.is_lt, A.mult, ["rho%d" % q], ["yv%d" % q])
+
+        def o_j(q):
+            c = slice(q * Q, (q + 1) * Q)
+            l = slice(q * Q // 16, (q + 1) * Q // 16)
+            ek = "e16%d" % (q * Q // H)
+            tt(T.nw[:, c], T[tr][:, P:P + W].indirect(T.e16[:, l]), T.yv[:, c], A.add, [tr, ek, "yv%d" % q], ["nw%d" % q])
+            act(T[tw][:, P:P + W].indirect(T.e16[:, l]), T.nw[:, c], F.Silu, [ek, "nw%d" % q], [tw])
+
+        def hk(nm, h):
+            return [nm + "0", nm + "1"] if h is None else ["%s%d" % (nm, h)]
+
+        def hero(h):
+            o, ok, c0, c1, _ = part(h)
+            rk = ["rho%d" % q for q in range(c0 // Q, c1 // Q)]
+            mms([(o, T.dd[:, 128 * k:128 * k + 128], T.rho[:, c0 + k:c1:16], False, k == 15) for k in range(16)], ["dd"] + rk, [ok])
+            for x in range(c0 // H, c1 // H):
+                mms([(ps[2 + x][:], T.ir[:], T.rho[:, x * H:(x + 1) * H], True, False)], ["ir"] + rk, ["ps%d" % (2 + x)])
+
+        def d_n(h):
+            o, ok, _, _, l = part(h)
+            ts(T.nl[:, l], o, 0.0, None, A.is_gt, None, [ok], hk("nl", h))
+
+        def d_a(h):
+            o, ok, _, _, l = part(h)
+            tt(T.oc[:, l], T.c0[:, l], o, A.max, hk("c0", h) + [ok], hk("oa", h))
+
+        def d_16(h):
+            l = part(h)[4]
+            ts(T.oc16[:, l], T.oc[:, l], float(W + P), float(P), A.min, A.add, hk("oa", h), hk("oa16", h))
+
+        def d_x():
+            tt(T.xf[:], T.par[:], T.nl[:], A.is_equal, ["par0", "par1", "nl0", "nl1"], ["xf"])
+
+        def d_c():
+            tt(cf, T.ev[:], T.xf[:], A.add, ["ev", "xf"], ["cf"])
+            if hop:
+                mms([(ps[7][:, 0:32], T.if32[:], T.oc[:, 64:96], True, True), (ps[7][:, 32:64], T.sh[:], T.oc[:, 96:128], True, True)],
+                    ["if32", "sh", "cf"], ["ps7"])
+
+        def spread(h):
+            mms([(ps[2 + h][:, k:H:16], T.bb[:, 128 * k:128 * k + 128], T.nl[:, lh[h]], False, k == 15) for k in range(16)],
+                ["bb", "nl%d" % h], ["ps%d" % (2 + h)])
+
+        def d_cn():
+            if hop:
+                nb = b + 1
+                cp(T["cs%d" % nb][:], ps[7][:, 0:64], ["ps7"], ["cs%d" % nb])
+                send(1, "cr%d" % nb, T["cr%d" % nb][:], [T["cs%d" % nb][:]], ["cs%d" % nb])
+            else:
+                cp(T.oc16[:, 64:128], cf, ["cf"], ["cn16"])
+
+        o_2(0), o_0(0), next(rest, None)
+        if t == 0:
+            late_constants(1)
+        if not last:
+            o_p(0), o_2(1), o_e(0), o_0(1), o_f(0), o_r(0), o_p(1), o_i(0), o_e(1), o_j(0), o_f(1), o_r(1)
+        if last:
+            o_2(1), o_0(1), o_r(0), o_r(1), hero(0), o_r(2), o_r(3), hero(1)
+            rest = weights(t)
+            d_a(0), d_n(0), spread(0), d_16(0), next(rest), d_a(1), d_n(1), spread(1), d_16(1)
+            for _ in rest:
+                pass
+        elif hop:
+            o_r(2), o_r(3), hero(None), o_i(1), o_v(), o_j(1)
+            d_n(None), d_a(None), d_x(), d_16(None), d_c(), spread(1), spread(0), o_i(2), o_i(3), d_cn(), o_j(2), o_j(3)
+        else:
+            o_v(), o_i(1), o_r(2), o_j(1), o_r(3), hero(None), o_i(2), o_j(2)
+            d_n(None), d_a(None), spread(0), spread(1), o_i(3), d_x(), d_16(None), d_c(), o_j(3), d_cn()
+
+    for i in range(NQ):
+        c = slice(i * Q, (i + 1) * Q)
+        if i * Q < H:
+            dma("s" if i % 2 == 0 else "a", T.tl[:, c], T.fin[:, c], ["fin%d" % i], [])
+        else:
+            dma("s", T.tl[0:96, c], T.fin[32:128, c], ["fin%d" % i], [])
+            dma("a", T.tl[96:128, c], T.fin[0:32, c], ["fin%d" % i], [])
+    for s in total:
+        if max(waited[q].get(s, 0) for q in eng) < total[s]:
+            g.wait_ge(T.sem[s], total[s])

@@ -5,10 +5,10 @@ from concourse.mybir import AluOpType as A, ActivationFunctionType as F
 
 W, K, NT = 2048, 1024, 6
 H = K // 2
-NQ = 4
-Q = K // NQ
+E = K // 8
 P = 256
 WP = W + 2 * P
+RW = 160
 CK = 32.0
 KM = 2.0 ** -48
 KI = 2.0 ** -52
@@ -29,6 +29,30 @@ def _fit(e0, sign):
 SM, BM = _fit(-52, 1)
 SI, BI = _fit(-48, -1)
 
+BAR = {0: 0, 2: 1, 4: 4, 6: 4}
+SUM = {0: 5, 2: 7, 4: 7, 6: 5}
+HERO = {0: 6, 4: 7}
+ROT = {0: 0, 2: 1, 4: 1, 6: 0, 8: 1}
+FIN = [0, 2, 4, 6, 8]
+WHOLE = False
+ORDER = [
+    "copy00 u04 u48 inv04 bar04 inv48 bar48 consts00 sign04 sign48 wrap00 wrap11 +u04 cell04 cell48 +u48 ways04 ways48 consts10 add04 add48 z08 coff04 cint04 m02 m24 consts20 par04 rho02 ef04 coff48 cint48 m46 m68 flag02 eoff04 par48 rho24 old02 ef48 put02 flag24 rho46 eoff48 old24 put24 flag46 rho68 two04 hero08 two48 old46 put46 flag68 old68 put68 null08 even08 oa08 xf08 aoff08 cf08 spread48 +z04 +cell48 +cell04 spread04 noff08 +copy00 unpack10",
+    "inv04 bar04 inv48 bar48 -plain04 -plain48 -y04 -y48 -clip04 sign04 sign48 wrap11 wrap00 ways04 add04 ways48 add48 consts30 coff04 cint04 m02 m24 -clip48 par04 coff48 cint48 z48 m46 m68 ef04 rho02 par48 rho24 hero04 rho46 flag02 eoff04 rho68 hero48 two04 ef48 flag24 null04 old02 put02 xf04 even08 old24 put24 null48 cf04 oa04 eoff48 flag46 xf48 go04 oa48 flag68 cf48 spread04 two48 shift48 +u48 +u04 spread48 +z08 old46 put46 old68 put68 go48 aoff08 +copy00 unpack20 gather48",
+    "inv04 -rot48 bar04 inv48 bar48 -fused04 -y04 -clip04 -on04 cfl04 cfl48 -times48 sign04 sign48 wrap11 wrap00 cell48 +u04 cell04 -y48 ways04 ways48 add04 add48 coff04 m02 m24 cint04 -clip48 -on48 -tally00 par04 rho02 cint48 ef04 coff48 m46 m68 flag02 eoff04 par48 rho24 old02 ef48 put02 flag24 rho46 old24 put24 flag46 eoff48 rho68 two04 hero08 old46 put46 flag68 even08 old68 put68 null08 oa08 xf08 two48 spread04 spread48 +u48 aoff08 cf08 noff08 +copy00 gather48",
+    "inv04 cell48 -rot48 bar04 cell04 inv48 bar48 -fused04 -y04 -clip04 sign04 sign48 wrap00 wrap11 ways04 add04 ways48 add48 z04 -times48 coff04 cint04 m02 m24 -y48 par04 cint48 coff48 -clip48 z48 m46 m68 rho02 ef04 rho24 +u04 hero04 par48 rho46 eoff04 flag02 rho68 flag24 hero48 null04 old02 put02 ef48 xf04 even08 old24 put24 null48 cf04 oa04 flag46 xf48 eoff48 go04 flag68 cf48 two48 two04 spread04 +u48 shift48 spread48 +z08 old46 put46 old68 oa48 go48 put68 aoff08 +copy00 gather48",
+    "inv04 -rot48 bar04 inv48 bar48 -fused04 -y04 cfl04 -clip04 cfl48 -on04 sign04 wrap00 wrap11 sign48 cell04 +u04 cell48 -times48 -y48 ways04 ways48 add04 +u48 add48 coff04 m02 m24 cint04 -clip48 -on48 -tally00 par04 rho02 coff48 ef04 cint48 m46 m68 flag02 eoff04 par48 rho24 old02 put02 ef48 flag24 rho46 eoff48 old24 put24 flag46 rho68 two04 hero08 old46 put46 flag68 old68 put68 null08 even08 spread04 two48 oa08 xf08 aoff08 cf08 noff08",
+    "inv04 cell48 -spread48 z04 cell04 bar04 inv48 bar48 -fused04 -y04 sign04 -gather48 sign48 wrap00 wrap11 -rot48 -clip04 ways04 add04 ways48 add48 coff04 -times48 m02 m24 cint04 -y48 coff48 cint48 z48 m68 m46 rho02 rho24 hero04 two04 rho68 rho46 -clip48 oa04 hero48 null04 aoff04 spread04 two48 oa48 fused02 aoff48 null48 spread48 gather46 rot46 gather68 rot68 y02 fused24 clip02 y24 home02 times46 clip24 home24 y46 times68 clip46 y68 home46 clip68 home68",
+]
+ORDER = [
+'copy00 inv04 u48 u04 bar04 inv48 bar48 consts10 consts00 sign04 wrap00 sign48 wrap11 cell48 cell04 ways04 ways48 add04 +u04 +u48 z08 add48 cint04 coff04 m02 m24 consts20 par04 rho02 ef04 coff48 cint48 m46 m68 flag02 eoff04 par48 rho24 old02 put02 ef48 flag24 rho46 old24 put24 rho68 hero08 eoff48 flag46 even08 flag68 old46 old68 put48 null08 oa08 xf08 aoff08 cf08 plain04 consts30 noff08 +copy00 unpack10',
+'inv04 -two04 cell48 -two48 cell04 -spread48 -spread04 bar04 inv48 bar48 -plain48 -y48 -y04 -clip48 -clip04 sign04 sign48 wrap11 wrap00 ways04 add04 ways48 add48 coff04 cint04 m02 m24 par04 ef04 coff48 cint48 m46 m68 rho02 par48 rho24 z48 z04 hero04 flag02 eoff04 rho46 old02 rho68 two04 hero48 null04 flag24 put02 flag46 ef48 even08 xf04 old24 oa04 eoff48 put24 cf04 null48 flag68 old46 go04 xf48 old68 oa48 cf48 two48 spread04 spread48 shift48 +z08 put48 aoff08 go48 +copy00 unpack20 gather48',
+'inv04 u48 -rot48 u04 bar04 inv48 bar48 -fused04 -y04 -clip04 -on04 cfl48 sign04 wrap00 wrap11 sign48 cfl04 -times48 -y48 ways04 ways48 cell04 add04 +u04 cell48 add48 coff04 m02 m24 cint04 -clip48 par04 -on48 -tally00 rho02 coff48 ef04 cint48 m46 m68 flag02 eoff04 rho24 old02 put02 par48 flag24 rho46 ef48 old24 put24 eoff48 rho68 +u48 two04 two48 hero08 flag46 even08 flag68 old46 old68 put48 oa08 null08 xf08 cf08 aoff08 fused04 noff08 +copy00 gather48',
+'inv04 z04 -spread04 cell04 -spread48 -rot48 bar04 inv48 cell48 bar48 -y04 -clip04 -times48 sign04 sign48 wrap00 wrap11 -y48 ways04 add04 ways48 add48 coff04 cint04 m02 m24 -clip48 par04 coff48 cint48 ef04 rho02 eoff04 rho24 m68 m46 flag02 rho68 old02 rho46 +u48 z48 hero04 two04 +u04 hero48 null04 flag24 put02 oa04 even08 par48 xf04 old24 cf04 ef48 null48 oa48 put24 flag46 eoff48 xf48 go04 aoff08 flag68 cf48 spread04 two48 spread48 shift48 old46 old68 go48 gather48 put48 +copy00',
+'inv04 z08 -rot48 bar04 inv48 bar48 -fused04 -y04 cfl04 -clip04 -times48 -on04 sign04 wrap00 sign48 wrap11 cfl48 -y48 ways04 ways48 cell04 cell48 +u04 add04 add48 coff04 m02 m24 cint04 -clip48 par04 -on48 -tally00 cint48 rho02 ef04 coff48 m46 m68 flag02 eoff04 rho24 old02 put02 flag24 par48 rho46 old24 ef48 rho68 flag46 eoff48 put24 two48 two04 hero08 flag68 old46 old68 put48 even08 null08 xf08 cf08 noff08 oa08 aoff08 fused04',
+'inv04 cell04 u48 cell48 -spread04 bar04 z04 inv48 bar48 -spread48 -y04 sign04 -gather48 sign48 wrap00 wrap11 -rot48 ways04 -clip04 add04 ways48 add48 coff04 -times48 m02 m24 cint04 -y48 coff48 cint48 z48 m68 m46 rho02 rho24 hero04 rho68 rho46 two04 hero48 oa04 null04 -clip48 aoff04 spread04 two48 oa48 fused02 aoff48 null48 gather46 spread48 rot46 gather68 rot68 y02 fused24 clip02 y24 home02 times46 clip24 home24 y46 times68 clip46 y68 home46 clip68 home68',
+]
+ORDER = ['copy00 inv04 inv48 wrap11 u04 u48 bar04 bar48 consts00 consts10 sign04 wrap00 sign48 ways04 ways48 cell48 z08 +u48 cell04 add04 +u04 add48 coff04 m02 m24 cint04 par04 ef04 consts20 eoff04 rho02 cint48 coff48 m46 m68 flag02 rho24 old02 put02 flag24 par48 rho46 ef48 old24 rho68 flag46 eoff48 even08 put24 two04 hero08 flag68 old46 put46 null08 oa08 old68 consts40 xf08 consts30 aoff08 cf08 plain48 noff08 put68 +copy00 unpack10', 'inv04 -two48 z04 cell48 cell04 -spread48 -spread04 bar04 inv48 bar48 -plain04 -y48 -y04 -clip48 -clip04 sign04 wrap11 sign48 wrap00 ways04 add04 ways48 add48 coff04 cint04 m02 m24 par04 ef04 coff48 cint48 m46 m68 rho02 eoff04 rho24 flag02 rho46 old02 rho68 par48 z48 two04 hero04 hero48 two48 flag24 put02 even08 ef48 null04 old24 xf04 null48 flag46 eoff48 put24 cf04 xf48 flag68 go04 cf48 old46 put46 old68 spread04 shift48 put68 go48 oa04 oa48 aoff08 +copy00 unpack20', 'inv04 inv48 -spread48 u48 u04 bar04 bar48 -fused04 -fused48 -y04 cfl04 -y48 -clip04 cfl48 -clip48 -on04 -on48 sign04 wrap11 sign48 wrap00 ways04 ways48 cell04 +u04 cell48 z08 add04 add48 coff04 m02 m24 cint04 par04 ef04 cint48 rho02 eoff04 coff48 m46 m68 flag02 rho24 old02 put02 par48 flag24 rho46 ef48 old24 put24 flag46 eoff48 rho68 two04 +u48 hero08 even08 old46 put46 flag68 oa08 null08 old68 xf08 aoff08 nm48 cf08 put68 noff08 +copy00', 'inv04 -spread04 cell48 cell04 z04 bar04 inv48 -fused04 -arho48 -y04 -clip04 bar48 -factor48 sign04 sign48 wrap00 wrap11 ways04 ways48 +u04 add04 +u48 add48 -yu48 coff04 cint04 m02 m24 -clip48 par04 cint48 coff48 rho02 ef04 rho24 m68 m46 eoff04 flag02 rho68 old02 rho46 z48 two04 hero04 hero48 put02 null04 flag24 par48 even08 xf04 old24 ef48 null48 cf04 flag46 put24 xf48 go04 eoff48 cf48 oa04 old46 oa48 spread04 shift48 put46 go48 flag68 nm48 aoff08 old68 put68 +copy00', 'inv04 inv48 -arho48 -fused04 cfl04 -y04 z08 -factor48 cell04 bar04 bar48 sign04 wrap00 sign48 wrap11 -yu48 -clip04 cfl48 -clip48 ways04 ways48 cell48 add04 +u48 add48 coff04 m02 m24 cint04 par04 -on48 -on04 -tally00 ef04 cint48 rho02 coff48 eoff04 m46 m68 flag02 rho24 old02 put02 par48 flag24 rho46 ef48 old24 flag46 eoff48 rho68 put24 two04 hero08 old46 put46 flag68 null08 even08 old68 oa08 xf08 cf08 put68 noff08 aoff08 fused04', 'inv04 -two48 u04 -spread04 z04 -spread48 inv48 cell04 cell48 bar04 bar48 -y04 sign04 wrap00 sign48 -gather48 more00 wrap11 -clip04 ways04 add04 -rot48 ways48 add48 coff04 m02 m24 cint04 -times48 coff48 rho02 rho24 m68 m46 hero04 cint48 rho68 rho46 oa04 -y48 null04 aoff04 -clip48 z48 hero48 two04 oa48 fused02 aoff48 null48 gather46 two48 spread04 spread48 rot46 gather68 rot68 y02 fused24 clip02 y24 home02 times46 clip24 home24 y46 times68 clip46 y68 home46 clip68 home68']
+
 SCRATCH = {
     "sgs": ("sbuf", [128, WP], "bfloat16"), "als": ("sbuf", [128, WP + 16], "bfloat16"),
     "mjs": ("sbuf", [128, W], "bfloat16"), "nxs": ("sbuf", [128, W], "bfloat16"),
@@ -39,38 +63,39 @@ SCRATCH = {
     "uz": ("sbuf", [8, 12, K], "bfloat16"), "raw": ("sbuf", [8, 8, K], "bfloat16"),
     "stg": ("sbuf", [128, 512], "bfloat16"),
     "l1": ("dram", [128, 256], "bfloat16"), "l2": ("dram", [128, 256], "bfloat16"),
-    "pb": ("sbuf", [128, 2], "bfloat16"), "pi": ("sbuf", [128, 4], "int32"), "pf": ("sbuf", [128, 12], "float32"),
-    "vw": ("sbuf", [128, 144], "int32"), "vt": ("sbuf", [128, 128], "int32"),
+    "pi": ("sbuf", [128, 4], "int32"), "pf": ("sbuf", [128, 12], "float32"),
+    "vw": ("sbuf", [128, RW], "int32"), "vt": ("sbuf", [128, RW], "int32"),
+    "vb": ("sbuf", [128, 128], "int32"), "vi": ("sbuf", [128, 128], "int32"), "vm": ("sbuf", [128, 16], "int32"),
     "vz": ("sbuf", [8, 144], "int32"), "vz2": ("sbuf", [8, 128], "int32"),
-    "bb": ("sbuf", [128, W], "bfloat16"), "dd": ("sbuf", [128, W], "bfloat16"),
-    "eq": ("sbuf", [128, 128], "bfloat16"), "i32": ("sbuf", [128, 128], "bfloat16"), "ir": ("sbuf", [128, 128], "bfloat16"),
-    "if32": ("sbuf", [128, 128], "float32"), "sh": ("sbuf", [128, 128], "float32"),
+    "mk": ("sbuf", [128, 16], "float32"), "wt": ("sbuf", [128, 128], "bfloat16"), "blk": ("sbuf", [128, 128], "bfloat16"),
+    "bb": ("sbuf", [128, 16, 128], "bfloat16"), "dd": ("sbuf", [128, 16, 128], "bfloat16"), "bn": ("sbuf", [128, 16, RW], "bfloat16"),
+    "idw": ("sbuf", [128, RW], "bfloat16"), "i32": ("sbuf", [128, 128], "bfloat16"), "ir": ("sbuf", [128, RW], "bfloat16"),
+    "irf": ("sbuf", [128, RW], "float32"), "if32": ("sbuf", [128, 128], "float32"), "sh": ("sbuf", [128, 128], "float32"),
     "ta": ("sbuf", [128, 128], "bfloat16"), "dm": ("sbuf", [128, 128], "bfloat16"),
     "cw": ("sbuf", [128, 144], "float16"), "zw": ("sbuf", [8, 144], "bfloat16"),
-    "ua": ("sbuf", [8, 128], "float32"), "uc": ("sbuf", [8, 128], "float32"), "ub": ("sbuf", [8, 128], "bfloat16"),
-    "cst": ("sbuf", [128, 64], "bfloat16"),
+    "ub": ("sbuf", [8, 128], "bfloat16"), "cst": ("sbuf", [128, 64], "bfloat16"),
     "mi": ("sbuf", [128, K], "bfloat16"), "sn": ("sbuf", [128, K], "bfloat16"), "pr": ("sbuf", [128, K], "float16"),
     "mg": ("sbuf", [128, K], "bfloat16"), "rho": ("sbuf", [128, K], "bfloat16"), "yv": ("sbuf", [128, K], "bfloat16"),
+    "ag": ("sbuf", [128, K], "bfloat16"),
     "nw": ("sbuf", [128, K], "float32"), "tt": ("sbuf", [128, K], "float32"), "yy": ("sbuf", [128, K], "float32"),
     "oc": ("sbuf", [128, 128], "float32"), "oc16": ("sbuf", [128, 128], "uint16"),
     "c0": ("sbuf", [128, 64], "int32"), "c16": ("sbuf", [128, 64], "uint16"),
     "par": ("sbuf", [128, 64], "int32"), "ef": ("sbuf", [128, 64], "float32"), "e16": ("sbuf", [128, 64], "uint16"),
-    "ev": ("sbuf", [128, 64], "int32"), "nl": ("sbuf", [128, 64], "bfloat16"), "xf": ("sbuf", [128, 64], "float32"),
-    "fin": ("sbuf", [128, K], "float32"),
+    "ev": ("sbuf", [128, 64], "int32"), "nl": ("sbuf", [128, 64], "bfloat16"), "nm": ("sbuf", [128, 32], "bfloat16"),
+    "xf": ("sbuf", [128, 64], "float32"),
+    "fin": ("sbuf", [128, K], "float32"), "tin": ("sbuf", [128, K], "float32"), "res": ("sbuf", [128, K], "float32"),
 }
 for _b in (1, 2):
     SCRATCH["cs%d" % _b] = ("sbuf", [128, 64], "uint16")
     SCRATCH["cr%d" % _b] = ("sbuf", [128, 64], "uint16")
     SCRATCH["win%d" % _b] = ("sbuf", [128, K], "float32")
-    SCRATCH["tin%d" % _b] = ("sbuf", [128, K], "float32")
-    SCRATCH["lw%d" % _b] = ("dram", [128, H], "float32")
-    SCRATCH["lt%d" % _b] = ("dram", [128, H], "float32")
 for _t in range(NT):
     SCRATCH["w%d" % _t] = ("sbuf", [128, K], "float32")
 for _b in range(8):
     SCRATCH["ps%d" % _b] = ("psum", [128, 512], "float32")
 
-ARR = ["l1", "l2", "cr1", "cr2", "lw1", "lw2", "lt1", "lt2", "wl1", "wl2", "tl1", "tl2"] + ["fin%d" % i for i in range(NQ)]
+ARR = ["l1", "l2", "tin"] + ["%s%d_%d" % (_n, _b, _h) for _n in ("cr", "win") for _b in (1, 2) for _h in (0, 1) if not (WHOLE and _n == "cr" and _h)] \
+    + ["fin%d" % i for i in range(len(FIN) - 1)]
 SEMAPHORES = ["qv", "qa", "qp", "qg", "ls"] + ["r_" + n for n in ARR] + ["d%d" % i for i in range(64)]
 
 
@@ -118,11 +143,11 @@ def rank_program(g, core, T, topo):
         fn().then_inc(T.sem["q" + q], 1)
         note(("q" + q, cnt[q], q), reads, writes)
 
-    def dma(q, out, in_, reads, writes):
+    def dma(q, out, in_, reads, writes, accum=None):
         order(q, reads, writes)
         s = "d%d" % cnt["d"]
         cnt["d"] += 1
-        eng[q].dma_start(out, in_).then_inc(T.sem[s], 16)
+        (eng[q].dma_start(out, in_, accum_op=accum) if accum is not None else eng[q].dma_start(out, in_)).then_inc(T.sem[s], 16)
         note((s, 16, None), reads, writes)
 
     def mms(lst, reads, writes):
@@ -147,9 +172,15 @@ def rank_program(g, core, T, topo):
         cnt["ls"] += len(topo.engines(core, dst))
         total["ls"] = cnt["ls"]
 
-    def arrives(hop, name, key):
+    def ek(nm, a, b):
+        return ["%s%d" % (nm, x) for x in range(a, b)]
+
+    def arrives(hop, name):
         src = T.cores[(rank - hop) % n]
-        note(("r_" + name, len(topo.engines(src, core)), None), [], [key])
+        keys = ek(name[:-1], 4 * int(name[-1]), 4 * int(name[-1]) + 4) if "_" in name else [name]
+        if WHOLE and name.startswith("cr"):
+            keys = ek(name[:-1], 0, 8)
+        note(("r_" + name, len(topo.engines(src, core)), None), [], keys)
 
     V, S = g.vector, g.scalar
 
@@ -175,28 +206,24 @@ def rank_program(g, core, T, topo):
             op("a", lambda: S.activation(out, in_, f, bias=bias, scale=scale), reads, writes)
 
     ps = [T["ps%d" % b] for b in range(8)]
-    for nm, hop in (("l1", 1), ("l2", 2)):
-        arrives(hop, nm, nm)
-    for b in (1, 2):
-        arrives(1, "cr%d" % b, "cr%d" % b)
-        arrives(1, "lw%d" % b, "lw%d" % b)
-        arrives(1, "lt%d" % b, "lt%d" % b)
-        arrives(1, "wl%d" % b, "win%d_0" % b)
-        arrives(1, "tl%d" % b, "tin%d_0" % b)
-    for i in range(NQ):
-        arrives(2, "fin%d" % i, "fin%d" % i)
+    for nm in ARR:
+        arrives(2 if nm == "l2" or nm.startswith("fin") else -1 if nm == "tin" else 1, nm)
 
-    dma("s", T.mjs[:, 0:K], T.mj[:, 0:K], [], ["mjs0"])
-    dma("a", T.mjs[:, K:W], T.mj[:, K:W], [], ["mjs1"])
-    dma("s", T.nxs[:], T.nx[:], [], ["nxs"])
-    dma("a", T.ces[:], T.ce[:], [], ["ces"])
-    dma("a", T.uz[:, 0:2, :], T.uu[:, 0:2 * K], [], ["u0"])
-    dma("s", T.uz[:, 2:4, :], T.zz[:, 0:2 * K], [], ["z0"])
-    dma("s", T.rps[:], T.rp[:], [], ["rps"])
-    for nm, src in (("sg", T.sg), ("al", T.al)):
+    def wrapped(nm, src):
         dma("s", T[nm + "s"][:, P:P + W], src[:], [], [nm + "s"])
         dma("s", T[nm + "s"][:, 0:P], src[:, W - P:W], [], [nm + "l"])
         dma("s", T[nm + "s"][:, P + W:WP], src[:, 0:P], [], [nm + "r"])
+
+    dma("s", T.mjs[:, 0:K], T.mj[:, 0:K], [], ["mjs0"])
+    dma("a", T.mjs[:, K:W], T.mj[:, K:W], [], ["mjs1"])
+    dma("s", T.ces[:], T.ce[:], [], ["ces"])
+    dma("a", T.nxs[:, 0:K], T.nx[:, 0:K], [], ["nxs0"])
+    dma("s", T.nxs[:, K:W], T.nx[:, K:W], [], ["nxs1"])
+    dma("a", T.uz[:, 0:2, :], T.uu[:, 0:2 * K], [], ["u0"])
+    wrapped("sg", T.sg)
+    dma("s", T.rps[:], T.rp[:], [], ["rps"])
+    dma("s", T.uz[:, 2:4, :], T.zz[:, 0:2 * K], [], ["z0"])
+    wrapped("al", T.al)
     for b in (1, 2):
         for x, src in enumerate((T.uu, T.zz)):
             c = (b - 1) * 256 + x * 128
@@ -204,67 +231,74 @@ def rank_program(g, core, T, topo):
 
     pf = [T.pf[:, i:i + 1] for i in range(12)]
     vq = T.vw[:, 0:128]
-    op("g", lambda: g.iota(T.vw[:], [[1, 144]], 0, -1), [], ["vw"])
-    op("g", lambda: g.iota(T.pi[:, 0:1], [[0, 1]], 0, 1), [], ["pi0"])
+    eq = T.idw[:, 0:128]
+    op("g", lambda: g.iota(T.vw[:], [[1, RW]], 0, -1), [], ["vw"])
+    op("g", lambda: g.iota(T.vb[:], [[-16, 8], [0, 16]], 0, 1), [], ["vb"])
+    op("g", lambda: g.iota(T.vi[:], [[0, 8], [1, 16]], 0, 0), [], ["vi"])
     op("g", lambda: g.iota(T.vz[:], [[1, 144]], 0, -16), [], ["vz"])
-    fill(T.bb[:], -2.0, ["bb"])
-    op("g", lambda: g.affine_select(T.bb[:], T.bb[:], [[-1, 16], [-16, 8], [0, 16]], A.is_equal, 0.0, 0, 1), ["bb"], ["bb"])
-    ts(T.eq[:], vq, 0.0, None, A.is_equal, None, ["vw"], ["eq"])
-    act(T.i32[:], T.eq[:], F.Silu, ["eq"], ["i32"], 0.0, CK)
-    ts(T.pi[:, 1:2], T.pi[:, 0:1], 15, None, A.bitwise_and, None, ["pi0"], ["pi1"])
-    ts(T.ua[:], T.vz[:, 0:128], 1.0, None, A.max, None, ["vz"], ["ua"])
-    cp(pf[0], T.pi[:, 1:2], ["pi1"], ["pf0"])
-    ts(T.vz2[:], T.vz[:, 0:128], 4, None, A.arith_shift_right, None, ["vz"], ["vz2"])
-    ts(pf[8], pf[0], 15.0, None, A.is_equal, None, ["pf0"], ["pf8"])
-    ts(pf[1], pf[0], 1.0, None, A.max, None, ["pf0"], ["pf1"])
-    ts(pf[9], pf[8], -16.0, 1.0, A.mult, A.add, ["pf8"], ["pf9"])
-    ts(pf[10], pf[8], 2.0, -1.0, A.mult, A.add, ["pf8"], ["pf10"])
-    op("v", lambda: V.reciprocal(pf[5], pf[1]), ["pf1"], ["pf5"])
-    ts(T.ta[:], vq, pf[9], pf[10], A.is_equal, A.mult, ["vw", "pf9", "pf10"], ["ta"])
-    ts(T.uc[:], T.vz2[:], 0.0, -2.0 * KI, A.is_equal, A.mult, ["vz2"], ["uc"])
-    tt(T.dm[:], T.ta[:], T.eq[:], A.add, ["ta", "eq"], ["dm"])
+    op("g", lambda: g.iota(T.pi[:, 0:1], [[0, 1]], 0, 1), [], ["pi0"])
+    op("g", lambda: g.iota(T.dd[:], [[0, W]], 0, 0, allow_small_or_imprecise_dtypes=True), [], ["dd"])
+    op("g", lambda: g.affine_select(T.dd[:], T.dd[:], [[-256, 16], [-16, 8], [255, 16]], A.not_equal, (2.0 ** 20) / KM, 0, 1), ["dd"], ["dd"])
 
+    def make_bn(c0, ng, key):
+        v = T.bn[:, :, c0:c0 + 16 * ng]
+        op("g", lambda: g.iota(v, [[0, 256 * ng]], -2, 0, allow_small_or_imprecise_dtypes=True), [], [key])
+        op("g", lambda: g.affine_select(v, v, [[-1, 16], [-16, ng], [0, 16]], A.is_equal, 0.0, 0, 1), [key], [key])
+
+    make_bn(0, 8, "bn")
+    ts(T.vt[:], T.vw[:], 127, None, A.bitwise_and, None, ["vw"], ["vt"])
+    ts(T.vm[:], T.vw[:, 0:16], 15, None, A.bitwise_and, None, ["vw"], ["vm"])
+    ts(T.vb[:], T.vb[:], 4, None, A.arith_shift_right, None, ["vb"], ["vb"])
+    ts(T.idw[:], T.vt[:], 0.0, None, A.is_equal, None, ["vt"], ["idw"])
+    act(T.i32[:], eq, F.Silu, ["idw"], ["i32"], 0.0, CK)
+    ts(T.mk[:], T.vm[:], 0.0, None, A.is_equal, None, ["vm"], ["mk"])
+    ts(T.wt[:], T.vb[:], 0.0, 1.0 / KI, A.is_equal, A.mult, ["vb"], ["wt"])
+    ts(pf[0], T.mk[:, 15:16], -16.0, 1.0, A.mult, A.add, ["mk"], ["pf0"])
+    ts(pf[1], T.mk[:, 15:16], 2.0, -1.0, A.mult, A.add, ["mk"], ["pf1"])
+    tt(T.blk[:], T.wt[:], T.vi[:], A.mult, ["wt", "vi"], ["blk"])
+    ts(T.ta[:], vq, pf[0], pf[1], A.is_equal, A.mult, ["vw", "pf0", "pf1"], ["ta"])
+    ts(T.vz2[:], T.vz[:, 0:128], 4, None, A.arith_shift_right, None, ["vz"], ["vz2"])
+    tt(T.dm[:], T.ta[:], eq, A.add, ["ta", "idw"], ["dm"])
+    ts(T.ub[:], T.vz2[:], 0.0, None, A.is_equal, None, ["vz2"], ["ub"])
+    ts(T.pi[:, 1:2], T.pi[:, 0:1], 15, None, A.bitwise_and, None, ["pi0"], ["pi1"])
+
+    blocks = [slice(b * 512, (b + 1) * 512) for b in range(4)]
     for b in range(4):
-        c = slice(b * 512, (b + 1) * 512)
-        mk = "mjs%d" % (b // 2)
-        ts(T.f1[:, c], T.mjs[:, c], 0.375, 2.0, A.min, A.mult, [mk], ["f1%d" % b])
-        ts(T.f2[:, c], T.mjs[:, c], 0.15, 5.0, A.min, A.mult, [mk], ["f2%d" % b])
-        mms([(ps[b][:], T.i32[:], T.mjs[:, c], True, False), (ps[b][:], T.i32[:], T.f1[:, c], False, False),
-             (ps[b][:], T.i32[:], T.f2[:, c], False, True)], ["i32", mk, "f1%d" % b, "f2%d" % b], ["ps%d" % b])
-        act(T.tb0[:, P + b * 512:P + (b + 1) * 512], ps[b][:], F.Silu, ["ps%d" % b], ["tb0" if b == 3 else "tb0p%d" % b], -CK, 2.0)
-    for b in range(4, 8):
-        mms([(ps[b][:], T.dm[:], T.nxs[:, (b - 4) * 512:(b - 3) * 512], True, True)], ["dm", "nxs"], ["ps%d" % b])
-    cp(T.oc16[:, 64:128], T.ces[:], ["ces"], ["cn16"])
-    op("v", lambda: V.reciprocal(T.ua[:], T.ua[:]), ["ua"], ["ua"])
-    fill(T.dd[:], (2.0 ** 20) / KM, ["dd"])
-    op("g", lambda: g.affine_select(T.dd[:], T.dd[:], [[-256, 16], [-16, 8], [255, 16]], A.is_equal, 0.0, 0, 1), ["dd"], ["dd"])
-    tt(T.ub[:], T.ua[:], T.uc[:], A.mult, ["ua", "uc"], ["ub"])
-    cp(T.pb[:, 0:1], pf[5], ["pf5"], ["pb"])
-    ts(pf[2], pf[0], 0.0, 17.0 * KI, A.is_equal, A.add, ["pf0"], ["pf2"])
-    ts(pf[7], T.pb[:, 0:1], pf[1], -17.0 * KI, A.mult, A.mult, ["pb", "pf1"], ["pf7"])
-    ts(pf[6], pf[5], KI, pf[2], A.mult, A.add, ["pf5", "pf2"], ["pf6"])
-    ts(pf[4], pf[0], -1.0, 15.0, A.mult, A.add, ["pf0"], ["pf4"])
-    tt(pf[3], pf[6], pf[7], A.add, ["pf6", "pf7"], ["pf3"])
-    for b in range(4, 8):
-        cp(T.et[:, (b - 4) * 512:(b - 3) * 512], ps[b][:], ["ps%d" % b], ["et" if b == 7 else "etp%d" % b])
-    ts(T.cw[:], T.vw[:], pf[4], 0.5, A.is_equal, A.mult, ["vw", "pf4"], ["cw"])
-    ts(T.if32[:], vq, 0.0, None, A.is_equal, None, ["vw"], ["if32"])
-    cp(T.oc[:, 64:128], T.ces[:], ["ces"], ["cf"])
+        c, mk = blocks[b], "mjs%d" % (b // 2)
+        ts(T.f1[:, c], T.mjs[:, c], 1.0 / 6, 12.0, A.min, A.mult, [mk], ["f1%d" % b])
+        ts(T.f2[:, c], T.mjs[:, c], 0.75, 4.0, A.min, A.mult, [mk], ["f2%d" % b])
+        mms([(ps[b][:], T.i32[:], T.f1[:, c], True, False), (ps[b][:], T.i32[:], T.f2[:, c], False, True)],
+            ["i32", "f1%d" % b, "f2%d" % b], ["ps%d" % b])
+        act(T.tb0[:, P + b * 512:P + (b + 1) * 512], ps[b][:], F.Silu, ["ps%d" % b], ["tb0" if b == 3 else "tb0p%d" % b], -CK, 1.0)
+    for b in range(4):
+        mms([(ps[4 + b][:], T.dm[:], T.nxs[:, blocks[b]], True, True)], ["dm", "nxs%d" % (b // 2)], ["ps%d" % (4 + b)])
+    cp(T.oc16[:, 64:128], T.ces[:], ["ces"], ek("cn16", 0, 8))
+    for k in range(16):
+        ts(T.bb[:, k, :], T.blk[:], T.mk[:, k:k + 1], None, A.mult, None, ["blk", "mk"], ["bb"] if k == 15 else [])
+    for b in (0, 1, 2, 3):
+        cp(T.et[:, blocks[b]], ps[4 + b][:], ["ps%d" % (4 + b)], ["et" if b == 3 else "etp%d" % b])
 
     def late_constants(x):
         if x == 0:
+            ts(pf[4], T.pi[:, 1:2], -1.0, 15.0, A.mult, A.add, ["pi1"], ["pf4"])
+            ts(T.if32[:], vq, 0.0, None, A.is_equal, None, ["vw"], ["if32"])
+            cp(T.oc[:, 64:128], T.ces[:], ["ces"], ek("cf", 0, 8))
+            ts(T.cw[:], T.vw[:, 0:144], pf[4], 0.5, A.is_equal, A.mult, ["vw", "pf4"], ["cw"])
+        if x == 1:
             ts(T.zw[:], T.vz[:], 15.0, 4096.0, A.is_equal, A.mult, ["vz"], ["zw"])
             fill(T.cst[:], 3072.0 / CK, ["cst"])
-        if x == 1:
             ts(T.v2[:], T.rps[:], 2.0, None, A.mult, None, ["rps"], ["v2"])
-            ts(T.ir[:], vq, 0.0, -2.0 / KM, A.is_equal, A.mult, ["vw"], ["ir"])
-            fill(T.als[:, WP:WP + 16], -1.0, ["als0"])
         if x == 2:
-            ts(T.vt[:], vq, 127, None, A.bitwise_and, None, ["vw"], ["vt"])
-            ts(T.sh[:], T.vt[:], 16.0, None, A.is_equal, None, ["vt"], ["sh"])
+            ts(T.ir[:], T.idw[:], -2.0 / KM, None, A.mult, None, ["idw"], ["ir"])
+            fill(T.als[:, WP:WP + 16], -1.0, ["als0"])
+        if x == 3:
+            ts(T.sh[:], T.vt[:, 0:128], 16.0, None, A.is_equal, None, ["vt"], ["sh"])
+        if x == 4:
+            ts(T.irf[:], T.idw[:], -2.0 / KM, None, A.mult, None, ["idw"], ["irf"])
 
     send(1, "l1", T.l1[:], [T.stg[:, 0:256]], ["stg10", "stg11"])
     send(2, "l2", T.l2[:], [T.stg[:, 256:512]], ["stg20", "stg21"])
+    make_bn(128, 2, "bn2")
 
     def unpack_uz(b):
         r0 = 4 * (b - 1)
@@ -275,241 +309,245 @@ def rank_program(g, core, T, topo):
         dma("s", T.uz[b:8, 4 * b:4 * b + 4, H:K], T.raw[0:8 - b, r0:r0 + 4, H:K], rk, ["uzm%d" % b])
         dma("s", T.uz[0:b, 4 * b:4 * b + 4, H:K], T.raw[8 - b:8, r0:r0 + 4, H:K], rk, ["uzn%d" % b])
 
-    def weights(t):
-        b = t // 2
-        last = t == NT - 1
-        hop = t % 2 == 1 and not last
-        prev = "win%d" % b if t % 2 == 0 else "w%d" % (t - 1)
-        w = T["w%d" % t]
-        npc = NQ if last else 2
-        pc = K // npc
-        pcs = list(range(npc))[::-1] if hop else list(range(npc))
+    def cols(a, b):
+        return slice(a * E, b * E)
 
-        def qk(nm, i):
-            return ["%s%d" % (nm, x) for x in range(i * NQ // npc, (i + 1) * NQ // npc)]
+    def lst(a, b, at=0):
+        return slice(at + a * 8, at + b * 8)
 
-        def o_t(i):
-            c = slice(i * pc, (i + 1) * pc)
-            src = T.als[:].indirect(T.oc16[:, i * pc // 16:(i + 1) * pc // 16])
-            hf = i * pc // H
-            if t == 0:
-                cp(T.tt[:, c], src, ["als", "all", "alr", "als0", "oa16%d" % hf], qk("tt", i))
-            else:
-                pk = ["%s_%d" % (prev, hf)] + (["%s_2" % prev] if hf == 1 else [])
-                tt(T.tt[:, c], src, T[prev][:, c], A.mult, ["als", "all", "alr", "als0", "oa16%d" % hf] + pk, qk("tt", i))
-
-        def o_y(i):
-            c = slice(i * pc, (i + 1) * pc)
-            hf = i * pc // H
-            tt(T.yy[:, c], T.tt[:, c], ps[2 + hf][:, i * pc - hf * H:(i + 1) * pc - hf * H], A.mult,
-               qk("tt", i) + ["ps%d" % (2 + hf)], qk("yy", i))
-
-        def o_c(i):
-            c = slice(i * pc, (i + 1) * pc)
-            ts(w[:, c], T.yy[:, c], 0.125, 4.0, A.max, A.min, qk("yy", i), ["w%d_%d" % (t, i)])
-            if hop:
-                nb = b + 1
-                if i == 1:
-                    send(1, "lw%d" % nb, T["lw%d" % nb][:], [w[:, c]], ["w%d_1" % t])
-                else:
-                    send(1, "wl%d" % nb, T["win%d" % nb][:, c], [w[:, c]], ["w%d_0" % t])
-            if last:
-                hf = i * pc // H
-                send(2, "fin%d" % i, T.fin[:, c], [T.tin2[:, c], T.w4[:, c], w[:, c]],
-                     ["tin2_%d" % hf, "tin2_2", "w4_%d" % hf, "w5_%d" % i])
-
-        o_t(pcs[0])
-        if last:
-            yield
-        for j in range(npc):
-            if j + 1 < npc:
-                o_t(pcs[j + 1])
-            o_y(pcs[j])
-            if j > 0:
-                o_c(pcs[j - 1])
-        yield
-        o_c(pcs[-1])
-        if hop:
-            nb = b + 1
-            lw, win, lt, tin = T["lw%d" % nb], T["win%d" % nb], T["lt%d" % nb], T["tin%d" % nb]
-            dma("s", win[16:128, H:K], lw[0:112, :], ["lw%d" % nb], ["win%d_1" % nb])
-            dma("s", win[0:16, H:K], lw[112:128, :], ["lw%d" % nb], ["win%d_2" % nb])
-            for hf in (1, 0):
-                c = slice(hf * H, (hf + 1) * H)
-                srcs = [T["w%d" % (t - 1)][:, c], w[:, c]]
-                ks = ["w%d_%d" % (t - 1, hf), "w%d_%d" % (t, hf)]
-                if b > 0:
-                    srcs.append(T["tin%d" % b][:, c])
-                    ks += ["tin%d_%d" % (b, hf), "tin%d_2" % b]
-                if hf == 1:
-                    send(1, "lt%d" % nb, lt[:], srcs, ks)
-                else:
-                    send(1, "tl%d" % nb, tin[:, c], srcs, ks)
-            dma("g", tin[16:128, H:K], lt[0:112, :], ["lt%d" % nb], ["tin%d_1" % nb])
-            dma("g", tin[0:16, H:K], lt[112:128, :], ["lt%d" % nb], ["tin%d_2" % nb])
-
-    cf = T.oc[:, 64:128]
-    for t in range(NT):
-        b = t // 2
-        last = t == NT - 1
-        hop = t % 2 == 1 and not last
+    def step(t):
+        st = t // 2
         tr, tw = "tb%d" % (t % 2), "tb%d" % (1 - t % 2)
-        iu, iz = 4 * b + t % 2, 4 * b + 2 + t % 2
-        uk = ["u0"] if b == 0 else ["uzl%d" % b, "uzm%d" % b, "uzn%d" % b]
-        zk = ["z0"] if b == 0 else uk
-        came = b > 0 and t % 2 == 0
-        cn = "cr%d" % b if came else "cn16"
+        iu, iz = 4 * st + t % 2, 4 * st + 2 + t % 2
+        uk = ["u0"] if st == 0 else ["uzl%d" % st, "uzm%d" % st, "uzn%d" % st]
+        zk = ["z0"] if st == 0 else uk
+        came = st > 0 and t % 2 == 0
+        prev = "win%d" % st if t % 2 == 0 else "w%d" % (t - 1)
+        w = T["w%d" % t]
 
-        def cells(h):
-            return T[cn][:, 32 * h:32 * h + 32] if came else T.oc16[:, 64 + 32 * h:96 + 32 * h]
+        def cells(a, b):
+            return T["cr%d" % st][:, lst(a, b)] if came else T.oc16[:, lst(a, b, 64)]
 
-        if not last:
+        def cn(a, b):
+            return ek("cr%d_" % st if came else "cn16", a, b)
+
+        def bank(table, a, n):
+            at = 8 * a if table is SUM else 0
+            return ps[table[a]][:, at:at + n], "ps%d" % table[a]
+
+        def classes(tile, a, b):
+            return [tile[:, a * E + k:b * E:16] for k in range(16)]
+
+        def copy(a, b):
             dma("s", T[tw][:, P:P + W], T[tr][:, P:P + W], [tr], [tw])
-        if t in (1, 3):
-            unpack_uz((t + 1) // 2)
-        for h in range(2):
-            c = slice(h * H, (h + 1) * H)
-            act(T.mi[:, c], T[tr][:, P:P + W].indirect(cells(h)), F.Silu, [tr, cn], ["mi%d" % h], BI, SI)
-            mms([(ps[h][:], T.ub[:], T.uz[:, iu, c], True, False)], ["ub"] + uk, ["ps%d" % h])
-            mms([(ps[h][:, k:H:16], T.bb[:, 128 * k:128 * k + 128], T.mi[:, h * H + k:(h + 1) * H:16], False, k == 15) for k in range(16)],
-                ["bb", "mi%d" % h], ["ps%d" % h])
-        for h in range(2):
-            act(T.sn[:, h * H:(h + 1) * H], ps[h][:], F.Sign, ["ps%d" % h, "pf3"], ["sn%d" % h], pf[3], -1.0)
-        act(T[tr][:, 0:P], T[tr][:, W:W + P], F.Copy, [tr], [tr + "l"])
-        act(T[tr][:, P + W:WP], T[tr][:, P:2 * P], F.Copy, [tr], [tr + "r"])
-        rest = weights(t - 1) if t > 0 else iter(())
-        next(rest, None)
-        if t == 1:
-            late_constants(2)
-        if came:
-            cp(cf, T[cn][:], [cn], ["cf"])
-        for h in range(2):
-            c = slice(h * H, (h + 1) * H)
-            tt(T.pr[:, c], T.et[:].indirect(cells(h)), T.sn[:, c], A.mult, ["et", cn, "sn%d" % h], ["pr%d" % h])
-            o = ps[4 + h][:, 0:32]
-            mms([(o, T.if32[:], T.oc[:, 64 + 32 * h:96 + 32 * h], True, False)], ["if32", "cf"], ["ps%d" % (4 + h)])
-            mms([(o, T.cw[:, 15 - k:143 - k], T.pr[:, h * H + k:(h + 1) * H:16], False, k == 15) for k in range(16)],
-                ["cw", "pr%d" % h], ["ps%d" % (4 + h)])
-        lh = [slice(0, 32), slice(32, 64)]
 
-        def part(h):
-            if h is None:
-                return ps[6][:, 0:64], "ps6", 0, K, slice(0, 64)
-            return ps[6 + h][:, 0:32], "ps%d" % (6 + h), h * H, (h + 1) * H, lh[h]
+        def wrap(a, b):
+            if a == 0:
+                act(T[tr][:, 0:P], T[tr][:, W:W + P], F.Copy, [tr], [tr + "l"])
+            else:
+                act(T[tr][:, P + W:WP], T[tr][:, P:2 * P], F.Copy, [tr], [tr + "r"])
 
-        if t == 0:
-            late_constants(0)
-        for h in ((0, 1) if last else (None,)):
-            o, ok, c0, c1, l = part(h)
-            mms([(o, T.i32[:], T.cst[:, l], True, False)] +
-                [(o, T.zw[:, 15 - k:143 - k], T.uz[:, iz, c0 + k:c1:16], False, False) for k in range(16)],
+        def u(a, b):
+            o, ok = bank(BAR, a, (b - a) * E)
+            mms([(o, T.ub[:], T.uz[:, iu, cols(a, b)], True, False)], ["ub"] + uk, [ok])
+
+        def inv(a, b):
+            act(T.mi[:, cols(a, b)], T[tr][:, P:P + W].indirect(cells(a, b)), F.Silu, [tr] + cn(a, b), ek("mi", a, b), BI, SI)
+
+        def bar(a, b):
+            mms([(ps[BAR[a]][:, k:(b - a) * E:16], T.bb[:, k, :], x, False, k == 15) for k, x in enumerate(classes(T.mi, a, b))],
+                ["bb"] + ek("mi", a, b), ["ps%d" % BAR[a]])
+
+        def sign(a, b):
+            o, ok = bank(BAR, a, (b - a) * E)
+            act(T.sn[:, cols(a, b)], o, F.Sign, [ok], ek("sn", a, b), 0.5, 1.0)
+
+        def ways(a, b):
+            tt(T.pr[:, cols(a, b)], T.et[:].indirect(cells(a, b)), T.sn[:, cols(a, b)], A.mult, ["et"] + cn(a, b) + ek("sn", a, b), ek("pr", a, b))
+
+        def cfl(a, b):
+            cp(T.oc[:, lst(a, b, 64)], cells(a, b), cn(a, b), ek("cf", a, b))
+
+        def cell(a, b):
+            o, ok = bank(SUM, a, (b - a) * 8)
+            mms([(o, T.if32[:], T.oc[:, lst(a, b, 64)], True, False)], ["if32"] + ek("cf", a, b), [ok])
+
+        def add(a, b):
+            o, ok = bank(SUM, a, (b - a) * 8)
+            mms([(o, T.cw[:, 15 - k:143 - k], x, False, k == 15) for k, x in enumerate(classes(T.pr, a, b))], ["cw"] + ek("pr", a, b), [ok])
+
+        def cint(a, b):
+            o, ok = bank(SUM, a, (b - a) * 8)
+            cp(T.c0[:, lst(a, b)], o, [ok], ek("c0", a, b))
+
+        def coff(a, b):
+            o, ok = bank(SUM, a, (b - a) * 8)
+            ts(T.c16[:, lst(a, b)], o, float(P), None, A.add, None, [ok], ek("c16", a, b))
+
+        def m(a, b):
+            act(T.mg[:, cols(a, b)], T[tr][:].indirect(T.c16[:, lst(a, b)]), F.Silu, [tr, tr + "l", tr + "r"] + ek("c16", a, b), ek("mg", a, b), BM, SM)
+
+        def par(a, b):
+            ts(T.par[:, lst(a, b)], T.c0[:, lst(a, b)], 1, None, A.bitwise_and, None, ek("c0", a, b), ek("par", a, b))
+
+        def ef(a, b):
+            tt(T.ef[:, lst(a, b)], T.par[:, lst(a, b)], T.v2[:, lst(a, b, 64 * t)], A.add, ek("par", a, b) + ["v2"], ek("ef", a, b))
+
+        def eoff(a, b):
+            cp(T.e16[:, lst(a, b)], T.ef[:, lst(a, b)], ek("ef", a, b), ek("e16", a, b))
+
+        def even(a, b):
+            ts(T.ev[:, lst(a, b)], T.c0[:, lst(a, b)], W - 2, None, A.bitwise_and, None, ek("c0", a, b), ek("ev", a, b))
+
+        def rho(a, b):
+            c = cols(a, b)
+            tt(T.rho[:, c], T.sgs[:].indirect(T.c16[:, lst(a, b)]), T.mg[:, c], A.mult, ["sgs", "sgl", "sgr"] + ek("c16", a, b) + ek("mg", a, b), ek("rho", a, b))
+
+        def flag(a, b):
+            ts(T.yv[:, cols(a, b)], T.rho[:, cols(a, b)], -KM, -CK, A.is_lt, A.mult, ek("rho", a, b), ek("yv", a, b))
+
+        def old(a, b):
+            c = cols(a, b)
+            tt(T.nw[:, c], T[tr][:, P:P + W].indirect(T.e16[:, lst(a, b)]), T.yv[:, c], A.add, [tr] + ek("e16", a, b) + ek("yv", a, b), ek("nw", a, b))
+
+        def put(a, b):
+            act(T[tw][:, P:P + W].indirect(T.e16[:, lst(a, b)]), T.nw[:, cols(a, b)], F.Silu, ek("e16", a, b) + ek("nw", a, b), [tw])
+
+        def z(a, b):
+            o, ok = bank(HERO, a, (b - a) * 8)
+            mms([(o, T.i32[:], T.cst[:, lst(a, b)], True, False)] +
+                [(o, T.zw[:, 15 - k:143 - k], T.uz[:, iz, a * E + k:b * E:16], False, False) for k in range(16)],
                 ["i32", "cst", "zw"] + zk, [ok])
 
-        def o_0(h):
-            cp(T.c0[:, lh[h]], ps[4 + h][:, 0:32], ["ps%d" % (4 + h)], ["c0%d" % h])
+        def hero(a, b):
+            o, ok = bank(HERO, a, (b - a) * 8)
+            mms([(o, T.dd[:, k, :], x, False, k == 15) for k, x in enumerate(classes(T.rho, a, b))], ["dd"] + ek("rho", a, b), [ok])
 
-        def o_p(h):
-            ts(T.par[:, lh[h]], T.c0[:, lh[h]], 1, None, A.bitwise_and, None, ["c0%d" % h], ["par%d" % h])
+        def null(a, b):
+            o, ok = bank(HERO, a, (b - a) * 8)
+            ts(T.nl[:, lst(a, b)], o, 0.0, None, A.is_gt, None, [ok], ek("nl", a, b))
 
-        def o_e(h):
-            tt(T.ef[:, lh[h]], T.par[:, lh[h]], T.v2[:, 64 * t + 32 * h:64 * t + 32 * h + 32], A.add, ["par%d" % h, "v2"], ["ef%d" % h])
+        def oa(a, b):
+            o, ok = bank(HERO, a, (b - a) * 8)
+            tt(T.oc[:, lst(a, b)], T.c0[:, lst(a, b)], o, A.max, ek("c0", a, b) + [ok], ek("oa", a, b))
 
-        def o_f(h):
-            cp(T.e16[:, lh[h]], T.ef[:, lh[h]], ["ef%d" % h], ["e16%d" % h])
+        def aoff(a, b):
+            ts(T.oc16[:, lst(a, b)], T.oc[:, lst(a, b)], float(W + P), float(P), A.min, A.add, ek("oa", a, b), ek("oa16", a, b))
 
-        def o_v():
-            ts(T.ev[:], T.c0[:], W - 2, None, A.bitwise_and, None, ["c00", "c01"], ["ev"])
+        def xf(a, b):
+            tt(T.xf[:, lst(a, b)], T.par[:, lst(a, b)], T.nl[:, lst(a, b)], A.is_equal, ek("par", a, b) + ek("nl", a, b), ek("xf", a, b))
 
-        def o_2(h):
-            ts(T.c16[:, lh[h]], ps[4 + h][:, 0:32], float(P), None, A.add, None, ["ps%d" % (4 + h)], ["c16%d" % h])
-            for q in range(h * NQ // 2, (h + 1) * NQ // 2):
-                act(T.mg[:, q * Q:(q + 1) * Q], T[tr][:].indirect(T.c16[:, q * Q // 16:(q + 1) * Q // 16]), F.Silu,
-                    [tr, tr + "l", tr + "r", "c16%d" % h], ["mg%d" % q], BM, SM)
+        def cf(a, b):
+            tt(T.oc[:, lst(a, b, 64)], T.ev[:, lst(a, b)], T.xf[:, lst(a, b)], A.add, ek("ev", a, b) + ek("xf", a, b), ek("cf", a, b))
 
-        def o_r(q):
-            c = slice(q * Q, (q + 1) * Q)
-            tt(T.rho[:, c], T.sgs[:].indirect(T.c16[:, q * Q // 16:(q + 1) * Q // 16]), T.mg[:, c], A.mult,
-               ["sgs", "sgl", "sgr", "c16%d" % (q * Q // H), "mg%d" % q], ["rho%d" % q])
+        def noff(a, b):
+            cp(T.oc16[:, lst(a, b, 64)], T.oc[:, lst(a, b, 64)], ek("cf", a, b), ek("cn16", a, b))
 
-        def o_i(q):
-            c = slice(q * Q, (q + 1) * Q)
-            ts(T.yv[:, c], T.rho[:, c], -KM, -CK, A.is_lt, A.mult, ["rho%d" % q], ["yv%d" % q])
+        def shift(a, b):
+            mms([(ps[SUM[0]][:, 0:32], T.if32[:], T.oc[:, lst(0, 4, 64)], True, True)] * (a == 0) +
+                [(ps[SUM[0]][:, 32:64], T.sh[:], T.oc[:, lst(4, 8, 64)], True, True)], ["sh", "if32"] + ek("cf", a, b), ["ps%d" % SUM[0]])
 
-        def o_j(q):
-            c = slice(q * Q, (q + 1) * Q)
-            l = slice(q * Q // 16, (q + 1) * Q // 16)
-            ek = "e16%d" % (q * Q // H)
-            tt(T.nw[:, c], T[tr][:, P:P + W].indirect(T.e16[:, l]), T.yv[:, c], A.add, [tr, ek, "yv%d" % q], ["nw%d" % q])
-            act(T[tw][:, P:P + W].indirect(T.e16[:, l]), T.nw[:, c], F.Silu, [ek, "nw%d" % q], [tw])
+        def go(a, b):
+            src, sk = (ps[SUM[0]][:, lst(a, b)], ["ps%d" % SUM[0]]) if b == 8 else (T.oc[:, lst(a, b, 64)], ek("cf", a, b))
+            cs = T["cs%d" % (st + 1)][:, lst(a, b)]
+            cp(cs, src, sk, ["cs%d%d" % (st, a)])
+            send(1, "cr%d_%d" % (st + 1, a // 4), T["cr%d" % (st + 1)][:, lst(a, b)], [cs], ["cs%d%d" % (st, a)])
 
-        def hk(nm, h):
-            return [nm + "0", nm + "1"] if h is None else ["%s%d" % (nm, h)]
+        def turn(tile, a):
+            r = 16 * st * (a // 4)
+            return tile[:, r:r + 128]
 
-        def hero(h):
-            o, ok, c0, c1, _ = part(h)
-            rk = ["rho%d" % q for q in range(c0 // Q, c1 // Q)]
-            mms([(o, T.dd[:, 128 * k:128 * k + 128], T.rho[:, c0 + k:c1:16], False, k == 15) for k in range(16)], ["dd"] + rk, [ok])
-            for x in range(c0 // H, c1 // H):
-                mms([(ps[2 + x][:], T.ir[:], T.rho[:, x * H:(x + 1) * H], True, False)], ["ir"] + rk, ["ps%d" % (2 + x)])
+        def two(a, b):
+            mms([(ps[2 + a // 4][:], turn(T.ir, a), T.rho[:, cols(a, b)], True, False)], ["ir"] + ek("rho", a, b), ["ps%d" % (2 + a // 4)])
 
-        def d_n(h):
-            o, ok, _, _, l = part(h)
-            ts(T.nl[:, l], o, 0.0, None, A.is_gt, None, [ok], hk("nl", h))
+        def nulls(a, x):
+            return [(ps[2 + a // 4][:, k:H:16], turn(T.bn[:, k, :], a), x, False, k == 15) for k in range(16)]
 
-        def d_a(h):
-            o, ok, _, _, l = part(h)
-            tt(T.oc[:, l], T.c0[:, l], o, A.max, hk("c0", h) + [ok], hk("oa", h))
+        def spread(a, b):
+            mms(nulls(a, T.nl[:, lst(a, b)]), ["bn"] + ["bn2"] * (st > 0) + ek("nl", a, b), ["ps%d" % (2 + a // 4)])
 
-        def d_16(h):
-            l = part(h)[4]
-            ts(T.oc16[:, l], T.oc[:, l], float(W + P), float(P), A.min, A.add, hk("oa", h), hk("oa16", h))
+        def alpha(a, b):
+            return T.als[:].indirect(T.oc16[:, lst(a, b)])
 
-        def d_x():
-            tt(T.xf[:], T.par[:], T.nl[:], A.is_equal, ["par0", "par1", "nl0", "nl1"], ["xf"])
+        def ak(a, b):
+            return ["als", "all", "alr", "als0"] + ek("oa16", a, b)
 
-        def d_c():
-            tt(cf, T.ev[:], T.xf[:], A.add, ["ev", "xf"], ["cf"])
-            if hop:
-                mms([(ps[7][:, 0:32], T.if32[:], T.oc[:, 64:96], True, True), (ps[7][:, 32:64], T.sh[:], T.oc[:, 96:128], True, True)],
-                    ["if32", "sh", "cf"], ["ps7"])
+        def fused(a, b):
+            tt(T.tt[:, cols(a, b)], alpha(a, b), T[prev][:, cols(a, b)], A.mult, ak(a, b) + ek(prev + "_", a, b), ek("tt", a, b))
 
-        def spread(h):
-            mms([(ps[2 + h][:, k:H:16], T.bb[:, 128 * k:128 * k + 128], T.nl[:, lh[h]], False, k == 15) for k in range(16)],
-                ["bb", "nl%d" % h], ["ps%d" % (2 + h)])
+        def plain(a, b):
+            cp(T.tt[:, cols(a, b)], alpha(a, b), ak(a, b), ek("tt", a, b))
 
-        def d_cn():
-            if hop:
-                nb = b + 1
-                cp(T["cs%d" % nb][:], ps[7][:, 0:64], ["ps7"], ["cs%d" % nb])
-                send(1, "cr%d" % nb, T["cr%d" % nb][:], [T["cs%d" % nb][:]], ["cs%d" % nb])
-            else:
-                cp(T.oc16[:, 64:128], cf, ["cf"], ["cn16"])
+        def aplain(a, b):
+            act(T.tt[:, cols(a, b)], alpha(a, b), F.Copy, ak(a, b), ek("tt", a, b))
 
-        o_2(0), o_0(0), next(rest, None)
-        if t == 0:
-            late_constants(1)
-        if not last:
-            o_p(0), o_2(1), o_e(0), o_0(1), o_f(0), o_r(0), o_p(1), o_i(0), o_e(1), o_j(0), o_f(1), o_r(1)
-        if last:
-            o_2(1), o_0(1), o_r(0), o_r(1), hero(0), o_r(2), o_r(3), hero(1)
-            rest = weights(t)
-            d_a(0), d_n(0), spread(0), d_16(0), next(rest), d_a(1), d_n(1), spread(1), d_16(1)
-            for _ in rest:
-                pass
-        elif hop:
-            o_r(2), o_r(3), hero(None), o_i(1), o_v(), o_j(1)
-            d_n(None), d_a(None), d_x(), d_16(None), d_c(), spread(1), spread(0), o_i(2), o_i(3), d_cn(), o_j(2), o_j(3)
-        else:
-            o_v(), o_i(1), o_r(2), o_j(1), o_r(3), hero(None), o_i(2), o_j(2)
-            d_n(None), d_a(None), spread(0), spread(1), o_i(3), d_x(), d_16(None), d_c(), o_j(3), d_cn()
+        def y(a, b):
+            h = a // 4
+            tt(T.yy[:, cols(a, b)], T.tt[:, cols(a, b)], ps[2 + h][:, cols(a - 4 * h, b - 4 * h)], A.mult, ek("tt", a, b) + ["ps%d" % (2 + h)], ek("yy", a, b))
 
-    for i in range(NQ):
-        c = slice(i * Q, (i + 1) * Q)
-        if i * Q < H:
-            dma("s" if i % 2 == 0 else "a", T.tl[:, c], T.fin[:, c], ["fin%d" % i], [])
-        else:
-            dma("s", T.tl[0:96, c], T.fin[32:128, c], ["fin%d" % i], [])
-            dma("a", T.tl[96:128, c], T.fin[0:32, c], ["fin%d" % i], [])
+        def nm(a, b):
+            ts(T.nm[:], T.nl[:, lst(4, 8)], -1.0, None, A.mult, None, ek("nl", 4, 8), ["nm"])
+
+        def arho(a, b):
+            tt(T.tt[:, H:K], alpha(4, 8), T.rho[:, H:K], A.mult, ak(4, 8) + ek("rho", 4, 8), ek("tt", 4, 8))
+
+        def factor(a, b):
+            mms([(ps[3][:], turn(T.irf, 4), T.tt[:, H:K], True, False)] + nulls(4, T.nm[:]), ["irf", "bn", "bn2", "nm"] + ek("tt", 4, 8), ["ps3"])
+
+        def yu(a, b):
+            tt(T.yy[:, H:K], ps[3][:], T[prev][:, H:K], A.mult, ["ps3"] + ek(prev + "_", 4, 8), ek("yy", 4, 8))
+
+        def gather(a, b):
+            act(T.ag[:, cols(a, b)], alpha(a, b), F.Copy, ak(a, b), ek("ag", a, b))
+
+        def rot(a, b):
+            o, ok = bank(ROT, a if b - a < 4 else 8, (b - a) * E)
+            mms([(o, turn(T.idw, a), T.ag[:, cols(a, b)], True, True)], ["idw"] + ek("ag", a, b), [ok])
+
+        def times(a, b):
+            o, ok = bank(ROT, a if b - a < 4 else 8, (b - a) * E)
+            tt(T.tt[:, cols(a, b)], o, T[prev][:, cols(a, b)], A.mult, [ok] + ek(prev + "_", a, b), ek("tt", a, b))
+
+        def clip(a, b):
+            ts(w[:, cols(a, b)], T.yy[:, cols(a, b)], 0.125, 4.0, A.max, A.min, ek("yy", a, b), ek("w%d_" % t, a, b))
+
+        def on(a, b):
+            c = cols(a, b)
+            send(1, "win%d_%d" % (st + 1, a // 4), T["win%d" % (st + 1)][:, c], [w[:, c]], ek("w%d_" % t, a, b))
+
+        def tally(a, b):
+            send(-1, "tin", T.tin[:], [T.win1[:], T.w2[:], T.w3[:]], ek("win1_", 0, 8) + ek("w2_", 0, 8) + ek("w3_", 0, 8))
+
+        def more(a, b):
+            dma("g", T.tin[:], T.w0[:], ["tin"] + ek("w0_", 0, 8), ["tin"], A.add)
+
+        def home(a, b):
+            c = cols(a, b)
+            send(2, "fin%d" % FIN.index(a), T.fin[:, c], [T.w4[:, c], w[:, c]], ek("w4_", a, b) + ek("w5_", a, b))
+
+        def consts(a, b):
+            late_constants(a)
+
+        def unpack(a, b):
+            unpack_uz(a)
+
+        return {"copy": copy, "u": u, "inv": inv, "bar": bar, "ways": ways, "wrap": wrap, "cfl": cfl, "sign": sign, "cell": cell, "add": add,
+                "cint": cint, "coff": coff, "m": m, "par": par, "ef": ef, "eoff": eoff, "even": even, "rho": rho, "flag": flag,
+                "old": old, "put": put, "z": z, "hero": hero, "null": null, "oa": oa, "aoff": aoff, "xf": xf, "cf": cf, "noff": noff,
+                "shift": shift, "go": go, "two": two, "spread": spread, "fused": fused, "plain": plain, "aplain": aplain, "y": y, "nm": nm, "arho": arho,
+                "factor": factor, "yu": yu, "gather": gather, "rot": rot, "times": times, "clip": clip, "on": on, "tally": tally, "more": more,
+                "home": home, "consts": consts, "unpack": unpack}
+
+    calls = [step(t) for t in range(NT)]
+    for t in range(NT):
+        for word in ORDER[t].split():
+            off = word.count("+") - word.count("-")
+            calls[t + off][word[abs(off):-2]](int(word[-2]), int(word[-1]))
+
+    for i in range(len(FIN) - 1):
+        c = cols(FIN[i], FIN[i + 1])
+        tt(T.res[:, c], T.fin[:, c], T.tin[:, c], A.add, ["fin%d" % i, "tin"], ["res%d" % i])
+        dma("s" if i % 2 == 0 else "a", T.tl[:, c], T.res[:, c], ["res%d" % i], [])
     for s in total:
         if max(waited[q].get(s, 0) for q in eng) < total[s]:
             g.wait_ge(T.sem[s], total[s])

@@ -32,26 +32,26 @@ SI, BI = _fit(-48, -1)
 BAR = {0: 0, 2: 1, 4: 4, 6: 4}
 SUM = {0: 5, 2: 7, 4: 7, 6: 5}
 HERO = {0: 6, 4: 7}
-ROT = {0: 0, 2: 1, 4: 1, 6: 0, 8: 1}
+ROT = {0: 0, 2: 1, 4: 5, 6: 0, 8: 1}
+TAL = {0: 4, 4: 1}
 FIN = [0, 2, 4, 6, 8]
-WHOLE = False
 ORDER = [
-    "copy00 u04 u48 inv04 bar04 inv48 bar48 consts00 sign04 sign48 wrap00 wrap11 +u04 cell04 cell48 +u48 ways04 ways48 consts10 add04 add48 z08 coff04 cint04 m02 m24 consts20 par04 rho02 ef04 coff48 cint48 m46 m68 flag02 eoff04 par48 rho24 old02 ef48 put02 flag24 rho46 eoff48 old24 put24 flag46 rho68 two04 hero08 two48 old46 put46 flag68 old68 put68 null08 even08 oa08 xf08 aoff08 cf08 spread48 +z04 +cell48 +cell04 spread04 noff08 +copy00 unpack10",
-    "inv04 bar04 inv48 bar48 -plain04 -plain48 -y04 -y48 -clip04 sign04 sign48 wrap11 wrap00 ways04 add04 ways48 add48 consts30 coff04 cint04 m02 m24 -clip48 par04 coff48 cint48 z48 m46 m68 ef04 rho02 par48 rho24 hero04 rho46 flag02 eoff04 rho68 hero48 two04 ef48 flag24 null04 old02 put02 xf04 even08 old24 put24 null48 cf04 oa04 eoff48 flag46 xf48 go04 oa48 flag68 cf48 spread04 two48 shift48 +u48 +u04 spread48 +z08 old46 put46 old68 put68 go48 aoff08 +copy00 unpack20 gather48",
-    "inv04 -rot48 bar04 inv48 bar48 -fused04 -y04 -clip04 -on04 cfl04 cfl48 -times48 sign04 sign48 wrap11 wrap00 cell48 +u04 cell04 -y48 ways04 ways48 add04 add48 coff04 m02 m24 cint04 -clip48 -on48 -tally00 par04 rho02 cint48 ef04 coff48 m46 m68 flag02 eoff04 par48 rho24 old02 ef48 put02 flag24 rho46 old24 put24 flag46 eoff48 rho68 two04 hero08 old46 put46 flag68 even08 old68 put68 null08 oa08 xf08 two48 spread04 spread48 +u48 aoff08 cf08 noff08 +copy00 gather48",
-    "inv04 cell48 -rot48 bar04 cell04 inv48 bar48 -fused04 -y04 -clip04 sign04 sign48 wrap00 wrap11 ways04 add04 ways48 add48 z04 -times48 coff04 cint04 m02 m24 -y48 par04 cint48 coff48 -clip48 z48 m46 m68 rho02 ef04 rho24 +u04 hero04 par48 rho46 eoff04 flag02 rho68 flag24 hero48 null04 old02 put02 ef48 xf04 even08 old24 put24 null48 cf04 oa04 flag46 xf48 eoff48 go04 flag68 cf48 two48 two04 spread04 +u48 shift48 spread48 +z08 old46 put46 old68 oa48 go48 put68 aoff08 +copy00 gather48",
-    "inv04 -rot48 bar04 inv48 bar48 -fused04 -y04 cfl04 -clip04 cfl48 -on04 sign04 wrap00 wrap11 sign48 cell04 +u04 cell48 -times48 -y48 ways04 ways48 add04 +u48 add48 coff04 m02 m24 cint04 -clip48 -on48 -tally00 par04 rho02 coff48 ef04 cint48 m46 m68 flag02 eoff04 par48 rho24 old02 put02 ef48 flag24 rho46 eoff48 old24 put24 flag46 rho68 two04 hero08 old46 put46 flag68 old68 put68 null08 even08 spread04 two48 oa08 xf08 aoff08 cf08 noff08",
-    "inv04 cell48 -spread48 z04 cell04 bar04 inv48 bar48 -fused04 -y04 sign04 -gather48 sign48 wrap00 wrap11 -rot48 -clip04 ways04 add04 ways48 add48 coff04 -times48 m02 m24 cint04 -y48 coff48 cint48 z48 m68 m46 rho02 rho24 hero04 two04 rho68 rho46 -clip48 oa04 hero48 null04 aoff04 spread04 two48 oa48 fused02 aoff48 null48 spread48 gather46 rot46 gather68 rot68 y02 fused24 clip02 y24 home02 times46 clip24 home24 y46 times68 clip46 y68 home46 clip68 home68",
+    'vm00 vt00 mk00 vb00 idw00 irf00 ick00 iff00 pfa00 pfb00 wt00 ta00 blk00 dm00 diffs10 diffs00 feats00 ir00 table10 feats10 feats20 feats30 diffs20 diffs30 state00 state10 state20 vz00 first00 bb02 minus00 ub00 state31 bb68 firstf00 bb46 bb24 zw00 cst00 table21 cwz00 table31 cw00 copy00 table00 inv04 inv48 u48 u04 cell04 bar04 bar48 sign04 sign48 wrap00 wrap11 ways04 ways48 z08 +u04 cell48 add04 add48 coff04 cint04 vtwo01 m02 m24 par04 ef04 coff48 m46 m68 rho02 cint48 eoff04 flag02 rho24 old02 par48 flag24 rho46 put02 old24 ef48 rho68 eoff48 flag46 flag68 old46 put24 hero08 two48 two04 even08 null08 old68 oa08 xf08 sh00 aoff08 cf08 vtwo15 noff08 put46 plain48 plain04 put68 +copy00 unpack10',
+    'inv04 z04 cell48 cell04 u48 -spread48 -spread04 bar04 inv48 bar48 -y48 -y04 -clip48 sign04 wrap00 sign48 wrap11 ways04 add04 ways48 add48 coff04 cint04 m02 m24 -clip04 par04 cint48 coff48 rho02 ef04 m46 m68 rho24 eoff04 flag02 rho46 old02 rho68 z48 hero04 two04 hero48 put02 null04 flag24 par48 even08 xf04 old24 ef48 null48 put24 cf04 flag46 xf48 eoff48 flag68 go04 cf48 old46 put46 old68 two48 spread04 spread48 shift48 +u04 put68 go48 oa04 oa48 aoff08 +copy00 unpack20',
+    'inv04 inv48 bar04 u48 bar48 -fused04 -fused48 -y04 -y48 cfl04 -clip04 cfl48 -clip48 -on04 -on48 more10 sign04 sign48 wrap11 wrap00 ways04 ways48 cell04 cell48 z08 +u04 add04 add48 coff04 m02 m24 cint04 par04 ef04 cint48 rho02 coff48 eoff04 m46 m68 flag02 rho24 old02 put02 par48 flag24 rho46 ef48 old24 put24 eoff48 flag46 rho68 hero08 two04 old46 even08 flag68 put46 null08 old68 xf08 oa08 put68 cf08 aoff08 noff08 +copy00',
+    'inv04 -spread04 cell48 cell04 inv48 -fused04 -arho48 -y04 -nm48 -clip04 z04 u48 bar04 bar48 -factor48 sign04 sign48 wrap00 wrap11 ways04 ways48 add04 add48 -yu48 coff04 cint04 m02 m24 -clip48 -tally00 cint48 par04 coff48 rho02 ef04 rho24 eoff04 flag02 m68 m46 rho68 old02 rho46 hero04 z48 hero48 put02 flag24 null04 par48 even08 old24 xf04 ef48 null48 cf04 eoff48 xf48 go04 flag46 put24 cf48 oa04 old46 oa48 two04 shift48 spread04 +z08 +u48 put46 go48 flag68 aoff08 nm48 old68 arho48 put68 +copy00',
+    'inv04 inv48 -fused04 u04 -factor48 bar04 bar48 sign04 wrap00 sign48 wrap11 -y04 cfl04 -clip04 -yu48 cfl48 -clip48 ways04 ways48 cell48 cell04 add04 add48 cint04 coff04 m02 m24 par04 -on04 -on48 -tally00 more20 ef04 coff48 cint48 rho02 par48 eoff04 flag02 m68 m46 rho24 old02 put02 ef48 flag24 rho46 old24 rho68 flag46 eoff48 put24 +u04 two04 hero08 flag68 old46 put46 old68 null08 oa08 even08 xf08 put68 aoff08 nm48 cf08 arho48 noff08',
+    'inv04 inv48 u48 -spread04 z04 cell04 cell48 -factor48 -fused04 -y04 bar04 bar48 -yu48 -clip04 sign04 wrap11 sign48 wrap00 -clip48 four04 four48 more30 ways04 add04 ways48 add48 coff04 coff48 cint48 m02 m24 rho02 rho24 m68 m46 z48 hero04 rho68 rho46 cint04 oa04 null04 aoff04 hero48 two04 oa48 fused02 aoff48 null48 gather46 gather68 spread04 two48 spread48 rot46 rot68 early04 late04 early48 late48 y02 fused24 y24 times46 home02 home24 y46 times68 y68 home46 home68',
 ]
 ORDER = [
-'copy00 inv04 u48 u04 bar04 inv48 bar48 consts10 consts00 sign04 wrap00 sign48 wrap11 cell48 cell04 ways04 ways48 add04 +u04 +u48 z08 add48 cint04 coff04 m02 m24 consts20 par04 rho02 ef04 coff48 cint48 m46 m68 flag02 eoff04 par48 rho24 old02 put02 ef48 flag24 rho46 old24 put24 rho68 hero08 eoff48 flag46 even08 flag68 old46 old68 put48 null08 oa08 xf08 aoff08 cf08 plain04 consts30 noff08 +copy00 unpack10',
-'inv04 -two04 cell48 -two48 cell04 -spread48 -spread04 bar04 inv48 bar48 -plain48 -y48 -y04 -clip48 -clip04 sign04 sign48 wrap11 wrap00 ways04 add04 ways48 add48 coff04 cint04 m02 m24 par04 ef04 coff48 cint48 m46 m68 rho02 par48 rho24 z48 z04 hero04 flag02 eoff04 rho46 old02 rho68 two04 hero48 null04 flag24 put02 flag46 ef48 even08 xf04 old24 oa04 eoff48 put24 cf04 null48 flag68 old46 go04 xf48 old68 oa48 cf48 two48 spread04 spread48 shift48 +z08 put48 aoff08 go48 +copy00 unpack20 gather48',
-'inv04 u48 -rot48 u04 bar04 inv48 bar48 -fused04 -y04 -clip04 -on04 cfl48 sign04 wrap00 wrap11 sign48 cfl04 -times48 -y48 ways04 ways48 cell04 add04 +u04 cell48 add48 coff04 m02 m24 cint04 -clip48 par04 -on48 -tally00 rho02 coff48 ef04 cint48 m46 m68 flag02 eoff04 rho24 old02 put02 par48 flag24 rho46 ef48 old24 put24 eoff48 rho68 +u48 two04 two48 hero08 flag46 even08 flag68 old46 old68 put48 oa08 null08 xf08 cf08 aoff08 fused04 noff08 +copy00 gather48',
-'inv04 z04 -spread04 cell04 -spread48 -rot48 bar04 inv48 cell48 bar48 -y04 -clip04 -times48 sign04 sign48 wrap00 wrap11 -y48 ways04 add04 ways48 add48 coff04 cint04 m02 m24 -clip48 par04 coff48 cint48 ef04 rho02 eoff04 rho24 m68 m46 flag02 rho68 old02 rho46 +u48 z48 hero04 two04 +u04 hero48 null04 flag24 put02 oa04 even08 par48 xf04 old24 cf04 ef48 null48 oa48 put24 flag46 eoff48 xf48 go04 aoff08 flag68 cf48 spread04 two48 spread48 shift48 old46 old68 go48 gather48 put48 +copy00',
-'inv04 z08 -rot48 bar04 inv48 bar48 -fused04 -y04 cfl04 -clip04 -times48 -on04 sign04 wrap00 sign48 wrap11 cfl48 -y48 ways04 ways48 cell04 cell48 +u04 add04 add48 coff04 m02 m24 cint04 -clip48 par04 -on48 -tally00 cint48 rho02 ef04 coff48 m46 m68 flag02 eoff04 rho24 old02 put02 flag24 par48 rho46 old24 ef48 rho68 flag46 eoff48 put24 two48 two04 hero08 flag68 old46 old68 put48 even08 null08 xf08 cf08 noff08 oa08 aoff08 fused04',
-'inv04 cell04 u48 cell48 -spread04 bar04 z04 inv48 bar48 -spread48 -y04 sign04 -gather48 sign48 wrap00 wrap11 -rot48 ways04 -clip04 add04 ways48 add48 coff04 -times48 m02 m24 cint04 -y48 coff48 cint48 z48 m68 m46 rho02 rho24 hero04 rho68 rho46 two04 hero48 oa04 null04 -clip48 aoff04 spread04 two48 oa48 fused02 aoff48 null48 gather46 spread48 rot46 gather68 rot68 y02 fused24 clip02 y24 home02 times46 clip24 home24 y46 times68 clip46 y68 home46 clip68 home68',
+'vt00 vm00 idw00 ick00 mk00 vb00 pfa00 pfb00 wt00 ta00 blk00 dm00 diffs00 table00 diffs10 table10 feats00 state00 feats10 state10 feats20 state20 feats30 state30 diffs20 diffs30 vz00 first00 ub00 bb08 table21 table31 copy00 inv04 inv48 u48 u04 bar04 bar48 iff00 cwz00 firstf00 cw00 sign04 sign48 wrap11 wrap00 ir00 irf00 ways04 ways48 vtwo01 zw00 cst00 cell04 cell48 +u04 add04 add48 z08 coff04 cint04 m02 m24 minus00 par04 ef04 coff48 eoff04 rho02 m46 m68 rho24 flag02 flag24 old02 cint48 rho46 par48 old24 put02 flag46 ef48 rho68 eoff48 even08 flag68 old46 put24 +u48 two04 hero08 put46 oa08 null08 old68 xf08 aoff08 cf08 noff08 plain48 plain04 sh00 vtwo15 put68 +copy00 unpack10',
+'inv04 -two48 z04 cell48 cell04 -spread48 -spread04 bar04 inv48 bar48 -y48 -y04 -clip48 sign04 wrap00 sign48 wrap11 ways04 add04 ways48 add48 coff04 cint04 m02 m24 -clip04 par04 cint48 coff48 rho02 ef04 m46 m68 rho24 flag02 eoff04 rho46 old02 rho68 flag24 z48 two04 hero04 hero48 put02 even08 null04 par48 old24 xf04 ef48 null48 flag46 put24 cf04 eoff48 xf48 flag68 go04 cf48 old46 put46 old68 two48 spread04 shift48 put68 go48 oa04 oa48 aoff08 +copy00 unpack20',
+'inv04 inv48 u48 u04 -spread48 z08 bar04 bar48 -fused04 -fused48 -y04 cfl04 -y48 cfl48 -clip04 -clip48 -on04 -on48 more10 sign04 wrap00 sign48 wrap11 ways04 ways48 cell04 cell48 +u04 add04 add48 coff04 m02 m24 cint04 par04 ef04 cint48 rho02 coff48 eoff04 m68 m46 flag02 rho24 old02 put02 par48 flag24 rho46 ef48 old24 put24 rho68 eoff48 flag46 +u48 two04 hero08 flag68 old46 put46 even08 null08 old68 xf08 oa08 cf08 aoff08 nm48 put68 noff08 +copy00',
+'inv04 -spread04 cell04 cell48 z04 bar04 inv48 -fused04 -arho48 -y04 -clip04 bar48 -factor48 sign04 sign48 wrap00 wrap11 ways04 ways48 add04 add48 -yu48 coff04 cint04 m02 m24 -clip48 -tally00 coff48 par04 cint48 rho02 ef04 rho24 flag02 eoff04 m68 m46 rho68 old02 rho46 +u48 +u04 z48 two04 hero04 hero48 put02 flag24 null04 par48 even08 old24 ef48 xf04 null48 flag46 cf04 xf48 eoff48 go04 cf48 put24 old46 oa04 oa48 spread04 shift48 +z08 put46 go48 flag68 nm48 aoff08 old68 arho48 put68 +copy00',
+'inv04 inv48 -fused04 -factor48 bar04 bar48 sign04 wrap11 sign48 wrap00 cfl04 -y04 cfl48 -yu48 -clip04 ways04 ways48 cell04 +u04 cell48 add04 add48 +u48 cint04 coff04 m02 m24 -clip48 par04 -on04 -on48 -tally00 more20 cint48 coff48 ef04 rho02 par48 eoff04 m68 m46 flag02 rho24 old02 put02 ef48 flag24 rho46 old24 eoff48 rho68 flag46 put24 two04 hero08 flag68 old46 put46 old68 null08 oa08 even08 xf08 put68 aoff08 nm48 cf08 arho48 noff08',
+'inv04 inv48 -spread04 z04 -fused04 -y04 -factor48 bar04 cell48 cell04 bar48 -yu48 -clip04 sign04 wrap11 sign48 wrap00 -clip48 four04 four48 more30 ways04 add04 ways48 add48 coff04 coff48 cint48 m02 m24 rho02 rho24 m68 m46 z48 hero04 rho68 rho46 cint04 null04 oa04 aoff04 two04 hero48 oa48 fused02 aoff48 null48 gather46 gather68 two48 spread04 spread48 rot46 rot68 early04 late04 early48 late48 y02 fused24 y24 times46 home02 home24 y46 times68 y68 home46 home68',
 ]
-ORDER = ['copy00 inv04 inv48 wrap11 u04 u48 bar04 bar48 consts00 consts10 sign04 wrap00 sign48 ways04 ways48 cell48 z08 +u48 cell04 add04 +u04 add48 coff04 m02 m24 cint04 par04 ef04 consts20 eoff04 rho02 cint48 coff48 m46 m68 flag02 rho24 old02 put02 flag24 par48 rho46 ef48 old24 rho68 flag46 eoff48 even08 put24 two04 hero08 flag68 old46 put46 null08 oa08 old68 consts40 xf08 consts30 aoff08 cf08 plain48 noff08 put68 +copy00 unpack10', 'inv04 -two48 z04 cell48 cell04 -spread48 -spread04 bar04 inv48 bar48 -plain04 -y48 -y04 -clip48 -clip04 sign04 wrap11 sign48 wrap00 ways04 add04 ways48 add48 coff04 cint04 m02 m24 par04 ef04 coff48 cint48 m46 m68 rho02 eoff04 rho24 flag02 rho46 old02 rho68 par48 z48 two04 hero04 hero48 two48 flag24 put02 even08 ef48 null04 old24 xf04 null48 flag46 eoff48 put24 cf04 xf48 flag68 go04 cf48 old46 put46 old68 spread04 shift48 put68 go48 oa04 oa48 aoff08 +copy00 unpack20', 'inv04 inv48 -spread48 u48 u04 bar04 bar48 -fused04 -fused48 -y04 cfl04 -y48 -clip04 cfl48 -clip48 -on04 -on48 sign04 wrap11 sign48 wrap00 ways04 ways48 cell04 +u04 cell48 z08 add04 add48 coff04 m02 m24 cint04 par04 ef04 cint48 rho02 eoff04 coff48 m46 m68 flag02 rho24 old02 put02 par48 flag24 rho46 ef48 old24 put24 flag46 eoff48 rho68 two04 +u48 hero08 even08 old46 put46 flag68 oa08 null08 old68 xf08 aoff08 nm48 cf08 put68 noff08 +copy00', 'inv04 -spread04 cell48 cell04 z04 bar04 inv48 -fused04 -arho48 -y04 -clip04 bar48 -factor48 sign04 sign48 wrap00 wrap11 ways04 ways48 +u04 add04 +u48 add48 -yu48 coff04 cint04 m02 m24 -clip48 par04 cint48 coff48 rho02 ef04 rho24 m68 m46 eoff04 flag02 rho68 old02 rho46 z48 two04 hero04 hero48 put02 null04 flag24 par48 even08 xf04 old24 ef48 null48 cf04 flag46 put24 xf48 go04 eoff48 cf48 oa04 old46 oa48 spread04 shift48 put46 go48 flag68 nm48 aoff08 old68 put68 +copy00', 'inv04 inv48 -arho48 -fused04 cfl04 -y04 z08 -factor48 cell04 bar04 bar48 sign04 wrap00 sign48 wrap11 -yu48 -clip04 cfl48 -clip48 ways04 ways48 cell48 add04 +u48 add48 coff04 m02 m24 cint04 par04 -on48 -on04 -tally00 ef04 cint48 rho02 coff48 eoff04 m46 m68 flag02 rho24 old02 put02 par48 flag24 rho46 ef48 old24 flag46 eoff48 rho68 put24 two04 hero08 old46 put46 flag68 null08 even08 old68 oa08 xf08 cf08 put68 noff08 aoff08 fused04', 'inv04 -two48 u04 -spread04 z04 -spread48 inv48 cell04 cell48 bar04 bar48 -y04 sign04 wrap00 sign48 -gather48 more00 wrap11 -clip04 ways04 add04 -rot48 ways48 add48 coff04 m02 m24 cint04 -times48 coff48 rho02 rho24 m68 m46 hero04 cint48 rho68 rho46 oa04 -y48 null04 aoff04 -clip48 z48 hero48 two04 oa48 fused02 aoff48 null48 gather46 two48 spread04 spread48 rot46 gather68 rot68 y02 fused24 clip02 y24 home02 times46 clip24 home24 y46 times68 clip46 y68 home46 clip68 home68']
+ORDER = ['vm00 vt00 mk00 idw00 ick00 pfa00 pfb00 vb00 ta00 wt00 dm00 diffs00 table00 diffs10 table10 cst00 feats00 state00 feats10 state10 feats20 state20 feats30 vz00 blk00 state30 ub00 first00 bb08 copy00 iff00 inv04 inv48 u04 diffs30 u48 diffs20 bar04 bar48 sign04 firstf00 cwz00 zw00 table21 cw00 table31 sh00 vtwo01 sign48 wrap11 irf00 ways04 ways48 cell04 cell48 +u04 add04 +u48 add48 coff04 ir00 wrap00 m02 m24 cint04 minus00 par04 ef04 coff48 rho02 eoff04 m68 m46 rho24 flag02 flag24 old02 cint48 rho46 par48 old24 put02 ef48 rho68 eoff48 flag46 flag68 old46 even08 put24 two04 z08 hero08 put46 null08 oa08 old68 xf08 vtwo15 cf08 aoff08 noff08 plain48 plain04 put68 +copy00 unpack10', 'inv04 -two48 z04 -spread04 cell48 cell04 -spread48 inv48 bar04 bar48 -y48 -y04 -clip48 sign04 sign48 wrap00 wrap11 ways04 add04 ways48 add48 coff04 cint04 m02 m24 -clip04 par04 coff48 cint48 rho02 ef04 m46 m68 rho24 flag02 eoff04 rho46 old02 rho68 flag24 z48 hero04 two04 hero48 put02 null04 even08 par48 old24 ef48 xf04 null48 flag46 put24 eoff48 cf04 xf48 flag68 go04 cf48 old46 put46 old68 two48 spread04 spread48 shift48 +u04 +u48 put68 go48 oa04 oa48 aoff08 +copy00 unpack20', 'inv04 inv48 z08 bar04 bar48 -fused04 -fused48 -y04 cfl04 -y48 cfl48 -clip04 -clip48 -on04 -on48 more10 sign04 sign48 wrap11 wrap00 ways04 ways48 cell04 cell48 +u04 add04 +u48 add48 coff04 m02 m24 cint04 par04 ef04 cint48 rho02 coff48 eoff04 m68 m46 flag02 rho24 old02 put02 flag24 par48 rho46 old24 ef48 put24 rho68 eoff48 flag46 two04 hero08 flag68 old46 put46 null08 oa08 even08 old68 xf08 aoff08 cf08 put68 noff08 +copy00', 'inv04 -spread04 z04 cell48 cell04 bar04 inv48 -fused04 -nm48 -y04 -arho48 -clip04 bar48 -factor48 sign04 sign48 wrap00 wrap11 ways04 ways48 add04 +u04 add48 -yu48 coff04 cint04 m02 m24 -clip48 -tally00 coff48 cint48 par04 rho02 ef04 rho24 flag02 eoff04 m68 m46 rho68 old02 rho46 z48 +u48 two04 hero04 hero48 put02 flag24 null04 even08 par48 old24 xf04 ef48 null48 flag46 cf04 xf48 eoff48 go04 cf48 put24 oa04 old46 spread04 shift48 put46 oa48 go48 flag68 aoff08 nm48 old68 arho48 put68 +copy00', 'inv04 inv48 -fused04 z08 -factor48 bar04 bar48 sign04 sign48 wrap11 wrap00 cfl04 -y04 cfl48 -clip04 -yu48 ways04 ways48 cell04 cell48 +u04 add04 +u48 add48 coff04 cint04 m02 m24 -clip48 par04 -on04 -on48 -tally00 more20 coff48 cint48 ef04 rho02 eoff04 par48 m46 m68 flag02 rho24 old02 put02 flag24 rho46 ef48 old24 eoff48 rho68 flag46 put24 two04 hero08 flag68 old46 put46 old68 null08 oa08 even08 xf08 put68 aoff08 nm48 cf08 arho48 noff08', 'inv04 inv48 z04 cell48 cell04 -spread04 -fused04 -y04 -factor48 bar04 bar48 -yu48 -clip04 sign04 sign48 wrap11 wrap00 -clip48 four04 four48 more30 ways04 add04 ways48 add48 coff04 coff48 cint48 m02 m24 rho02 rho24 m68 m46 z48 hero04 rho68 rho46 cint04 oa04 null04 aoff04 two04 hero48 oa48 fused02 aoff48 null48 gather46 gather68 two48 spread04 spread48 rot46 early04 rot68 late04 early48 late48 y02 fused24 y24 times46 home02 home24 y46 times68 y68 home46 home68']
 
 SCRATCH = {
     "sgs": ("sbuf", [128, WP], "bfloat16"), "als": ("sbuf", [128, WP + 16], "bfloat16"),
@@ -63,7 +63,7 @@ SCRATCH = {
     "uz": ("sbuf", [8, 12, K], "bfloat16"), "raw": ("sbuf", [8, 8, K], "bfloat16"),
     "stg": ("sbuf", [128, 512], "bfloat16"),
     "l1": ("dram", [128, 256], "bfloat16"), "l2": ("dram", [128, 256], "bfloat16"),
-    "pi": ("sbuf", [128, 4], "int32"), "pf": ("sbuf", [128, 12], "float32"),
+    "pf": ("sbuf", [128, 4], "float32"),
     "vw": ("sbuf", [128, RW], "int32"), "vt": ("sbuf", [128, RW], "int32"),
     "vb": ("sbuf", [128, 128], "int32"), "vi": ("sbuf", [128, 128], "int32"), "vm": ("sbuf", [128, 16], "int32"),
     "vz": ("sbuf", [8, 144], "int32"), "vz2": ("sbuf", [8, 128], "int32"),
@@ -81,22 +81,21 @@ SCRATCH = {
     "oc": ("sbuf", [128, 128], "float32"), "oc16": ("sbuf", [128, 128], "uint16"),
     "c0": ("sbuf", [128, 64], "int32"), "c16": ("sbuf", [128, 64], "uint16"),
     "par": ("sbuf", [128, 64], "int32"), "ef": ("sbuf", [128, 64], "float32"), "e16": ("sbuf", [128, 64], "uint16"),
-    "ev": ("sbuf", [128, 64], "int32"), "nl": ("sbuf", [128, 64], "bfloat16"), "nm": ("sbuf", [128, 32], "bfloat16"),
+    "ev": ("sbuf", [128, 64], "int32"), "nl": ("sbuf", [128, 64], "bfloat16"), "nm": ("sbuf", [128, 64], "bfloat16"),
     "xf": ("sbuf", [128, 64], "float32"),
-    "fin": ("sbuf", [128, K], "float32"), "tin": ("sbuf", [128, K], "float32"), "res": ("sbuf", [128, K], "float32"),
 }
+for _n in ["fin", "tin2", "tin3", "res", "w4in", "win1", "win2"] + ["w%d" % _t for _t in range(NT)]:
+    SCRATCH[_n] = ("sbuf", [128, K], "float32")
 for _b in (1, 2):
     SCRATCH["cs%d" % _b] = ("sbuf", [128, 64], "uint16")
     SCRATCH["cr%d" % _b] = ("sbuf", [128, 64], "uint16")
-    SCRATCH["win%d" % _b] = ("sbuf", [128, K], "float32")
-for _t in range(NT):
-    SCRATCH["w%d" % _t] = ("sbuf", [128, K], "float32")
 for _b in range(8):
     SCRATCH["ps%d" % _b] = ("psum", [128, 512], "float32")
 
-ARR = ["l1", "l2", "tin"] + ["%s%d_%d" % (_n, _b, _h) for _n in ("cr", "win") for _b in (1, 2) for _h in (0, 1) if not (WHOLE and _n == "cr" and _h)] \
-    + ["fin%d" % i for i in range(len(FIN) - 1)]
-SEMAPHORES = ["qv", "qa", "qp", "qg", "ls"] + ["r_" + n for n in ARR] + ["d%d" % i for i in range(64)]
+ARR = {"l1": 1, "l2": 2, "tin2": -1, "tin3": -1, "w4in_0": 2, "w4in_1": 2}
+ARR.update({"%s%d_%d" % (_n, _b, _h): 1 for _n in ("cr", "win") for _b in (1, 2) for _h in (0, 1)})
+ARR.update({"fin%d" % _i: 2 for _i in range(len(FIN) - 1)})
+SEMAPHORES = ["qv", "qa", "qp", "qg", "ls"] + ["r_" + _n for _n in ARR] + ["d%d" % _i for _i in range(64)]
 
 
 def rank_program(g, core, T, topo):
@@ -158,29 +157,24 @@ def rank_program(g, core, T, topo):
             return ins
         op("p", fn, reads, writes)
 
-    def send(hop, name, out, srcs, reads):
-        dst = T.cores[(rank + hop) % n]
+    def lanes(src, dst):
+        far = [c for c in T.cores if topo.chip(c) != topo.chip(src)][0]
+        return [e for e in topo.engines(src, dst) if topo.chip(dst) != topo.chip(src) or e not in topo.engines(src, far)]
+
+    def send(name, out, src, reads):
+        dst = T.cores[(rank + ARR[name]) % n]
         rid, pid, _ = topo.addr(dst)
-        m = topo.mask(core, dst)
         order("g", reads, [])
-        if len(srcs) == 1:
-            g.remote_dma(out, srcs[0], T.sem["r_" + name], T.sem.ls, pid, rid, m)
-        else:
-            g.remote_dma_fused([RemoteDMATransfer(dst_ids=[DstId(rid=rid, pnc=pid)], dma_engine_mask=m,
-                                                  remote_sem=T.sem["r_" + name], srcs=srcs, dsts=[out], alu_op=1)],
-                               local_sem=T.sem.ls)
-        cnt["ls"] += len(topo.engines(core, dst))
+        g.remote_dma(out, src, T.sem["r_" + name], T.sem.ls, pid, rid, sum(1 << e for e in lanes(core, dst)))
+        cnt["ls"] += len(lanes(core, dst))
         total["ls"] = cnt["ls"]
 
     def ek(nm, a, b):
         return ["%s%d" % (nm, x) for x in range(a, b)]
 
-    def arrives(hop, name):
-        src = T.cores[(rank - hop) % n]
+    for name in ARR:
         keys = ek(name[:-1], 4 * int(name[-1]), 4 * int(name[-1]) + 4) if "_" in name else [name]
-        if WHOLE and name.startswith("cr"):
-            keys = ek(name[:-1], 0, 8)
-        note(("r_" + name, len(topo.engines(src, core)), None), [], keys)
+        note(("r_" + name, len(lanes(T.cores[(rank - ARR[name]) % n], core)), None), [], keys)
 
     V, S = g.vector, g.scalar
 
@@ -206,8 +200,6 @@ def rank_program(g, core, T, topo):
             op("a", lambda: S.activation(out, in_, f, bias=bias, scale=scale), reads, writes)
 
     ps = [T["ps%d" % b] for b in range(8)]
-    for nm in ARR:
-        arrives(2 if nm == "l2" or nm.startswith("fin") else -1 if nm == "tin" else 1, nm)
 
     def wrapped(nm, src):
         dma("s", T[nm + "s"][:, P:P + W], src[:], [], [nm + "s"])
@@ -215,9 +207,9 @@ def rank_program(g, core, T, topo):
         dma("s", T[nm + "s"][:, P + W:WP], src[:, 0:P], [], [nm + "r"])
 
     dma("s", T.mjs[:, 0:K], T.mj[:, 0:K], [], ["mjs0"])
-    dma("a", T.mjs[:, K:W], T.mj[:, K:W], [], ["mjs1"])
-    dma("s", T.ces[:], T.ce[:], [], ["ces"])
     dma("a", T.nxs[:, 0:K], T.nx[:, 0:K], [], ["nxs0"])
+    dma("s", T.mjs[:, K:W], T.mj[:, K:W], [], ["mjs1"])
+    dma("a", T.ces[:], T.ce[:], [], ["ces"])
     dma("s", T.nxs[:, K:W], T.nx[:, K:W], [], ["nxs1"])
     dma("a", T.uz[:, 0:2, :], T.uu[:, 0:2 * K], [], ["u0"])
     wrapped("sg", T.sg)
@@ -229,16 +221,16 @@ def rank_program(g, core, T, topo):
             c = (b - 1) * 256 + x * 128
             dma("s", T.stg[:, c:c + 128], src[:, 2 * b * K:2 * (b + 1) * K], [], ["stg%d%d" % (b, x)])
 
-    pf = [T.pf[:, i:i + 1] for i in range(12)]
+    pf = [T.pf[:, i:i + 1] for i in range(2)]
     vq = T.vw[:, 0:128]
     eq = T.idw[:, 0:128]
     op("g", lambda: g.iota(T.vw[:], [[1, RW]], 0, -1), [], ["vw"])
     op("g", lambda: g.iota(T.vb[:], [[-16, 8], [0, 16]], 0, 1), [], ["vb"])
     op("g", lambda: g.iota(T.vi[:], [[0, 8], [1, 16]], 0, 0), [], ["vi"])
     op("g", lambda: g.iota(T.vz[:], [[1, 144]], 0, -16), [], ["vz"])
-    op("g", lambda: g.iota(T.pi[:, 0:1], [[0, 1]], 0, 1), [], ["pi0"])
-    op("g", lambda: g.iota(T.dd[:], [[0, W]], 0, 0, allow_small_or_imprecise_dtypes=True), [], ["dd"])
-    op("g", lambda: g.affine_select(T.dd[:], T.dd[:], [[-256, 16], [-16, 8], [255, 16]], A.not_equal, (2.0 ** 20) / KM, 0, 1), ["dd"], ["dd"])
+    fill(T.dd[:, 0:10, :], 0.0, ["dz"])
+    op("g", lambda: g.iota(T.dd[:, 10:16, :], [[0, 768]], 0, 0, allow_small_or_imprecise_dtypes=True), [], ["dd"])
+    op("g", lambda: g.affine_select(T.dd[:], T.dd[:], [[-256, 16], [-16, 8], [255, 16]], A.not_equal, (2.0 ** 20) / KM, 0, 1), ["dd", "dz"], ["dd"])
 
     def make_bn(c0, ng, key):
         v = T.bn[:, :, c0:c0 + 16 * ng]
@@ -246,61 +238,40 @@ def rank_program(g, core, T, topo):
         op("g", lambda: g.affine_select(v, v, [[-1, 16], [-16, ng], [0, 16]], A.is_equal, 0.0, 0, 1), [key], [key])
 
     make_bn(0, 8, "bn")
-    ts(T.vt[:], T.vw[:], 127, None, A.bitwise_and, None, ["vw"], ["vt"])
-    ts(T.vm[:], T.vw[:, 0:16], 15, None, A.bitwise_and, None, ["vw"], ["vm"])
-    ts(T.vb[:], T.vb[:], 4, None, A.arith_shift_right, None, ["vb"], ["vb"])
-    ts(T.idw[:], T.vt[:], 0.0, None, A.is_equal, None, ["vt"], ["idw"])
-    act(T.i32[:], eq, F.Silu, ["idw"], ["i32"], 0.0, CK)
-    ts(T.mk[:], T.vm[:], 0.0, None, A.is_equal, None, ["vm"], ["mk"])
-    ts(T.wt[:], T.vb[:], 0.0, 1.0 / KI, A.is_equal, A.mult, ["vb"], ["wt"])
-    ts(pf[0], T.mk[:, 15:16], -16.0, 1.0, A.mult, A.add, ["mk"], ["pf0"])
-    ts(pf[1], T.mk[:, 15:16], 2.0, -1.0, A.mult, A.add, ["mk"], ["pf1"])
-    tt(T.blk[:], T.wt[:], T.vi[:], A.mult, ["wt", "vi"], ["blk"])
-    ts(T.ta[:], vq, pf[0], pf[1], A.is_equal, A.mult, ["vw", "pf0", "pf1"], ["ta"])
-    ts(T.vz2[:], T.vz[:, 0:128], 4, None, A.arith_shift_right, None, ["vz"], ["vz2"])
-    tt(T.dm[:], T.ta[:], eq, A.add, ["ta", "idw"], ["dm"])
-    ts(T.ub[:], T.vz2[:], 0.0, None, A.is_equal, None, ["vz2"], ["ub"])
-    ts(T.pi[:, 1:2], T.pi[:, 0:1], 15, None, A.bitwise_and, None, ["pi0"], ["pi1"])
-
-    blocks = [slice(b * 512, (b + 1) * 512) for b in range(4)]
-    for b in range(4):
-        c, mk = blocks[b], "mjs%d" % (b // 2)
-        ts(T.f1[:, c], T.mjs[:, c], 1.0 / 6, 12.0, A.min, A.mult, [mk], ["f1%d" % b])
-        ts(T.f2[:, c], T.mjs[:, c], 0.75, 4.0, A.min, A.mult, [mk], ["f2%d" % b])
-        mms([(ps[b][:], T.i32[:], T.f1[:, c], True, False), (ps[b][:], T.i32[:], T.f2[:, c], False, True)],
-            ["i32", "f1%d" % b, "f2%d" % b], ["ps%d" % b])
-        act(T.tb0[:, P + b * 512:P + (b + 1) * 512], ps[b][:], F.Silu, ["ps%d" % b], ["tb0" if b == 3 else "tb0p%d" % b], -CK, 1.0)
-    for b in range(4):
-        mms([(ps[4 + b][:], T.dm[:], T.nxs[:, blocks[b]], True, True)], ["dm", "nxs%d" % (b // 2)], ["ps%d" % (4 + b)])
-    cp(T.oc16[:, 64:128], T.ces[:], ["ces"], ek("cn16", 0, 8))
-    for k in range(16):
-        ts(T.bb[:, k, :], T.blk[:], T.mk[:, k:k + 1], None, A.mult, None, ["blk", "mk"], ["bb"] if k == 15 else [])
-    for b in (0, 1, 2, 3):
-        cp(T.et[:, blocks[b]], ps[4 + b][:], ["ps%d" % (4 + b)], ["et" if b == 3 else "etp%d" % b])
-
-    def late_constants(x):
-        if x == 0:
-            ts(pf[4], T.pi[:, 1:2], -1.0, 15.0, A.mult, A.add, ["pi1"], ["pf4"])
-            ts(T.if32[:], vq, 0.0, None, A.is_equal, None, ["vw"], ["if32"])
-            cp(T.oc[:, 64:128], T.ces[:], ["ces"], ek("cf", 0, 8))
-            ts(T.cw[:], T.vw[:, 0:144], pf[4], 0.5, A.is_equal, A.mult, ["vw", "pf4"], ["cw"])
-        if x == 1:
-            ts(T.zw[:], T.vz[:], 15.0, 4096.0, A.is_equal, A.mult, ["vz"], ["zw"])
-            fill(T.cst[:], 3072.0 / CK, ["cst"])
-            ts(T.v2[:], T.rps[:], 2.0, None, A.mult, None, ["rps"], ["v2"])
-        if x == 2:
-            ts(T.ir[:], T.idw[:], -2.0 / KM, None, A.mult, None, ["idw"], ["ir"])
-            fill(T.als[:, WP:WP + 16], -1.0, ["als0"])
-        if x == 3:
-            ts(T.sh[:], T.vt[:, 0:128], 16.0, None, A.is_equal, None, ["vt"], ["sh"])
-        if x == 4:
-            ts(T.irf[:], T.idw[:], -2.0 / KM, None, A.mult, None, ["idw"], ["irf"])
-
-    send(1, "l1", T.l1[:], [T.stg[:, 0:256]], ["stg10", "stg11"])
-    send(2, "l2", T.l2[:], [T.stg[:, 256:512]], ["stg20", "stg21"])
+    send("l1", T.l1[:], T.stg[:, 0:256], ["stg10", "stg11"])
+    send("l2", T.l2[:], T.stg[:, 256:512], ["stg20", "stg21"])
     make_bn(128, 2, "bn2")
 
-    def unpack_uz(b):
+    blocks = [slice(b * 512, (b + 1) * 512) for b in range(4)]
+
+    def feats(a, b):
+        c, mk = blocks[a], "mjs%d" % (a // 2)
+        ts(T.f1[:, c], T.mjs[:, c], 1.0 / 6, 12.0, A.min, A.mult, [mk], ["f1%d" % a])
+        ts(T.f2[:, c], T.mjs[:, c], 0.75, 4.0, A.min, A.mult, [mk], ["f2%d" % a])
+        mms([(ps[a][:], T.i32[:], T.f1[:, c], True, False), (ps[a][:], T.i32[:], T.f2[:, c], False, True)],
+            ["i32", "f1%d" % a, "f2%d" % a], ["ps%d" % a])
+
+    def state(a, b):
+        o = T.tb0[:, P + a * 512:P + (a + 1) * 512]
+        if b:
+            ts(o, ps[a][:], -CK, None, A.add, None, ["ps%d" % a], ["tb0p%d" % a])
+        else:
+            act(o, ps[a][:], F.Silu, ["ps%d" % a], ["tb0p%d" % a], -CK, 1.0)
+
+    def diffs(a, b):
+        mms([(ps[4 + a][:], T.dm[:], T.nxs[:, blocks[a]], True, True)], ["dm", "nxs%d" % (a // 2)], ["ps%d" % (4 + a)])
+
+    def table(a, b):
+        if b:
+            cp(T.et[:, blocks[a]], ps[4 + a][:], ["ps%d" % (4 + a)], ["et%d" % a])
+        else:
+            act(T.et[:, blocks[a]], ps[4 + a][:], F.Copy, ["ps%d" % (4 + a)], ["et%d" % a])
+
+    def bb(a, b):
+        for k in range(2 * a, 2 * b):
+            ts(T.bb[:, k, :], T.blk[:], T.mk[:, k:k + 1], None, A.mult, None, ["blk", "mk"], ek("bb", a, b) if k == 2 * b - 1 else [])
+
+    def unpack(b, _):
         r0 = 4 * (b - 1)
         for x in range(2):
             dma("s", T.raw[:, r0 + 2 * x:r0 + 2 * x + 2, :], T["l%d" % b][:, 128 * x:128 * (x + 1)], ["l%d" % b], ["raw%d%d" % (b, x)])
@@ -308,6 +279,36 @@ def rank_program(g, core, T, topo):
         dma("s", T.uz[:, 4 * b:4 * b + 4, 0:H], T.raw[:, r0:r0 + 4, 0:H], rk, ["uzl%d" % b])
         dma("s", T.uz[b:8, 4 * b:4 * b + 4, H:K], T.raw[0:8 - b, r0:r0 + 4, H:K], rk, ["uzm%d" % b])
         dma("s", T.uz[0:b, 4 * b:4 * b + 4, H:K], T.raw[8 - b:8, r0:r0 + 4, H:K], rk, ["uzn%d" % b])
+
+    setup = {
+        "feats": feats, "state": state, "diffs": diffs, "table": table, "bb": bb, "unpack": unpack,
+        "vt": lambda a, b: ts(T.vt[:], T.vw[:], 127, None, A.bitwise_and, None, ["vw"], ["vt"]),
+        "vm": lambda a, b: ts(T.vm[:], T.vw[:, 0:16], 15, None, A.bitwise_and, None, ["vw"], ["vm"]),
+        "vb": lambda a, b: ts(T.vb[:], T.vb[:], 4, None, A.arith_shift_right, None, ["vb"], ["vb"]),
+        "idw": lambda a, b: ts(T.idw[:], T.vt[:], 0.0, None, A.is_equal, None, ["vt"], ["idw"]),
+        "ick": lambda a, b: act(T.i32[:], eq, F.Silu, ["idw"], ["i32"], 0.0, CK),
+        "mk": lambda a, b: ts(T.mk[:], T.vm[:], 0.0, None, A.is_equal, None, ["vm"], ["mk"]),
+        "wt": lambda a, b: ts(T.wt[:], T.vb[:], 0.0, 1.0 / KI, A.is_equal, A.mult, ["vb"], ["wt"]),
+        "pfa": lambda a, b: ts(pf[0], T.mk[:, 15:16], -16.0, 1.0, A.mult, A.add, ["mk"], ["pf0"]),
+        "pfb": lambda a, b: ts(pf[1], T.mk[:, 15:16], 2.0, -1.0, A.mult, A.add, ["mk"], ["pf1"]),
+        "blk": lambda a, b: tt(T.blk[:], T.wt[:], T.vi[:], A.mult, ["wt", "vi"], ["blk"]),
+        "ta": lambda a, b: ts(T.ta[:], vq, pf[0], pf[1], A.is_equal, A.mult, ["vw", "pf0", "pf1"], ["ta"]),
+        "vz": lambda a, b: ts(T.vz2[:], T.vz[:, 0:128], 4, None, A.arith_shift_right, None, ["vz"], ["vz2"]),
+        "dm": lambda a, b: tt(T.dm[:], T.ta[:], eq, A.add, ["ta", "idw"], ["dm"]),
+        "ub": lambda a, b: ts(T.ub[:], T.vz2[:], 0.0, None, A.is_equal, None, ["vz2"], ["ub"]),
+        "first": lambda a, b: cp(T.oc16[:, 64:128], T.ces[:], ["ces"], ek("cn16", 0, 8)),
+        "firstf": lambda a, b: cp(T.oc[:, 64:128], T.ces[:], ["ces"], ek("cf", 0, 8)),
+        "cwz": lambda a, b: ts(T.cw[:], T.idw[:, 0:144], 0.0, None, A.mult, None, ["idw"], ["cw"]),
+        "cw": lambda a, b: ts(T.cw[:, 15:143:16], T.vb[:, 0:128:16], 0.0, 0.5, A.is_equal, A.mult, ["vb", "cw"], ["cw"]),
+        "iff": lambda a, b: act(T.if32[:], eq, F.Copy, ["idw"], ["if32"]),
+        "zw": lambda a, b: ts(T.zw[:], T.vz[:], 15.0, 4096.0, A.is_equal, A.mult, ["vz"], ["zw"]),
+        "cst": lambda a, b: fill(T.cst[:], 3072.0 / CK, ["cst"]),
+        "vtwo": lambda a, b: ts(T.v2[:, 64 * a:64 * b], T.rps[:, 64 * a:64 * b], 2.0, None, A.mult, None, ["rps"], ek("v2", a, b)),
+        "ir": lambda a, b: act(T.ir[:], T.idw[:], F.Copy, ["idw"], ["ir"], 0.0, -2.0 / KM),
+        "irf": lambda a, b: act(T.irf[:], T.idw[:], F.Copy, ["idw"], ["irf"], 0.0, -2.0 / KM),
+        "minus": lambda a, b: fill(T.als[:, WP:WP + 16], -1.0, ["als0"]),
+        "sh": lambda a, b: ts(T.sh[:], T.vt[:, 0:128], 16.0, None, A.is_equal, None, ["vt"], ["sh"]),
+    }
 
     def cols(a, b):
         return slice(a * E, b * E)
@@ -318,6 +319,7 @@ def rank_program(g, core, T, topo):
     def step(t):
         st = t // 2
         tr, tw = "tb%d" % (t % 2), "tb%d" % (1 - t % 2)
+        tk = [tr] + (ek("tb0p", 0, 4) if t == 0 else [])
         iu, iz = 4 * st + t % 2, 4 * st + 2 + t % 2
         uk = ["u0"] if st == 0 else ["uzl%d" % st, "uzm%d" % st, "uzn%d" % st]
         zk = ["z0"] if st == 0 else uk
@@ -339,31 +341,31 @@ def rank_program(g, core, T, topo):
             return [tile[:, a * E + k:b * E:16] for k in range(16)]
 
         def copy(a, b):
-            dma("s", T[tw][:, P:P + W], T[tr][:, P:P + W], [tr], [tw])
+            dma("s", T[tw][:, P:P + W], T[tr][:, P:P + W], tk, [tw])
 
         def wrap(a, b):
             if a == 0:
-                act(T[tr][:, 0:P], T[tr][:, W:W + P], F.Copy, [tr], [tr + "l"])
+                act(T[tr][:, 0:P], T[tr][:, W:W + P], F.Copy, tk, [tr + "l"])
             else:
-                act(T[tr][:, P + W:WP], T[tr][:, P:2 * P], F.Copy, [tr], [tr + "r"])
+                act(T[tr][:, P + W:WP], T[tr][:, P:2 * P], F.Copy, tk, [tr + "r"])
 
         def u(a, b):
             o, ok = bank(BAR, a, (b - a) * E)
             mms([(o, T.ub[:], T.uz[:, iu, cols(a, b)], True, False)], ["ub"] + uk, [ok])
 
         def inv(a, b):
-            act(T.mi[:, cols(a, b)], T[tr][:, P:P + W].indirect(cells(a, b)), F.Silu, [tr] + cn(a, b), ek("mi", a, b), BI, SI)
+            act(T.mi[:, cols(a, b)], T[tr][:, P:P + W].indirect(cells(a, b)), F.Silu, tk + cn(a, b), ek("mi", a, b), BI, SI)
 
         def bar(a, b):
             mms([(ps[BAR[a]][:, k:(b - a) * E:16], T.bb[:, k, :], x, False, k == 15) for k, x in enumerate(classes(T.mi, a, b))],
-                ["bb"] + ek("mi", a, b), ["ps%d" % BAR[a]])
+                ek("bb", 0, 8) + ek("mi", a, b), ["ps%d" % BAR[a]])
 
         def sign(a, b):
             o, ok = bank(BAR, a, (b - a) * E)
             act(T.sn[:, cols(a, b)], o, F.Sign, [ok], ek("sn", a, b), 0.5, 1.0)
 
         def ways(a, b):
-            tt(T.pr[:, cols(a, b)], T.et[:].indirect(cells(a, b)), T.sn[:, cols(a, b)], A.mult, ["et"] + cn(a, b) + ek("sn", a, b), ek("pr", a, b))
+            tt(T.pr[:, cols(a, b)], T.et[:].indirect(cells(a, b)), T.sn[:, cols(a, b)], A.mult, ek("et", 0, 4) + cn(a, b) + ek("sn", a, b), ek("pr", a, b))
 
         def cfl(a, b):
             cp(T.oc[:, lst(a, b, 64)], cells(a, b), cn(a, b), ek("cf", a, b))
@@ -391,7 +393,7 @@ def rank_program(g, core, T, topo):
             ts(T.par[:, lst(a, b)], T.c0[:, lst(a, b)], 1, None, A.bitwise_and, None, ek("c0", a, b), ek("par", a, b))
 
         def ef(a, b):
-            tt(T.ef[:, lst(a, b)], T.par[:, lst(a, b)], T.v2[:, lst(a, b, 64 * t)], A.add, ek("par", a, b) + ["v2"], ek("ef", a, b))
+            tt(T.ef[:, lst(a, b)], T.par[:, lst(a, b)], T.v2[:, lst(a, b, 64 * t)], A.add, ek("par", a, b) + ["v2%d" % t], ek("ef", a, b))
 
         def eoff(a, b):
             cp(T.e16[:, lst(a, b)], T.ef[:, lst(a, b)], ek("ef", a, b), ek("e16", a, b))
@@ -408,7 +410,7 @@ def rank_program(g, core, T, topo):
 
         def old(a, b):
             c = cols(a, b)
-            tt(T.nw[:, c], T[tr][:, P:P + W].indirect(T.e16[:, lst(a, b)]), T.yv[:, c], A.add, [tr] + ek("e16", a, b) + ek("yv", a, b), ek("nw", a, b))
+            tt(T.nw[:, c], T[tr][:, P:P + W].indirect(T.e16[:, lst(a, b)]), T.yv[:, c], A.add, tk + ek("e16", a, b) + ek("yv", a, b), ek("nw", a, b))
 
         def put(a, b):
             act(T[tw][:, P:P + W].indirect(T.e16[:, lst(a, b)]), T.nw[:, cols(a, b)], F.Silu, ek("e16", a, b) + ek("nw", a, b), [tw])
@@ -444,14 +446,13 @@ def rank_program(g, core, T, topo):
             cp(T.oc16[:, lst(a, b, 64)], T.oc[:, lst(a, b, 64)], ek("cf", a, b), ek("cn16", a, b))
 
         def shift(a, b):
-            mms([(ps[SUM[0]][:, 0:32], T.if32[:], T.oc[:, lst(0, 4, 64)], True, True)] * (a == 0) +
-                [(ps[SUM[0]][:, 32:64], T.sh[:], T.oc[:, lst(4, 8, 64)], True, True)], ["sh", "if32"] + ek("cf", a, b), ["ps%d" % SUM[0]])
+            mms([(ps[SUM[0]][:, lst(a, b)], T.sh[:], T.oc[:, lst(a, b, 64)], True, True)], ["sh"] + ek("cf", a, b), ["ps%d" % SUM[0]])
 
         def go(a, b):
-            src, sk = (ps[SUM[0]][:, lst(a, b)], ["ps%d" % SUM[0]]) if b == 8 else (T.oc[:, lst(a, b, 64)], ek("cf", a, b))
+            src, sk = (ps[SUM[0]][:, lst(a, b)], ["ps%d" % SUM[0]]) if a else (T.oc[:, lst(a, b, 64)], ek("cf", a, b))
             cs = T["cs%d" % (st + 1)][:, lst(a, b)]
             cp(cs, src, sk, ["cs%d%d" % (st, a)])
-            send(1, "cr%d_%d" % (st + 1, a // 4), T["cr%d" % (st + 1)][:, lst(a, b)], [cs], ["cs%d%d" % (st, a)])
+            send("cr%d_%d" % (st + 1, a // 4), T["cr%d" % (st + 1)][:, lst(a, b)], cs, ["cs%d%d" % (st, a)])
 
         def turn(tile, a):
             r = 16 * st * (a // 4)
@@ -463,8 +464,10 @@ def rank_program(g, core, T, topo):
         def nulls(a, x):
             return [(ps[2 + a // 4][:, k:H:16], turn(T.bn[:, k, :], a), x, False, k == 15) for k in range(16)]
 
+        bk = ["bn"] + ["bn2"] * (st > 0)
+
         def spread(a, b):
-            mms(nulls(a, T.nl[:, lst(a, b)]), ["bn"] + ["bn2"] * (st > 0) + ek("nl", a, b), ["ps%d" % (2 + a // 4)])
+            mms(nulls(a, T.nl[:, lst(a, b)]), bk + ek("nl", a, b), ["ps%d" % (2 + a // 4)])
 
         def alpha(a, b):
             return T.als[:].indirect(T.oc16[:, lst(a, b)])
@@ -478,24 +481,22 @@ def rank_program(g, core, T, topo):
         def plain(a, b):
             cp(T.tt[:, cols(a, b)], alpha(a, b), ak(a, b), ek("tt", a, b))
 
-        def aplain(a, b):
-            act(T.tt[:, cols(a, b)], alpha(a, b), F.Copy, ak(a, b), ek("tt", a, b))
-
         def y(a, b):
             h = a // 4
             tt(T.yy[:, cols(a, b)], T.tt[:, cols(a, b)], ps[2 + h][:, cols(a - 4 * h, b - 4 * h)], A.mult, ek("tt", a, b) + ["ps%d" % (2 + h)], ek("yy", a, b))
 
         def nm(a, b):
-            ts(T.nm[:], T.nl[:, lst(4, 8)], -1.0, None, A.mult, None, ek("nl", 4, 8), ["nm"])
+            ts(T.nm[:, lst(a, b)], T.nl[:, lst(a, b)], -1.0, None, A.mult, None, ek("nl", a, b), ek("nm", a, b))
 
         def arho(a, b):
-            tt(T.tt[:, H:K], alpha(4, 8), T.rho[:, H:K], A.mult, ak(4, 8) + ek("rho", 4, 8), ek("tt", 4, 8))
+            tt(T.tt[:, cols(a, b)], alpha(a, b), T.rho[:, cols(a, b)], A.mult, ak(a, b) + ek("rho", a, b), ek("tt", a, b))
 
         def factor(a, b):
-            mms([(ps[3][:], turn(T.irf, 4), T.tt[:, H:K], True, False)] + nulls(4, T.nm[:]), ["irf", "bn", "bn2", "nm"] + ek("tt", 4, 8), ["ps3"])
+            mms([(ps[2 + a // 4][:], turn(T.irf, a), T.tt[:, cols(a, b)], True, False)] + nulls(a, T.nm[:, lst(a, b)]),
+                ["irf"] + bk + ek("nm", a, b) + ek("tt", a, b), ["ps%d" % (2 + a // 4)])
 
         def yu(a, b):
-            tt(T.yy[:, H:K], ps[3][:], T[prev][:, H:K], A.mult, ["ps3"] + ek(prev + "_", 4, 8), ek("yy", 4, 8))
+            tt(T.yy[:, cols(a, b)], ps[2 + a // 4][:], T[prev][:, cols(a, b)], A.mult, ["ps%d" % (2 + a // 4)] + ek(prev + "_", a, b), ek("yy", a, b))
 
         def gather(a, b):
             act(T.ag[:, cols(a, b)], alpha(a, b), F.Copy, ak(a, b), ek("ag", a, b))
@@ -513,30 +514,33 @@ def rank_program(g, core, T, topo):
 
         def on(a, b):
             c = cols(a, b)
-            send(1, "win%d_%d" % (st + 1, a // 4), T["win%d" % (st + 1)][:, c], [w[:, c]], ek("w%d_" % t, a, b))
+            send("win%d_%d" % (st + 1, a // 4), T["win%d" % (st + 1)][:, c], w[:, c], ek("w%d_" % t, a, b))
 
         def tally(a, b):
-            send(-1, "tin", T.tin[:], [T.win1[:], T.w2[:], T.w3[:]], ek("win1_", 0, 8) + ek("w2_", 0, 8) + ek("w3_", 0, 8))
+            send("tin%d" % t, T["tin%d" % t][:], w[:], ek("w%d_" % t, 0, 8))
 
         def more(a, b):
-            dma("g", T.tin[:], T.w0[:], ["tin"] + ek("w0_", 0, 8), ["tin"], A.add)
+            src, sk = (T["tin%d" % a], ["tin%d" % a]) if a > 1 else (T.w1, ek("w1_", 0, 8))
+            dma("g", T.w0[:], src[:], sk + ek("w0_", 0, 8), ek("w0_", 0, 8), A.add)
+
+        def four(a, b):
+            send("w4in_%d" % (a // 4), T.w4in[:, cols(a, b)], T.w4[:, cols(a, b)], ek("w4_", a, b))
+
+        def early(a, b):
+            mms([(ps[TAL[a]][:], T.if32[:], T.w0[:, cols(a, b)], True, False)], ["if32"] + ek("w0_", a, b), ["ps%d" % TAL[a]])
+
+        def late(a, b):
+            mms([(ps[TAL[a]][:], T.if32[:], T.w4in[:, cols(a, b)], False, True)], ["if32"] + ek("w4in_", a, b), ["ps%d" % TAL[a]])
 
         def home(a, b):
             c = cols(a, b)
-            send(2, "fin%d" % FIN.index(a), T.fin[:, c], [T.w4[:, c], w[:, c]], ek("w4_", a, b) + ek("w5_", a, b))
+            send("fin%d" % FIN.index(a), T.fin[:, c], T.yy[:, c], ek("yy", a, b))
 
-        def consts(a, b):
-            late_constants(a)
-
-        def unpack(a, b):
-            unpack_uz(a)
-
-        return {"copy": copy, "u": u, "inv": inv, "bar": bar, "ways": ways, "wrap": wrap, "cfl": cfl, "sign": sign, "cell": cell, "add": add,
-                "cint": cint, "coff": coff, "m": m, "par": par, "ef": ef, "eoff": eoff, "even": even, "rho": rho, "flag": flag,
-                "old": old, "put": put, "z": z, "hero": hero, "null": null, "oa": oa, "aoff": aoff, "xf": xf, "cf": cf, "noff": noff,
-                "shift": shift, "go": go, "two": two, "spread": spread, "fused": fused, "plain": plain, "aplain": aplain, "y": y, "nm": nm, "arho": arho,
-                "factor": factor, "yu": yu, "gather": gather, "rot": rot, "times": times, "clip": clip, "on": on, "tally": tally, "more": more,
-                "home": home, "consts": consts, "unpack": unpack}
+        return dict(setup, copy=copy, u=u, inv=inv, bar=bar, ways=ways, wrap=wrap, cfl=cfl, sign=sign, cell=cell, add=add, cint=cint, coff=coff,
+                    m=m, par=par, ef=ef, eoff=eoff, even=even, rho=rho, flag=flag, old=old, put=put, z=z, hero=hero, null=null, oa=oa,
+                    aoff=aoff, xf=xf, cf=cf, noff=noff, shift=shift, go=go, two=two, spread=spread, fused=fused, plain=plain, y=y, nm=nm,
+                    arho=arho, factor=factor, yu=yu, gather=gather, rot=rot, times=times, clip=clip, on=on, tally=tally, more=more,
+                    four=four, early=early, late=late, home=home)
 
     calls = [step(t) for t in range(NT)]
     for t in range(NT):
@@ -546,7 +550,9 @@ def rank_program(g, core, T, topo):
 
     for i in range(len(FIN) - 1):
         c = cols(FIN[i], FIN[i + 1])
-        tt(T.res[:, c], T.fin[:, c], T.tin[:, c], A.add, ["fin%d" % i, "tin"], ["res%d" % i])
+        h = FIN[i] // 4 * 4
+        ts(T.w5[:, c], T.fin[:, c], 0.125, 4.0, A.max, A.min, ["fin%d" % i], ["w5_%d" % i])
+        tt(T.res[:, c], T.w5[:, c], ps[TAL[h]][:, cols(FIN[i] - h, FIN[i + 1] - h)], A.add, ["w5_%d" % i, "ps%d" % TAL[h]], ["res%d" % i])
         dma("s" if i % 2 == 0 else "a", T.tl[:, c], T.res[:, c], ["res%d" % i], [])
     for s in total:
         if max(waited[q].get(s, 0) for q in eng) < total[s]:

import math
import numpy as np
from concourse.bass import DstId, RemoteDMATransfer
from concourse.mybir import AluOpType as A, ActivationFunctionType as F

W, K, NT = 2048, 1024, 6
H = K // 2
E = K // 8
P = 256
WP = W + 2 * P
RW = 160
CK = 32.0
KM = 2.0 ** -48
KI = 2.0 ** -52


def _fit(e0, sign):
    xs = []
    for k in range(5):
        t = (e0 + sign * k) * math.log(2.0)
        x = -40.0
        for _ in range(60):
            x = t - math.log(-x)
        xs.append(x)
    s, b = np.polyfit(np.arange(5.0), np.array(xs), 1)
    return float(s) / CK, float(b)


SM, BM = _fit(-52, 1)
SI, BI = _fit(-48, -1)

BAR = {0: 0, 2: 1, 4: 4, 6: 4}
SUM = {0: 5, 2: 7, 4: 7, 6: 5}
HERO = {0: 6, 4: 7}
ROT = {0: 0, 2: 1, 4: 5, 6: 0, 8: 1}
TAL = {0: 4, 4: 1}
FIN = [0, 2, 4, 6, 8]
ORDER = [
    'vm00 vt00 mk00 vb00 idw00 irf00 ick00 iff00 pfa00 pfb00 wt00 ta00 blk00 dm00 diffs10 diffs00 feats00 ir00 table10 feats10 feats20 feats30 diffs20 diffs30 state00 state10 state20 vz00 first00 bb02 minus00 ub00 state31 bb68 firstf00 bb46 bb24 zw00 cst00 table21 cwz00 table31 cw00 copy00 table00 inv04 inv48 u48 u04 cell04 bar04 bar48 sign04 sign48 wrap00 wrap11 ways04 ways48 z08 +u04 cell48 add04 add48 coff04 cint04 vtwo01 m02 m24 par04 ef04 coff48 m46 m68 rho02 cint48 eoff04 flag02 rho24 old02 par48 flag24 rho46 put02 old24 ef48 rho68 eoff48 flag46 flag68 old46 put24 hero08 two48 two04 even08 null08 old68 oa08 xf08 sh00 aoff08 cf08 vtwo15 noff08 put46 plain48 plain04 put68 +copy00 unpack10',
    'inv04 z04 cell48 cell04 u48 -spread48 -spread04 bar04 inv48 bar48 -y48 -y04 -clip48 sign04 wrap00 sign48 wrap11 ways04 add04 ways48 add48 coff04 cint04 m02 m24 -clip04 par04 cint48 coff48 rho02 ef04 m46 m68 rho24 eoff04 flag02 rho46 old02 rho68 z48 hero04 two04 hero48 put02 null04 flag24 par48 even08 xf04 old24 ef48 null48 put24 cf04 flag46 xf48 eoff48 flag68 go04 cf48 old46 put46 old68 two48 spread04 spread48 shift48 +u04 put68 go48 oa04 oa48 aoff08 +copy00 unpack20',
    'inv04 inv48 bar04 u48 bar48 -fused04 -fused48 -y04 -y48 cfl04 -clip04 cfl48 -clip48 -on04 -on48 more10 sign04 sign48 wrap11 wrap00 ways04 ways48 cell04 cell48 z08 +u04 add04 add48 coff04 m02 m24 cint04 par04 ef04 cint48 rho02 coff48 eoff04 m46 m68 flag02 rho24 old02 put02 par48 flag24 rho46 ef48 old24 put24 eoff48 flag46 rho68 hero08 two04 old46 even08 flag68 put46 null08 old68 xf08 oa08 put68 cf08 aoff08 noff08 +copy00',
    'inv04 -spread04 cell48 cell04 inv48 -fused04 -arho48 -y04 -nm48 -clip04 z04 u48 bar04 bar48 -factor48 sign04 sign48 wrap00 wrap11 ways04 ways48 add04 add48 -yu48 coff04 cint04 m02 m24 -clip48 -tally00 cint48 par04 coff48 rho02 ef04 rho24 eoff04 flag02 m68 m46 rho68 old02 rho46 hero04 z48 hero48 put02 flag24 null04 par48 even08 old24 xf04 ef48 null48 cf04 eoff48 xf48 go04 flag46 put24 cf48 oa04 old46 oa48 two04 shift48 spread04 +z08 +u48 put46 go48 flag68 aoff08 nm48 old68 arho48 put68 +copy00',
    'inv04 inv48 -fused04 u04 -factor48 bar04 bar48 sign04 wrap00 sign48 wrap11 -y04 cfl04 -clip04 -yu48 cfl48 -clip48 ways04 ways48 cell48 cell04 add04 add48 cint04 coff04 m02 m24 par04 -on04 -on48 -tally00 more20 ef04 coff48 cint48 rho02 par48 eoff04 flag02 m68 m46 rho24 old02 put02 ef48 flag24 rho46 old24 rho68 flag46 eoff48 put24 +u04 two04 hero08 flag68 old46 put46 old68 null08 oa08 even08 xf08 put68 aoff08 nm48 cf08 arho48 noff08',
    'inv04 inv48 u48 -spread04 z04 cell04 cell48 -factor48 -fused04 -y04 bar04 bar48 -yu48 -clip04 sign04 wrap11 sign48 wrap00 -clip48 four04 four48 more30 ways04 add04 ways48 add48 coff04 coff48 cint48 m02 m24 rho02 rho24 m68 m46 z48 hero04 rho68 rho46 cint04 oa04 null04 aoff04 hero48 two04 oa48 fused02 aoff48 null48 gather46 gather68 spread04 two48 spread48 rot46 rot68 early04 late04 early48 late48 y02 fused24 y24 times46 home02 home24 y46 times68 y68 home46 home68',
]
ORDER = [
'vt00 vm00 idw00 ick00 mk00 vb00 pfa00 pfb00 wt00 ta00 blk00 dm00 diffs00 table00 diffs10 table10 feats00 state00 feats10 state10 feats20 state20 feats30 state30 diffs20 diffs30 vz00 first00 ub00 bb08 table21 table31 copy00 inv04 inv48 u48 u04 bar04 bar48 iff00 cwz00 firstf00 cw00 sign04 sign48 wrap11 wrap00 ir00 irf00 ways04 ways48 vtwo01 zw00 cst00 cell04 cell48 +u04 add04 add48 z08 coff04 cint04 m02 m24 minus00 par04 ef04 coff48 eoff04 rho02 m46 m68 rho24 flag02 flag24 old02 cint48 rho46 par48 old24 put02 flag46 ef48 rho68 eoff48 even08 flag68 old46 put24 +u48 two04 hero08 put46 oa08 null08 old68 xf08 aoff08 cf08 noff08 plain48 plain04 sh00 vtwo15 put68 +copy00 unpack10',
'inv04 -two48 z04 cell48 cell04 -spread48 -spread04 bar04 inv48 bar48 -y48 -y04 -clip48 sign04 wrap00 sign48 wrap11 ways04 add04 ways48 add48 coff04 cint04 m02 m24 -clip04 par04 cint48 coff48 rho02 ef04 m46 m68 rho24 flag02 eoff04 rho46 old02 rho68 flag24 z48 two04 hero04 hero48 put02 even08 null04 par48 old24 xf04 ef48 null48 flag46 put24 cf04 eoff48 xf48 flag68 go04 cf48 old46 put46 old68 two48 spread04 shift48 put68 go48 oa04 oa48 aoff08 +copy00 unpack20',
'inv04 inv48 u48 u04 -spread48 z08 bar04 bar48 -fused04 -fused48 -y04 cfl04 -y48 cfl48 -clip04 -clip48 -on04 -on48 more10 sign04 wrap00 sign48 wrap11 ways04 ways48 cell04 cell48 +u04 add04 add48 coff04 m02 m24 cint04 par04 ef04 cint48 rho02 coff48 eoff04 m68 m46 flag02 rho24 old02 put02 par48 flag24 rho46 ef48 old24 put24 rho68 eoff48 flag46 +u48 two04 hero08 flag68 old46 put46 even08 null08 old68 xf08 oa08 cf08 aoff08 nm48 put68 noff08 +copy00',
'inv04 -spread04 cell04 cell48 z04 bar04 inv48 -fused04 -arho48 -y04 -clip04 bar48 -factor48 sign04 sign48 wrap00 wrap11 ways04 ways48 add04 add48 -yu48 coff04 cint04 m02 m24 -clip48 -tally00 coff48 par04 cint48 rho02 ef04 rho24 flag02 eoff04 m68 m46 rho68 old02 rho46 +u48 +u04 z48 two04 hero04 hero48 put02 flag24 null04 par48 even08 old24 ef48 xf04 null48 flag46 cf04 xf48 eoff48 go04 cf48 put24 old46 oa04 oa48 spread04 shift48 +z08 put46 go48 flag68 nm48 aoff08 old68 arho48 put68 +copy00',
'inv04 inv48 -fused04 -factor48 bar04 bar48 sign04 wrap11 sign48 wrap00 cfl04 -y04 cfl48 -yu48 -clip04 ways04 ways48 cell04 +u04 cell48 add04 add48 +u48 cint04 coff04 m02 m24 -clip48 par04 -on04 -on48 -tally00 more20 cint48 coff48 ef04 rho02 par48 eoff04 m68 m46 flag02 rho24 old02 put02 ef48 flag24 rho46 old24 eoff48 rho68 flag46 put24 two04 hero08 flag68 old46 put46 old68 null08 oa08 even08 xf08 put68 aoff08 nm48 cf08 arho48 noff08',
'inv04 inv48 -spread04 z04 -fused04 -y04 -factor48 bar04 cell48 cell04 bar48 -yu48 -clip04 sign04 wrap11 sign48 wrap00 -clip48 four04 four48 more30 ways04 add04 ways48 add48 coff04 coff48 cint48 m02 m24 rho02 rho24 m68 m46 z48 hero04 rho68 rho46 cint04 null04 oa04 aoff04 two04 hero48 oa48 fused02 aoff48 null48 gather46 gather68 two48 spread04 spread48 rot46 rot68 early04 late04 early48 late48 y02 fused24 y24 times46 home02 home24 y46 times68 y68 home46 home68',
]
ORDER = ['vm00 vt00 mk00 idw00 ick00 pfa00 pfb00 vb00 ta00 wt00 dm00 diffs00 table00 diffs10 table10 cst00 feats00 state00 feats10 state10 feats20 state20 feats30 vz00 blk00 state30 ub00 first00 bb08 copy00 iff00 inv04 inv48 u04 diffs30 u48 diffs20 bar04 bar48 sign04 firstf00 cwz00 zw00 table21 cw00 table31 sh00 vtwo01 sign48 wrap11 irf00 ways04 ways48 cell04 cell48 +u04 add04 +u48 add48 coff04 ir00 wrap00 m02 m24 cint04 minus00 par04 ef04 coff48 rho02 eoff04 m68 m46 rho24 flag02 flag24 old02 cint48 rho46 par48 old24 put02 ef48 rho68 eoff48 flag46 flag68 old46 even08 put24 two04 z08 hero08 put46 null08 oa08 old68 xf08 vtwo15 cf08 aoff08 noff08 plain48 plain04 put68 +copy00 unpack10', 'inv04 -two48 z04 -spread04 cell48 cell04 -spread48 inv48 bar04 bar48 -y48 -y04 -clip48 sign04 sign48 wrap00 wrap11 ways04 add04 ways48 add48 coff04 cint04 m02 m24 -clip04 par04 coff48 cint48 rho02 ef04 m46 m68 rho24 flag02 eoff04 rho46 old02 rho68 flag24 z48 hero04 two04 hero48 put02 null04 even08 par48 old24 ef48 xf04 null48 flag46 put24 eoff48 cf04 xf48 flag68 go04 cf48 old46 put46 old68 two48 spread04 spread48 shift48 +u04 +u48 put68 go48 oa04 oa48 aoff08 +copy00 unpack20', 'inv04 inv48 z08 bar04 bar48 -fused04 -fused48 -y04 cfl04 -y48 cfl48 -clip04 -clip48 -on04 -on48 more10 sign04 sign48 wrap11 wrap00 ways04 ways48 cell04 cell48 +u04 add04 +u48 add48 coff04 m02 m24 cint04 par04 ef04 cint48 rho02 coff48 eoff04 m68 m46 flag02 rho24 old02 put02 flag24 par48 rho46 old24 ef48 put24 rho68 eoff48 flag46 two04 hero08 flag68 old46 put46 null08 oa08 even08 old68 xf08 aoff08 cf08 put68 noff08 +copy00', 'inv04 -spread04 z04 cell48 cell04 bar04 inv48 -fused04 -nm48 -y04 -arho48 -clip04 bar48 -factor48 sign04 sign48 wrap00 wrap11 ways04 ways48 add04 +u04 add48 -yu48 coff04 cint04 m02 m24 -clip48 -tally00 coff48 cint48 par04 rho02 ef04 rho24 flag02 eoff04 m68 m46 rho68 old02 rho46 z48 +u48 two04 hero04 hero48 put02 flag24 null04 even08 par48 old24 xf04 ef48 null48 flag46 cf04 xf48 eoff48 go04 cf48 put24 oa04 old46 spread04 shift48 put46 oa48 go48 flag68 aoff08 nm48 old68 arho48 put68 +copy00', 'inv04 inv48 -fused04 z08 -factor48 bar04 bar48 sign04 sign48 wrap11 wrap00 cfl04 -y04 cfl48 -clip04 -yu48 ways04 ways48 cell04 cell48 +u04 add04 +u48 add48 coff04 cint04 m02 m24 -clip48 par04 -on04 -on48 -tally00 more20 coff48 cint48 ef04 rho02 eoff04 par48 m46 m68 flag02 rho24 old02 put02 flag24 rho46 ef48 old24 eoff48 rho68 flag46 put24 two04 hero08 flag68 old46 put46 old68 null08 oa08 even08 xf08 put68 aoff08 nm48 cf08 arho48 noff08', 'inv04 inv48 z04 cell48 cell04 -spread04 -fused04 -y04 -factor48 bar04 bar48 -yu48 -clip04 sign04 sign48 wrap11 wrap00 -clip48 four04 four48 more30 ways04 add04 ways48 add48 coff04 coff48 cint48 m02 m24 rho02 rho24 m68 m46 z48 hero04 rho68 rho46 cint04 oa04 null04 aoff04 two04 hero48 oa48 fused02 aoff48 null48 gather46 gather68 two48 spread04 spread48 rot46 early04 rot68 late04 early48 late48 y02 fused24 y24 times46 home02 home24 y46 times68 y68 home46 home68']

SCRATCH = {
    "sgs": ("sbuf", [128, WP], "bfloat16"), "als": ("sbuf", [128, WP + 16], "bfloat16"),
    "mjs": ("sbuf", [128, W], "bfloat16"), "nxs": ("sbuf", [128, W], "bfloat16"),
    "f1": ("sbuf", [128, W], "bfloat16"), "f2": ("sbuf", [128, W], "bfloat16"),
    "tb0": ("sbuf", [128, WP], "float32"), "tb1": ("sbuf", [128, WP], "float32"),
    "et": ("sbuf", [128, W], "float32"),
    "ces": ("sbuf", [128, 64], "int32"), "rps": ("sbuf", [128, 320], "int32"), "v2": ("sbuf", [128, 320], "float32"),
    "uz": ("sbuf", [8, 12, K], "bfloat16"), "raw": ("sbuf", [8, 8, K], "bfloat16"),
    "stg": ("sbuf", [128, 512], "bfloat16"),
    "l1": ("dram", [128, 256], "bfloat16"), "l2": ("dram", [128, 256], "bfloat16"),
    "pf": ("sbuf", [128, 4], "float32"),
    "vw": ("sbuf", [128, RW], "int32"), "vt": ("sbuf", [128, RW], "int32"),
    "vb": ("sbuf", [128, 128], "int32"), "vi": ("sbuf", [128, 128], "int32"), "vm": ("sbuf", [128, 16], "int32"),
    "vz": ("sbuf", [8, 144], "int32"), "vz2": ("sbuf", [8, 128], "int32"),
    "mk": ("sbuf", [128, 16], "float32"), "wt": ("sbuf", [128, 128], "bfloat16"), "blk": ("sbuf", [128, 128], "bfloat16"),
    "bb": ("sbuf", [128, 16, 128], "bfloat16"), "dd": ("sbuf", [128, 16, 128], "bfloat16"), "bn": ("sbuf", [128, 16, RW], "bfloat16"),
    "idw": ("sbuf", [128, RW], "bfloat16"), "i32": ("sbuf", [128, 128], "bfloat16"), "ir": ("sbuf", [128, RW], "bfloat16"),
    "irf": ("sbuf", [128, RW], "float32"), "if32": ("sbuf", [128, 128], "float32"), "sh": ("sbuf", [128, 128], "float32"),
    "ta": ("sbuf", [128, 128], "bfloat16"), "dm": ("sbuf", [128, 128], "bfloat16"),
    "cw": ("sbuf", [128, 144], "float16"), "zw": ("sbuf", [8, 144], "bfloat16"),
    "ub": ("sbuf", [8, 128], "bfloat16"), "cst": ("sbuf", [128, 64], "bfloat16"),
    "mi": ("sbuf", [128, K], "bfloat16"), "sn": ("sbuf", [128, K], "bfloat16"), "pr": ("sbuf", [128, K], "float16"),
    "mg": ("sbuf", [128, K], "bfloat16"), "rho": ("sbuf", [128, K], "bfloat16"), "yv": ("sbuf", [128, K], "bfloat16"),
    "ag": ("sbuf", [128, K], "bfloat16"),
    "nw": ("sbuf", [128, K], "float32"), "tt": ("sbuf", [128, K], "float32"), "yy": ("sbuf", [128, K], "float32"),
    "oc": ("sbuf", [128, 128], "float32"), "oc16": ("sbuf", [128, 128], "uint16"),
    "c0": ("sbuf", [128, 64], "int32"), "c16": ("sbuf", [128, 64], "uint16"),
    "par": ("sbuf", [128, 64], "int32"), "ef": ("sbuf", [128, 64], "float32"), "e16": ("sbuf", [128, 64], "uint16"),
    "ev": ("sbuf", [128, 64], "int32"), "nl": ("sbuf", [128, 64], "bfloat16"), "nm": ("sbuf", [128, 64], "bfloat16"),
    "xf": ("sbuf", [128, 64], "float32"),
}
for _n in ["fin", "tin2", "tin3", "res", "w4in", "win1", "win2"] + ["w%d" % _t for _t in range(NT)]:
    SCRATCH[_n] = ("sbuf", [128, K], "float32")
for _b in (1, 2):
    SCRATCH["cs%d" % _b] = ("sbuf", [128, 64], "uint16")
    SCRATCH["cr%d" % _b] = ("sbuf", [128, 64], "uint16")
for _b in range(8):
    SCRATCH["ps%d" % _b] = ("psum", [128, 512], "float32")

ARR = {"l1": 1, "l2": 2, "tin2": -1, "tin3": -1, "w4in_0": 2, "w4in_1": 2}
ARR.update({"%s%d_%d" % (_n, _b, _h): 1 for _n in ("cr", "win") for _b in (1, 2) for _h in (0, 1)})
ARR.update({"fin%d" % _i: 2 for _i in range(len(FIN) - 1)})
SEMAPHORES = ["qv", "qa", "qp", "qg", "ls"] + ["r_" + _n for _n in ARR] + ["d%d" % _i for _i in range(64)]


def rank_program(g, core, T, topo):
    rank = T.rank_of(core)
    if rank is None:
        return
    n = len(T.cores)
    eng = {"v": g.vector, "a": g.scalar, "p": g.tensor, "g": g, "s": g.sync}
    cnt = {"v": 0, "a": 0, "p": 0, "g": 0, "d": 0, "ls": 0}
    waited = {q: {} for q in eng}
    total = {}
    wr = {}
    rd = {}

    def need(q, ev, same):
        if ev is None or (ev[2] == q and not same):
            return
        if waited[q].get(ev[0], 0) < ev[1]:
            eng[q].wait_ge(T.sem[ev[0]], ev[1])
            waited[q][ev[0]] = ev[1]

    def order(q, reads, writes):
        for k in reads:
            need(q, wr.get(k), True)
            if k.startswith("ps"):
                for e in rd.get(k, []):
                    need(q, e, False)
        for k in writes:
            need(q, wr.get(k), q != "p")
            for e in rd.get(k, []):
                need(q, e, q != "p")

    def note(ev, reads, writes):
        total[ev[0]] = ev[1]
        for k in reads:
            rd.setdefault(k, []).append(ev)
        for k in writes:
            wr[k] = ev
            rd[k] = []

    def op(q, fn, reads, writes):
        order(q, reads, writes)
        cnt[q] += 1
        fn().then_inc(T.sem["q" + q], 1)
        note(("q" + q, cnt[q], q), reads, writes)

    def dma(q, out, in_, reads, writes, accum=None):
        order(q, reads, writes)
        s = "d%d" % cnt["d"]
        cnt["d"] += 1
        (eng[q].dma_start(out, in_, accum_op=accum) if accum is not None else eng[q].dma_start(out, in_)).then_inc(T.sem[s], 16)
        note((s, 16, None), reads, writes)

    def mms(lst, reads, writes):
        def fn():
            ins = None
            for m in lst:
                ins = g.tensor.matmul(m[0], m[1], m[2], m[3], m[4])
            return ins
        op("p", fn, reads, writes)

    def lanes(src, dst):
        far = [c for c in T.cores if topo.chip(c) != topo.chip(src)][0]
        return [e for e in topo.engines(src, dst) if topo.chip(dst) != topo.chip(src) or e not in topo.engines(src, far)]

    def send(name, out, src, reads):
        dst = T.cores[(rank + ARR[name]) % n]
        rid, pid, _ = topo.addr(dst)
        order("g", reads, [])
        g.remote_dma(out, src, T.sem["r_" + name], T.sem.ls, pid, rid, sum(1 << e for e in lanes(core, dst)))
        cnt["ls"] += len(lanes(core, dst))
        total["ls"] = cnt["ls"]

    def ek(nm, a, b):
        return ["%s%d" % (nm, x) for x in range(a, b)]

    for name in ARR:
        keys = ek(name[:-1], 4 * int(name[-1]), 4 * int(name[-1]) + 4) if "_" in name else [name]
        note(("r_" + name, len(lanes(T.cores[(rank - ARR[name]) % n], core)), None), [], keys)

    V, S = g.vector, g.scalar

    def ts(out, in0, s1, s2, o0, o1, reads, writes):
        if s2 is None:
            op("v", lambda: V.tensor_scalar(out, in0, s1, None, o0), reads, writes)
        else:
            op("v", lambda: V.tensor_scalar(out, in0, s1, s2, o0, o1), reads, writes)

    def tt(out, in0, in1, o, reads, writes):
        op("v", lambda: V.tensor_tensor(out, in0, in1, o), reads, writes)

    def cp(out, in_, reads, writes):
        op("v", lambda: V.tensor_copy(out, in_), reads, writes)

    def fill(out, x, writes):
        op("v", lambda: V.memset(out, x), [], writes)

    def act(out, in_, f, reads, writes, bias=None, scale=None):
        if bias is None:
            op("a", lambda: S.activation(out, in_, f), reads, writes)
        else:
            op("a", lambda: S.activation(out, in_, f, bias=bias, scale=scale), reads, writes)

    ps = [T["ps%d" % b] for b in range(8)]

    def wrapped(nm, src):
        dma("s", T[nm + "s"][:, P:P + W], src[:], [], [nm + "s"])
        dma("s", T[nm + "s"][:, 0:P], src[:, W - P:W], [], [nm + "l"])
        dma("s", T[nm + "s"][:, P + W:WP], src[:, 0:P], [], [nm + "r"])

    dma("s", T.mjs[:, 0:K], T.mj[:, 0:K], [], ["mjs0"])
    dma("a", T.nxs[:, 0:K], T.nx[:, 0:K], [], ["nxs0"])
    dma("s", T.mjs[:, K:W], T.mj[:, K:W], [], ["mjs1"])
    dma("a", T.ces[:], T.ce[:], [], ["ces"])
    dma("s", T.nxs[:, K:W], T.nx[:, K:W], [], ["nxs1"])
    dma("a", T.uz[:, 0:2, :], T.uu[:, 0:2 * K], [], ["u0"])
    wrapped("sg", T.sg)
    dma("s", T.rps[:], T.rp[:], [], ["rps"])
    dma("s", T.uz[:, 2:4, :], T.zz[:, 0:2 * K], [], ["z0"])
    wrapped("al", T.al)
    for b in (1, 2):
        for x, src in enumerate((T.uu, T.zz)):
            c = (b - 1) * 256 + x * 128
            dma("s", T.stg[:, c:c + 128], src[:, 2 * b * K:2 * (b + 1) * K], [], ["stg%d%d" % (b, x)])

    pf = [T.pf[:, i:i + 1] for i in range(2)]
    vq = T.vw[:, 0:128]
    eq = T.idw[:, 0:128]
    op("g", lambda: g.iota(T.vw[:], [[1, RW]], 0, -1), [], ["vw"])
    op("g", lambda: g.iota(T.vb[:], [[-16, 8], [0, 16]], 0, 1), [], ["vb"])
    op("g", lambda: g.iota(T.vi[:], [[0, 8], [1, 16]], 0, 0), [], ["vi"])
    op("g", lambda: g.iota(T.vz[:], [[1, 144]], 0, -16), [], ["vz"])
    fill(T.dd[:, 0:10, :], 0.0, ["dz"])
    op("g", lambda: g.iota(T.dd[:, 10:16, :], [[0, 768]], 0, 0, allow_small_or_imprecise_dtypes=True), [], ["dd"])
    op("g", lambda: g.affine_select(T.dd[:], T.dd[:], [[-256, 16], [-16, 8], [255, 16]], A.not_equal, (2.0 ** 20) / KM, 0, 1), ["dd", "dz"], ["dd"])

    def make_bn(c0, ng, key):
        v = T.bn[:, :, c0:c0 + 16 * ng]
        op("g", lambda: g.iota(v, [[0, 256 * ng]], -2, 0, allow_small_or_imprecise_dtypes=True), [], [key])
        op("g", lambda: g.affine_select(v, v, [[-1, 16], [-16, ng], [0, 16]], A.is_equal, 0.0, 0, 1), [key], [key])

    make_bn(0, 8, "bn")
    send("l1", T.l1[:], T.stg[:, 0:256], ["stg10", "stg11"])
    send("l2", T.l2[:], T.stg[:, 256:512], ["stg20", "stg21"])
    make_bn(128, 2, "bn2")

    blocks = [slice(b * 512, (b + 1) * 512) for b in range(4)]

    def feats(a, b):
        c, mk = blocks[a], "mjs%d" % (a // 2)
        ts(T.f1[:, c], T.mjs[:, c], 1.0 / 6, 12.0, A.min, A.mult, [mk], ["f1%d" % a])
        ts(T.f2[:, c], T.mjs[:, c], 0.75, 4.0, A.min, A.mult, [mk], ["f2%d" % a])
        mms([(ps[a][:], T.i32[:], T.f1[:, c], True, False), (ps[a][:], T.i32[:], T.f2[:, c], False, True)],
            ["i32", "f1%d" % a, "f2%d" % a], ["ps%d" % a])

    def state(a, b):
        o = T.tb0[:, P + a * 512:P + (a + 1) * 512]
        if b:
            ts(o, ps[a][:], -CK, None, A.add, None, ["ps%d" % a], ["tb0p%d" % a])
        else:
            act(o, ps[a][:], F.Silu, ["ps%d" % a], ["tb0p%d" % a], -CK, 1.0)

    def diffs(a, b):
        mms([(ps[4 + a][:], T.dm[:], T.nxs[:, blocks[a]], True, True)], ["dm", "nxs%d" % (a // 2)], ["ps%d" % (4 + a)])

    def table(a, b):
        if b:
            cp(T.et[:, blocks[a]], ps[4 + a][:], ["ps%d" % (4 + a)], ["et%d" % a])
        else:
            act(T.et[:, blocks[a]], ps[4 + a][:], F.Copy, ["ps%d" % (4 + a)], ["et%d" % a])

    def bb(a, b):
        for k in range(2 * a, 2 * b):
            ts(T.bb[:, k, :], T.blk[:], T.mk[:, k:k + 1], None, A.mult, None, ["blk", "mk"], ek("bb", a, b) if k == 2 * b - 1 else [])

    def unpack(b, _):
        r0 = 4 * (b - 1)
        for x in range(2):
            dma("s", T.raw[:, r0 + 2 * x:r0 + 2 * x + 2, :], T["l%d" % b][:, 128 * x:128 * (x + 1)], ["l%d" % b], ["raw%d%d" % (b, x)])
        rk = ["raw%d0" % b, "raw%d1" % b]
        dma("s", T.uz[:, 4 * b:4 * b + 4, 0:H], T.raw[:, r0:r0 + 4, 0:H], rk, ["uzl%d" % b])
        dma("s", T.uz[b:8, 4 * b:4 * b + 4, H:K], T.raw[0:8 - b, r0:r0 + 4, H:K], rk, ["uzm%d" % b])
        dma("s", T.uz[0:b, 4 * b:4 * b + 4, H:K], T.raw[8 - b:8, r0:r0 + 4, H:K], rk, ["uzn%d" % b])

    setup = {
        "feats": feats, "state": state, "diffs": diffs, "table": table, "bb": bb, "unpack": unpack,
        "vt": lambda a, b: ts(T.vt[:], T.vw[:], 127, None, A.bitwise_and, None, ["vw"], ["vt"]),
        "vm": lambda a, b: ts(T.vm[:], T.vw[:, 0:16], 15, None, A.bitwise_and, None, ["vw"], ["vm"]),
        "vb": lambda a, b: ts(T.vb[:], T.vb[:], 4, None, A.arith_shift_right, None, ["vb"], ["vb"]),
        "idw": lambda a, b: ts(T.idw[:], T.vt[:], 0.0, None, A.is_equal, None, ["vt"], ["idw"]),
        "ick": lambda a, b: act(T.i32[:], eq, F.Silu, ["idw"], ["i32"], 0.0, CK),
        "mk": lambda a, b: ts(T.mk[:], T.vm[:], 0.0, None, A.is_equal, None, ["vm"], ["mk"]),
        "wt": lambda a, b: ts(T.wt[:], T.vb[:], 0.0, 1.0 / KI, A.is_equal, A.mult, ["vb"], ["wt"]),
        "pfa": lambda a, b: ts(pf[0], T.mk[:, 15:16], -16.0, 1.0, A.mult, A.add, ["mk"], ["pf0"]),
        "pfb": lambda a, b: ts(pf[1], T.mk[:, 15:16], 2.0, -1.0, A.mult, A.add, ["mk"], ["pf1"]),
        "blk": lambda a, b: tt(T.blk[:], T.wt[:], T.vi[:], A.mult, ["wt", "vi"], ["blk"]),
        "ta": lambda a, b: ts(T.ta[:], vq, pf[0], pf[1], A.is_equal, A.mult, ["vw", "pf0", "pf1"], ["ta"]),
        "vz": lambda a, b: ts(T.vz2[:], T.vz[:, 0:128], 4, None, A.arith_shift_right, None, ["vz"], ["vz2"]),
        "dm": lambda a, b: tt(T.dm[:], T.ta[:], eq, A.add, ["ta", "idw"], ["dm"]),
        "ub": lambda a, b: ts(T.ub[:], T.vz2[:], 0.0, None, A.is_equal, None, ["vz2"], ["ub"]),
        "first": lambda a, b: cp(T.oc16[:, 64:128], T.ces[:], ["ces"], ek("cn16", 0, 8)),
        "firstf": lambda a, b: cp(T.oc[:, 64:128], T.ces[:], ["ces"], ek("cf", 0, 8)),
        "cwz": lambda a, b: ts(T.cw[:], T.idw[:, 0:144], 0.0, None, A.mult, None, ["idw"], ["cw"]),
        "cw": lambda a, b: ts(T.cw[:, 15:143:16], T.vb[:, 0:128:16], 0.0, 0.5, A.is_equal, A.mult, ["vb", "cw"], ["cw"]),
        "iff": lambda a, b: act(T.if32[:], eq, F.Copy, ["idw"], ["if32"]),
        "zw": lambda a, b: ts(T.zw[:], T.vz[:], 15.0, 4096.0, A.is_equal, A.mult, ["vz"], ["zw"]),
        "cst": lambda a, b: fill(T.cst[:], 3072.0 / CK, ["cst"]),
        "vtwo": lambda a, b: ts(T.v2[:, 64 * a:64 * b], T.rps[:, 64 * a:64 * b], 2.0, None, A.mult, None, ["rps"], ek("v2", a, b)),
        "ir": lambda a, b: act(T.ir[:], T.idw[:], F.Copy, ["idw"], ["ir"], 0.0, -2.0 / KM),
        "irf": lambda a, b: act(T.irf[:], T.idw[:], F.Copy, ["idw"], ["irf"], 0.0, -2.0 / KM),
        "minus": lambda a, b: fill(T.als[:, WP:WP + 16], -1.0, ["als0"]),
        "sh": lambda a, b: ts(T.sh[:], T.vt[:, 0:128], 16.0, None, A.is_equal, None, ["vt"], ["sh"]),
    }

    def cols(a, b):
        return slice(a * E, b * E)

    def lst(a, b, at=0):
        return slice(at + a * 8, at + b * 8)

    def step(t):
        st = t // 2
        tr, tw = "tb%d" % (t % 2), "tb%d" % (1 - t % 2)
        tk = [tr] + (ek("tb0p", 0, 4) if t == 0 else [])
        iu, iz = 4 * st + t % 2, 4 * st + 2 + t % 2
        uk = ["u0"] if st == 0 else ["uzl%d" % st, "uzm%d" % st, "uzn%d" % st]
        zk = ["z0"] if st == 0 else uk
        came = st > 0 and t % 2 == 0
        prev = "win%d" % st if t % 2 == 0 else "w%d" % (t - 1)
        w = T["w%d" % t]

        def cells(a, b):
            return T["cr%d" % st][:, lst(a, b)] if came else T.oc16[:, lst(a, b, 64)]

        def cn(a, b):
            return ek("cr%d_" % st if came else "cn16", a, b)

        def bank(table, a, n):
            at = 8 * a if table is SUM else 0
            return ps[table[a]][:, at:at + n], "ps%d" % table[a]

        def classes(tile, a, b):
            return [tile[:, a * E + k:b * E:16] for k in range(16)]

        def copy(a, b):
            dma("s", T[tw][:, P:P + W], T[tr][:, P:P + W], tk, [tw])

        def wrap(a, b):
            if a == 0:
                act(T[tr][:, 0:P], T[tr][:, W:W + P], F.Copy, tk, [tr + "l"])
            else:
                act(T[tr][:, P + W:WP], T[tr][:, P:2 * P], F.Copy, tk, [tr + "r"])

        def u(a, b):
            o, ok = bank(BAR, a, (b - a) * E)
            mms([(o, T.ub[:], T.uz[:, iu, cols(a, b)], True, False)], ["ub"] + uk, [ok])

        def inv(a, b):
            act(T.mi[:, cols(a, b)], T[tr][:, P:P + W].indirect(cells(a, b)), F.Silu, tk + cn(a, b), ek("mi", a, b), BI, SI)

        def bar(a, b):
            mms([(ps[BAR[a]][:, k:(b - a) * E:16], T.bb[:, k, :], x, False, k == 15) for k, x in enumerate(classes(T.mi, a, b))],
                ek("bb", 0, 8) + ek("mi", a, b), ["ps%d" % BAR[a]])

        def sign(a, b):
            o, ok = bank(BAR, a, (b - a) * E)
            act(T.sn[:, cols(a, b)], o, F.Sign, [ok], ek("sn", a, b), 0.5, 1.0)

        def ways(a, b):
            tt(T.pr[:, cols(a, b)], T.et[:].indirect(cells(a, b)), T.sn[:, cols(a, b)], A.mult, ek("et", 0, 4) + cn(a, b) + ek("sn", a, b), ek("pr", a, b))

        def cfl(a, b):
            cp(T.oc[:, lst(a, b, 64)], cells(a, b), cn(a, b), ek("cf", a, b))

        def cell(a, b):
            o, ok = bank(SUM, a, (b - a) * 8)
            mms([(o, T.if32[:], T.oc[:, lst(a, b, 64)], True, False)], ["if32"] + ek("cf", a, b), [ok])

        def add(a, b):
            o, ok = bank(SUM, a, (b - a) * 8)
            mms([(o, T.cw[:, 15 - k:143 - k], x, False, k == 15) for k, x in enumerate(classes(T.pr, a, b))], ["cw"] + ek("pr", a, b), [ok])

        def cint(a, b):
            o, ok = bank(SUM, a, (b - a) * 8)
            cp(T.c0[:, lst(a, b)], o, [ok], ek("c0", a, b))

        def coff(a, b):
            o, ok = bank(SUM, a, (b - a) * 8)
            ts(T.c16[:, lst(a, b)], o, float(P), None, A.add, None, [ok], ek("c16", a, b))

        def m(a, b):
            act(T.mg[:, cols(a, b)], T[tr][:].indirect(T.c16[:, lst(a, b)]), F.Silu, [tr, tr + "l", tr + "r"] + ek("c16", a, b), ek("mg", a, b), BM, SM)

        def par(a, b):
            ts(T.par[:, lst(a, b)], T.c0[:, lst(a, b)], 1, None, A.bitwise_and, None, ek("c0", a, b), ek("par", a, b))

        def ef(a, b):
            tt(T.ef[:, lst(a, b)], T.par[:, lst(a, b)], T.v2[:, lst(a, b, 64 * t)], A.add, ek("par", a, b) + ["v2%d" % t], ek("ef", a, b))

        def eoff(a, b):
            cp(T.e16[:, lst(a, b)], T.ef[:, lst(a, b)], ek("ef", a, b), ek("e16", a, b))

        def even(a, b):
            ts(T.ev[:, lst(a, b)], T.c0[:, lst(a, b)], W - 2, None, A.bitwise_and, None, ek("c0", a, b), ek("ev", a, b))

        def rho(a, b):
            c = cols(a, b)
            tt(T.rho[:, c], T.sgs[:].indirect(T.c16[:, lst(a, b)]), T.mg[:, c], A.mult, ["sgs", "sgl", "sgr"] + ek("c16", a, b) + ek("mg", a, b), ek("rho", a, b))

        def flag(a, b):
            ts(T.yv[:, cols(a, b)], T.rho[:, cols(a, b)], -KM, -CK, A.is_lt, A.mult, ek("rho", a, b), ek("yv", a, b))

        def old(a, b):
            c = cols(a, b)
            tt(T.nw[:, c], T[tr][:, P:P + W].indirect(T.e16[:, lst(a, b)]), T.yv[:, c], A.add, tk + ek("e16", a, b) + ek("yv", a, b), ek("nw", a, b))

        def put(a, b):
            act(T[tw][:, P:P + W].indirect(T.e16[:, lst(a, b)]), T.nw[:, cols(a, b)], F.Silu, ek("e16", a, b) + ek("nw", a, b), [tw])

        def z(a, b):
            o, ok = bank(HERO, a, (b - a) * 8)
            mms([(o, T.i32[:], T.cst[:, lst(a, b)], True, False)] +
                [(o, T.zw[:, 15 - k:143 - k], T.uz[:, iz, a * E + k:b * E:16], False, False) for k in range(16)],
                ["i32", "cst", "zw"] + zk, [ok])

        def hero(a, b):
            o, ok = bank(HERO, a, (b - a) * 8)
            mms([(o, T.dd[:, k, :], x, False, k == 15) for k, x in enumerate(classes(T.rho, a, b))], ["dd"] + ek("rho", a, b), [ok])

        def null(a, b):
            o, ok = bank(HERO, a, (b - a) * 8)
            ts(T.nl[:, lst(a, b)], o, 0.0, None, A.is_gt, None, [ok], ek("nl", a, b))

        def oa(a, b):
            o, ok = bank(HERO, a, (b - a) * 8)
            tt(T.oc[:, lst(a, b)], T.c0[:, lst(a, b)], o, A.max, ek("c0", a, b) + [ok], ek("oa", a, b))

        def aoff(a, b):
            ts(T.oc16[:, lst(a, b)], T.oc[:, lst(a, b)], float(W + P), float(P), A.min, A.add, ek("oa", a, b), ek("oa16", a, b))

        def xf(a, b):
            tt(T.xf[:, lst(a, b)], T.par[:, lst(a, b)], T.nl[:, lst(a, b)], A.is_equal, ek("par", a, b) + ek("nl", a, b), ek("xf", a, b))

        def cf(a, b):
            tt(T.oc[:, lst(a, b, 64)], T.ev[:, lst(a, b)], T.xf[:, lst(a, b)], A.add, ek("ev", a, b) + ek("xf", a, b), ek("cf", a, b))

        def noff(a, b):
            cp(T.oc16[:, lst(a, b, 64)], T.oc[:, lst(a, b, 64)], ek("cf", a, b), ek("cn16", a, b))

        def shift(a, b):
            mms([(ps[SUM[0]][:, lst(a, b)], T.sh[:], T.oc[:, lst(a, b, 64)], True, True)], ["sh"] + ek("cf", a, b), ["ps%d" % SUM[0]])

        def go(a, b):
            src, sk = (ps[SUM[0]][:, lst(a, b)], ["ps%d" % SUM[0]]) if a else (T.oc[:, lst(a, b, 64)], ek("cf", a, b))
            cs = T["cs%d" % (st + 1)][:, lst(a, b)]
            cp(cs, src, sk, ["cs%d%d" % (st, a)])
            send("cr%d_%d" % (st + 1, a // 4), T["cr%d" % (st + 1)][:, lst(a, b)], cs, ["cs%d%d" % (st, a)])

        def turn(tile, a):
            r = 16 * st * (a // 4)
            return tile[:, r:r + 128]

        def two(a, b):
            mms([(ps[2 + a // 4][:], turn(T.ir, a), T.rho[:, cols(a, b)], True, False)], ["ir"] + ek("rho", a, b), ["ps%d" % (2 + a // 4)])

        def nulls(a, x):
            return [(ps[2 + a // 4][:, k:H:16], turn(T.bn[:, k, :], a), x, False, k == 15) for k in range(16)]

        bk = ["bn"] + ["bn2"] * (st > 0)

        def spread(a, b):
            mms(nulls(a, T.nl[:, lst(a, b)]), bk + ek("nl", a, b), ["ps%d" % (2 + a // 4)])

        def alpha(a, b):
            return T.als[:].indirect(T.oc16[:, lst(a, b)])

        def ak(a, b):
            return ["als", "all", "alr", "als0"] + ek("oa16", a, b)

        def fused(a, b):
            tt(T.tt[:, cols(a, b)], alpha(a, b), T[prev][:, cols(a, b)], A.mult, ak(a, b) + ek(prev + "_", a, b), ek("tt", a, b))

        def plain(a, b):
            cp(T.tt[:, cols(a, b)], alpha(a, b), ak(a, b), ek("tt", a, b))

        def y(a, b):
            h = a // 4
            tt(T.yy[:, cols(a, b)], T.tt[:, cols(a, b)], ps[2 + h][:, cols(a - 4 * h, b - 4 * h)], A.mult, ek("tt", a, b) + ["ps%d" % (2 + h)], ek("yy", a, b))

        def nm(a, b):
            ts(T.nm[:, lst(a, b)], T.nl[:, lst(a, b)], -1.0, None, A.mult, None, ek("nl", a, b), ek("nm", a, b))

        def arho(a, b):
            tt(T.tt[:, cols(a, b)], alpha(a, b), T.rho[:, cols(a, b)], A.mult, ak(a, b) + ek("rho", a, b), ek("tt", a, b))

        def factor(a, b):
            mms([(ps[2 + a // 4][:], turn(T.irf, a), T.tt[:, cols(a, b)], True, False)] + nulls(a, T.nm[:, lst(a, b)]),
                ["irf"] + bk + ek("nm", a, b) + ek("tt", a, b), ["ps%d" % (2 + a // 4)])

        def yu(a, b):
            tt(T.yy[:, cols(a, b)], ps[2 + a // 4][:], T[prev][:, cols(a, b)], A.mult, ["ps%d" % (2 + a // 4)] + ek(prev + "_", a, b), ek("yy", a, b))

        def gather(a, b):
            act(T.ag[:, cols(a, b)], alpha(a, b), F.Copy, ak(a, b), ek("ag", a, b))

        def rot(a, b):
            o, ok = bank(ROT, a if b - a < 4 else 8, (b - a) * E)
            mms([(o, turn(T.idw, a), T.ag[:, cols(a, b)], True, True)], ["idw"] + ek("ag", a, b), [ok])

        def times(a, b):
            o, ok = bank(ROT, a if b - a < 4 else 8, (b - a) * E)
            tt(T.tt[:, cols(a, b)], o, T[prev][:, cols(a, b)], A.mult, [ok] + ek(prev + "_", a, b), ek("tt", a, b))

        def clip(a, b):
            ts(w[:, cols(a, b)], T.yy[:, cols(a, b)], 0.125, 4.0, A.max, A.min, ek("yy", a, b), ek("w%d_" % t, a, b))

        def on(a, b):
            c = cols(a, b)
            send("win%d_%d" % (st + 1, a // 4), T["win%d" % (st + 1)][:, c], w[:, c], ek("w%d_" % t, a, b))

        def tally(a, b):
            send("tin%d" % t, T["tin%d" % t][:], w[:], ek("w%d_" % t, 0, 8))

        def more(a, b):
            src, sk = (T["tin%d" % a], ["tin%d" % a]) if a > 1 else (T.w1, ek("w1_", 0, 8))
            dma("g", T.w0[:], src[:], sk + ek("w0_", 0, 8), ek("w0_", 0, 8), A.add)

        def four(a, b):
            send("w4in_%d" % (a // 4), T.w4in[:, cols(a, b)], T.w4[:, cols(a, b)], ek("w4_", a, b))

        def early(a, b):
            mms([(ps[TAL[a]][:], T.if32[:], T.w0[:, cols(a, b)], True, False)], ["if32"] + ek("w0_", a, b), ["ps%d" % TAL[a]])

        def late(a, b):
            mms([(ps[TAL[a]][:], T.if32[:], T.w4in[:, cols(a, b)], False, True)], ["if32"] + ek("w4in_", a, b), ["ps%d" % TAL[a]])

        def home(a, b):
            c = cols(a, b)
            send("fin%d" % FIN.index(a), T.fin[:, c], T.yy[:, c], ek("yy", a, b))

        return dict(setup, copy=copy, u=u, inv=inv, bar=bar, ways=ways, wrap=wrap, cfl=cfl, sign=sign, cell=cell, add=add, cint=cint, coff=coff,
                    m=m, par=par, ef=ef, eoff=eoff, even=even, rho=rho, flag=flag, old=old, put=put, z=z, hero=hero, null=null, oa=oa,
                    aoff=aoff, xf=xf, cf=cf, noff=noff, shift=shift, go=go, two=two, spread=spread, fused=fused, plain=plain, y=y, nm=nm,
                    arho=arho, factor=factor, yu=yu, gather=gather, rot=rot, times=times, clip=clip, on=on, tally=tally, more=more,
                    four=four, early=early, late=late, home=home)

    calls = [step(t) for t in range(NT)]
    for t in range(NT):
        for word in ORDER[t].split():
            off = word.count("+") - word.count("-")
            calls[t + off][word[abs(off):-2]](int(word[-2]), int(word[-1]))

    for i in range(len(FIN) - 1):
        c = cols(FIN[i], FIN[i + 1])
        h = FIN[i] // 4 * 4
        ts(T.w5[:, c], T.fin[:, c], 0.125, 4.0, A.max, A.min, ["fin%d" % i], ["w5_%d" % i])
        tt(T.res[:, c], T.w5[:, c], ps[TAL[h]][:, cols(FIN[i] - h, FIN[i + 1] - h)], A.add, ["w5_%d" % i, "ps%d" % TAL[h]], ["res%d" % i])
        dma("s" if i % 2 == 0 else "a", T.tl[:, c], T.res[:, c], ["res%d" % i], [])
    for s in total:
        if max(waited[q].get(s, 0) for q in eng) < total[s]:
            g.wait_ge(T.sem[s], total[s])
